import numpy as np
import ml_dtypes


def mxq(x, axis, fmt="e4m3"):
    dtype, down = {"e4m3": (ml_dtypes.float8_e4m3fn, 7), "e5m2": (ml_dtypes.float8_e5m2, 14)}[fmt]
    v = np.moveaxis(np.asarray(x, np.float32).astype(ml_dtypes.bfloat16).astype(np.float64), axis, -1)
    blocks = v.reshape(v.shape[:-1] + (-1, 32))
    amax = np.abs(blocks).max(-1, keepdims=True)
    byte = np.maximum(np.where(amax > 0, np.frexp(amax)[1] - 1 + 127, 0) - down, 1)
    scale = np.exp2(byte - 127.0)
    codes = (blocks / scale).astype(np.float32).astype(dtype).astype(np.float64)
    return np.moveaxis((codes * scale).reshape(v.shape), -1, axis)


WIDE = False


def mx_kscale(k):
    if not WIDE:
        return np.ones(k)
    levels = np.array([10, -10, 5, -5, 0])
    if k % 512:
        return np.exp2(np.random.permutation(np.resize(levels, k // 32))).repeat(32)
    a = np.empty((k // 512, 16))
    for p in range(k // 512):
        a[p, :8] = np.random.permutation(np.resize(levels, 8))
        for g in range(8):
            far = levels[np.abs(levels - a[p, g]) >= 10]
            a[p, g + 8] = far[np.random.randint(len(far))]
    return np.exp2(a.ravel()).repeat(32)


def f64(x):
    return np.asarray(x).astype(np.float64)


def striped(idx):
    return np.tile(idx.reshape(-1, 16).T, (8, 1)).astype(np.uint16)


def unstriped(offs):
    return offs[:16].T.reshape(-1).astype(np.int64)


E2M1 = np.array([0.0, 0.5, 1.0, 1.5, 2.0, 3.0, 4.0, 6.0, -0.0, -0.5, -1.0, -1.5, -2.0, -3.0, -4.0, -6.0])


def pack_weight(w, fmt):
    k, n = w.shape
    w = f64(np.asarray(w, np.float32).astype(ml_dtypes.bfloat16)).reshape(k // 32, 32, n)
    amax = np.abs(w).max(1)
    if fmt == "e4m3":
        byte = np.frexp(amax)[1] - 1 + 127 - 7
    else:
        mant, ex = np.frexp(amax / 6.0)
        byte = np.where(mant > 0.5, ex, ex - 1) + 127
    byte = np.clip(np.where(amax > 0, byte, 1), 1, 254)
    scaled = (w * np.exp2(127.0 - byte)[:, None, :]).reshape(k, n).astype(np.float32)
    by_word = np.ascontiguousarray(scaled.reshape(k // 512, 128, 4, n).transpose(0, 1, 3, 2))
    if fmt == "e4m3":
        words = by_word.astype(ml_dtypes.float8_e4m3fn).view(np.uint8)
    else:
        c = by_word.astype(ml_dtypes.float4_e2m1fn).view(np.uint8) & 0xF
        words = (c[..., 0::2] | (c[..., 1::2] << 4)).reshape(k // 512, 128, 2 * n)
    return np.ascontiguousarray(words), np.ascontiguousarray(byte.astype(np.uint8).reshape(k // 512, 16, n))


def unpack_weight(words, scales, fmt):
    g, _, n = scales.shape
    words = np.ascontiguousarray(words).reshape(g, 128, n, -1)
    if fmt == "e4m3":
        vals = words.view(ml_dtypes.float8_e4m3fn).astype(np.float64)
    else:
        nib = np.empty((g, 128, n, 4), np.uint8)
        nib[..., 0::2] = words & 0xF
        nib[..., 1::2] = words >> 4
        vals = E2M1[nib]
    vals = vals * np.repeat(np.exp2(scales.astype(np.float64) - 127.0), 8, axis=1)[..., None]
    return vals.transpose(0, 1, 3, 2).reshape(g * 512, n)


def gelu(v):
    return 0.5 * v * (1.0 + np.tanh(np.sqrt(2.0 / np.pi) * (v + 0.044715 * v**3)))


def striped8(idx):
    return np.concatenate([v.reshape(-1, 16).T for v in idx]).astype(np.uint16)


def unstriped8(offs):
    return np.stack([offs[16 * g:16 * g + 16].T.reshape(-1) for g in range(8)]).astype(np.int64)


def put_heads(h, wgs, idx8, t2):
    r = np.arange(h.shape[0])
    page = np.zeros((h.shape[0], t2))
    page[r[:, None], idx8[r % 512 // 64]] = wgs[r // 4 % 128] * h
    return page


def bf(x):
    return np.asarray(x, np.float32).astype(ml_dtypes.bfloat16)


def planes(Y):
    n, m = Y.shape
    b = f64(bf(Y)).reshape(n // 32, 32, m)
    amax = np.abs(b).max(1)
    byte = np.clip(np.where(amax > 0, np.frexp(amax)[1] - 1 + 127 - 7, 1), 1, 254)
    codes = (b * np.exp2(127.0 - byte)[:, None, :]).reshape(n, m).astype(np.float32).astype(ml_dtypes.float8_e4m3fn).view(np.uint8)
    words = codes.reshape(n // 512, 128, 4, m).transpose(0, 1, 3, 2)
    return np.ascontiguousarray(words), np.ascontiguousarray(byte.astype(np.uint8).reshape(n // 512, 16, m))


K, T, S, H, T2, N = 1536, 2048, 512, 512, 1024, 512

def setup_inputs():
    n = np.random.standard_normal
    s, u, w = mx_kscale(K)[:, None], mx_kscale(H)[:, None], mx_kscale(T2)[:, None]
    size = np.exp(0.8 * n(N))
    tab_words, tab_scales = pack_weight(n((K, T)) * s, "e4m3")
    w1_words, w1_scales = pack_weight(n((K, H)) / np.sqrt(K) / s, "e2m1")
    wc_words, wc_scales = pack_weight(n((T2, T2)) / np.sqrt(T2) / w, "e4m3")
    return {
        "tab_words": tab_words, "tab_scales": tab_scales,
        "offs": striped(np.random.permutation(T)[:S]),
        "w1_words": w1_words, "w1_scales": w1_scales,
        "b1": (0.5 * n(H)).astype(np.float32),
        "gain": (np.exp(0.3 * n(H)) * u[:, 0]).astype(np.float32),
        "offs2": striped8(np.stack([np.random.permutation(T2)[:S] for _ in range(8)])),
        "wgs": np.repeat(np.random.uniform(0.5, 2.0, (8, S)), 16, axis=0).astype(np.float32),
        "heat": (n((H, T2)) * u).astype(np.float32),
        "wv": (n((H, N)) / np.sqrt(H) / u * size[None, :]).astype(np.float32),
        "cond": (np.exp(0.3 * n((N, T2))) * size[:, None] * w.T / u).astype(np.float32),
        "wc_words": wc_words, "wc_scales": wc_scales,
    }

def reference(tab_words, tab_scales, offs, w1_words, w1_scales, b1, gain, offs2, wgs, heat, wv, cond, wc_words, wc_scales):
    v = unpack_weight(tab_words, tab_scales, "e4m3")[:, unstriped(offs)]
    w1 = unpack_weight(w1_words, w1_scales, "e2m1")
    wc = unpack_weight(wc_words, wc_scales, "e4m3")
    d = (w1.T @ v) + f64(b1)[:, None]
    h = 0.5 * d * (1.0 + np.tanh(np.sqrt(2.0 / np.pi) * (d + 0.044715 * d ** 3))) * f64(gain)[:, None]
    page = put_heads(h, f64(wgs), unstriped8(offs2), T2)
    z = f64(heat) - page
    left = mxq(f64(wv), 0, "e4m3").T @ mxq(z, 0, "e4m3")
    right = mxq((z * f64(cond)).T, 0, "e4m3").T @ wc
    y = left + right
    words, scales = planes(y)
    return y, words, scales

@@ -1,0 +1,294 @@
+from contextlib import ExitStack
+
+import concourse.mybir as mybir
+from concourse.masks import make_identity
+
+K, T, S, H, T2, N = 1536, 2048, 512, 512, 1024, 512
+FLOPS = 2 * K * H * S + 2 * H * N * T2 + 2 * N * T2 * T2
+
+F32 = mybir.dt.float32
+BF16 = mybir.dt.bfloat16
+I32 = mybir.dt.int32
+U32 = mybir.dt.uint32
+U16 = mybir.dt.uint16
+U8 = mybir.dt.uint8
+FP8X4 = mybir.dt.float8_e4m3fn_x4
+FP4X4 = mybir.dt.float4_e2m1fn_x4
+MULT = mybir.AluOpType.mult
+ADD = mybir.AluOpType.add
+GELU = mybir.ActivationFunctionType.Gelu_apprx_tanh
+
+P = 128
+PACK = 4
+QUADS = 4
+PASSES1 = K // 512
+PASSES2 = T2 // 512
+CHUNK = 256
+CHUNKS = T2 // CHUNK
+
+
+def tile_list_heating_loop_balance_kernel(
+    tc, tab_words, tab_scales, offs, w1_words, w1_scales, b1, gain, offs2, wgs, heat, wv, cond,
+    wc_words, wc_scales, out_0, out_1, out_2,
+):
+    nc = tc.nc
+    with ExitStack() as ctx:
+        keep = ctx.enter_context(tc.tile_pool(name="keep", bufs=1))
+        psum = ctx.enter_context(tc.psum_pool(name="psum", bufs=1))
+
+        def sb(name, shape, dtype, tag=None):
+            return keep.tile(shape, dtype, name=name, tag=tag or name, align_bytes=64)
+
+        def bank(b, name, shape):
+            return psum.tile(shape, F32, name=name, tag="bank%d" % b)
+
+        picks = keep.tile([P, S // 16], U16, name="picks")
+        places = keep.tile([P, S // 16], U16, name="places")
+        w1_plane_raw = sb("w1_plane_raw", [P, PASSES1 * H], U8)
+        tab_plane = sb("tab_plane", [P, PASSES1 * T], U8)
+        w1_raw = sb("w1_raw", [P, PASSES1 * 2 * H], U8)
+        tab_codes = [sb("tab_codes%d" % a, [P, T], U32) for a in range(PASSES1)]
+        wc_plane = sb("wc_plane", [P, T2], U8)
+
+        nc.vector.memset(w1_plane_raw[:].bitcast(I32), 0)
+        nc.vector.memset(tab_plane[:].bitcast(I32), 0)
+        nc.vector.memset(wc_plane[:].bitcast(I32), 0)
+
+        warm_in = sb("warm_in", [P, 8], F32)
+        warm_out = sb("warm_out", [P, 8], F32)
+        nc.gpsimd.memset(warm_in[:], 0.0)
+        nc.scalar.activation(warm_out[:], warm_in[:], GELU)
+        ident = sb("ident", [P, P], F32)
+        make_identity(nc, ident[:])
+
+        nc.sync.dma_start(picks[:], offs)
+        nc.sync.dma_start(
+            w1_raw[:].bitcast(I32).rearrange("p (a w) -> p a w", a=PASSES1),
+            w1_words.bitcast(I32).rearrange("a p w -> p a w"),
+        )
+        for q in range(QUADS):
+            nc.sync.dma_start(
+                w1_plane_raw[32 * q : 32 * q + 4, :].bitcast(I32).rearrange("r (a w) -> r a w", a=PASSES1),
+                w1_scales[:, 4 * q : 4 * q + 4, :].bitcast(I32).rearrange("a r w -> r a w"),
+            )
+        for q in range(QUADS):
+            nc.sync.dma_start(
+                tab_plane[32 * q : 32 * q + 4, :].bitcast(I32).rearrange("r (a w) -> r a w", a=PASSES1),
+                tab_scales[:, 4 * q : 4 * q + 4, :].bitcast(I32).rearrange("a r w -> r a w"),
+            )
+        for a in range(PASSES1):
+            nc.sync.dma_start(tab_codes[a][:].bitcast(I32), tab_words[a].rearrange("p t i -> p (t i)").bitcast(I32))
+        nc.sync.dma_start(places[:], offs2)
+        wgs_sb = sb("wgs_sb", [P, S], F32)
+        nc.sync.dma_start(wgs_sb[:], wgs)
+        bias = sb("bias", [P, PACK], F32)
+        gain_sb = sb("gain_sb", [P, PACK], F32)
+        nc.sync.dma_start(bias[:], b1.rearrange("(p i) -> p i", i=PACK))
+        nc.sync.dma_start(gain_sb[:], gain.rearrange("(p i) -> p i", i=PACK))
+        heat_rows = heat.rearrange("(p i) m -> p i m", i=PACK)
+        cond_rows = cond.rearrange("(p i) m -> p i m", i=PACK)
+        heat_sb = [sb("heat%d" % i, [P, T2], F32) for i in range(PACK)]
+        cond_sb = [sb("cond%d" % i, [P, T2], F32) for i in range(PACK)]
+        wc_codes = [sb("wc_codes%d" % a, [P, T2], U32) for a in range(PASSES2)]
+        wv_raw = sb("wv_raw", [P, PACK, N], F32)
+        for i in range(PACK):
+            nc.sync.dma_start(cond_sb[i][:], cond_rows[:, i, :])
+            nc.sync.dma_start(heat_sb[i][:], heat_rows[:, i, :])
+            if i == 1:
+                for q in range(QUADS):
+                    nc.sync.dma_start(
+                        wc_plane[32 * q : 32 * q + 4 * PASSES2, :].bitcast(I32),
+                        wc_scales[:, 4 * q : 4 * q + 4, :].bitcast(I32),
+                    )
+                for a in range(PASSES2):
+                    nc.sync.dma_start(
+                        wc_codes[a][:].bitcast(I32), wc_words[a].rearrange("p c i -> p (c i)").bitcast(I32)
+                    )
+        nc.sync.dma_start(wv_raw[:], wv.rearrange("(p j) c -> p j c", j=PACK))
+
+        w1_plane = sb("w1_plane", [P, PASSES1 * H], U8)
+        nc.vector.tensor_copy(
+            w1_plane[:].rearrange("p (a i m) -> p a i m", a=PASSES1, i=PACK),
+            w1_plane_raw[:].rearrange("p (a m i) -> p a i m", a=PASSES1, i=PACK),
+        )
+        w1_codes = sb("w1_codes", [P, PASSES1 * 2 * H], U8)
+        for a in range(PASSES1):
+            cols = slice(a * 2 * H, (a + 1) * 2 * H)
+            nc.vector.tensor_copy(
+                w1_codes[:, cols].bitcast(U16).rearrange("p (i m) -> p i m", i=PACK),
+                w1_raw[:, cols].bitcast(U16).rearrange("p (m i) -> p i m", i=PACK),
+            )
+        v_plane = [sb("v_plane%d" % a, [P, S], U8) for a in range(PASSES1)]
+        v_codes = [sb("v_codes%d" % a, [P, S], U32) for a in range(PASSES1)]
+        for a in range(PASSES1):
+            nc.vector.tensor_copy(v_plane[a][:], tab_plane[:, a * T : (a + 1) * T].indirect(picks[:]))
+        neg_gain = sb("neg_gain", [P, PACK], F32)
+        d = [bank(4 + (i + 3) % PACK, "d%d" % i, [P, S]) for i in range(PACK)]
+        for a in range(PASSES1):
+            nc.vector.tensor_copy(v_codes[a][:], tab_codes[a][:].indirect(picks[:]))
+            for i in range(PACK):
+                c0 = a * H + i * P
+                nc.tensor.matmul_mx(
+                    out=d[i][:],
+                    lhsT=w1_codes[:, 2 * c0 : 2 * (c0 + P)].bitcast(FP4X4),
+                    lhsT_scale=w1_plane[:, c0 : c0 + P],
+                    rhs=v_codes[a][:].bitcast(FP8X4),
+                    rhs_scale=v_plane[a][:],
+                    start=(a == 0),
+                    stop=(a == PASSES1 - 1),
+                )
+        nc.vector.tensor_scalar(neg_gain[:], gain_sb[:], -1.0, None, MULT)
+        tenants = ["w1_raw", "tab_plane", "tab_codes0", "tab_codes1"]
+        pages = [sb("page%d" % i, [P, T2], F32, tag=tenants[i]) for i in range(PACK)]
+        for i in range(PACK):
+            nc.gpsimd.memset(pages[i][:], 0.0)
+
+        z_pair = [sb("z_pair%d" % u, [P, 2, T2], F32) for u in range(2)]
+        z_round = [sb("z_round%d" % c, [P, CHUNK, PACK], BF16) for c in range(CHUNKS)]
+        z_codes = [sb("z_codes%d" % c, [P, CHUNK], U32) for c in range(CHUNKS)]
+        z_plane = [sb("z_plane%d" % c, [P, CHUNK], U8) for c in range(CHUNKS)]
+        zc = [sb("zc%d" % i, [P, T2], BF16) for i in range(PACK)]
+        zct = [sb("zct%d" % i, [P, T2], BF16) for i in range(PACK)]
+        zc_codes = [sb("zc_codes%d" % i, [P, PASSES2 * P], U32) for i in range(PACK)]
+        zc_plane = [sb("zc_plane%d" % i, [P, PASSES2 * P], U8) for i in range(PACK)]
+        wv_round = sb("wv_round", [P, N * PACK], BF16)
+        wv_codes = sb("wv_codes", [P, N], U32)
+        wv_plane = sb("wv_plane", [P, N], U8)
+        acc = {}
+
+        def scatter(i):
+            act = sb("act%d" % i, [P, S], F32, tag="heat%d" % (i - 1) if i else None)
+            nc.scalar.activation(act[:], d[i][:], GELU, bias=bias[:, i : i + 1])
+            nc.vector.tensor_tensor(pages[i][:].indirect(places[:]), act[:], wgs_sb[:], MULT)
+
+        def remainder(i, cols):
+            nc.vector.scalar_tensor_tensor(
+                z_pair[i // 2][:, i % 2, cols], pages[i][:, cols], neg_gain[:, i : i + 1], heat_sb[i][:, cols], MULT, ADD
+            )
+
+        def couple(i):
+            nc.vector.tensor_tensor(
+                zc[i][:].rearrange("p (u q e) -> p u q e", u=2, e=2),
+                z_pair[i // 2][:, i % 2, :].rearrange("p (q u e) -> p u q e", u=2, e=2),
+                cond_sb[i][:].rearrange("p (q u e) -> p u q e", u=2, e=2),
+                MULT,
+            )
+            turned = bank(7, "turned%d" % i, [P, 2 * PASSES2, P])
+            words = zc[i][:].bitcast(F32)
+            for b in range(2 * PASSES2):
+                nc.tensor.transpose(turned[:, b, :], words[:, b * P : (b + 1) * P], ident[:])
+            nc.scalar.copy(
+                zct[i][:].bitcast(F32).rearrange("q (a n u) -> q a n u", a=PASSES2, u=2),
+                turned[:].rearrange("q (u a) n -> q a n u", u=2),
+            )
+
+        def quantize_zc(i):
+            nc.vector.quantize_mx(out=zc_codes[i][:].bitcast(FP8X4), scales=zc_plane[i][:], in_=zct[i][:])
+
+        def round_z(u, c, on_vector):
+            dst = z_round[c][:, :, 2 * u : 2 * u + 2]
+            src = z_pair[u][:, :, c * CHUNK : (c + 1) * CHUNK].rearrange("p e m -> p m e")
+            if on_vector:
+                nc.vector.tensor_copy(dst, src)
+            else:
+                nc.scalar.copy(dst, src)
+
+        def quantize_z(c):
+            nc.vector.quantize_mx(
+                out=z_codes[c][:].bitcast(FP8X4), scales=z_plane[c][:], in_=z_round[c][:].rearrange("p m i -> p (m i)")
+            )
+
+        def right(i, c, first, last):
+            u = i // 2
+            if first:
+                acc[u, c] = bank(4 * u + c, "acc%d_%d" % (u, c), [P, 2, CHUNK])
+            cols = slice(c * CHUNK, (c + 1) * CHUNK)
+            for a in range(PASSES2):
+                nc.tensor.matmul_mx(
+                    out=acc[u, c][:, i % 2, :],
+                    lhsT=zc_codes[i][:, a * P : (a + 1) * P].bitcast(FP8X4),
+                    lhsT_scale=zc_plane[i][:, a * P : (a + 1) * P],
+                    rhs=wc_codes[a][:, cols].bitcast(FP8X4),
+                    rhs_scale=wc_plane[4 * a : P, cols],
+                    start=(first and a == 0),
+                    stop=(last and a == PASSES2 - 1),
+                )
+
+        def left(i, c, last):
+            nc.tensor.matmul_mx(
+                out=acc[i // 2, c][:, i % 2, :],
+                lhsT=wv_codes[:, i * P : (i + 1) * P].bitcast(FP8X4),
+                lhsT_scale=wv_plane[:, i * P : (i + 1) * P],
+                rhs=z_codes[c][:].bitcast(FP8X4),
+                rhs_scale=z_plane[c][:],
+                start=False,
+                stop=last,
+            )
+
+        whole = slice(0, T2)
+        scatter(0)
+        remainder(0, whole)
+        couple(0)
+        scatter(1)
+        quantize_zc(0)
+        for c in range(CHUNKS):
+            right(0, c, True, False)
+        remainder(1, whole)
+        couple(1)
+        scatter(2)
+        for c in range(CHUNKS):
+            round_z(0, c, False)
+        quantize_zc(1)
+        for c in range(CHUNKS):
+            right(1, c, False, False)
+        remainder(2, whole)
+        couple(2)
+        scatter(3)
+        nc.scalar.copy(
+            wv_round[:].rearrange("p (t m j) -> p m j t", t=PACK, j=PACK),
+            wv_raw[:].rearrange("p j (m t) -> p m j t", t=PACK),
+        )
+        quantize_zc(2)
+        nc.vector.quantize_mx(out=wv_codes[:].bitcast(FP8X4), scales=wv_plane[:], in_=wv_round[:])
+        for c in range(CHUNKS - 1):
+            right(2, c, True, False)
+        remainder(3, slice(0, T2 // 2))
+        remainder(3, slice(T2 // 2, T2))
+        round_z(1, 0, False)
+        round_z(1, 1, False)
+        couple(3)
+        right(2, CHUNKS - 1, True, False)
+        round_z(1, 2, True)
+        round_z(1, 3, True)
+        quantize_z(0)
+        quantize_z(1)
+        quantize_zc(3)
+        quantize_z(2)
+        quantize_z(3)
+
+        y = [sb("y%d" % c, [P, PACK, CHUNK], F32) for c in range(CHUNKS)]
+        y_round = [sb("y_round%d" % c, [P, CHUNK * PACK], BF16) for c in range(CHUNKS)]
+        y_codes = sb("y_codes", [P, T2], U32)
+        y_plane = sb("y_plane", [P, T2], U8)
+        out_rows = out_0.rearrange("(p i) m -> p i m", i=PACK)
+        out_words = out_1[0].rearrange("p m t -> p (m t)").bitcast(I32)
+        for c in range(CHUNKS):
+            cols = slice(c * CHUNK, (c + 1) * CHUNK)
+            left(0, c, False)
+            left(1, c, True)
+            left(2, c, False)
+            left(3, c, False)
+            right(3, c, False, True)
+            for u in range(2):
+                nc.scalar.copy(y[c][:, 2 * u : 2 * u + 2, :], acc[u, c][:])
+                nc.sync.dma_start(out_rows[:, 2 * u : 2 * u + 2, cols], y[c][:, 2 * u : 2 * u + 2, :])
+            nc.vector.tensor_copy(
+                y_round[c][:].rearrange("p (m j i) -> p m i j", j=4, i=PACK),
+                y[c][:].rearrange("p i (m j) -> p m i j", j=4),
+            )
+            nc.vector.quantize_mx(out=y_codes[:, cols].bitcast(FP8X4), scales=y_plane[:, cols], in_=y_round[c][:])
+            nc.sync.dma_start(out_words[:, cols], y_codes[:, cols].bitcast(I32))
+        for q in range(QUADS):
+            nc.sync.dma_start(
+                out_2[0, 4 * q : 4 * q + 4, :].bitcast(I32), y_plane[32 * q : 32 * q + 4, :].bitcast(I32)
+            )

@@ -50,41 +50,41 @@ def tile_list_heating_loop_balance_kernel(
         tab_codes = [sb("tab_codes%d" % a, [P, T], U32) for a in range(PASSES1)]
         wc_plane = sb("wc_plane", [P, T2], U8)
 
-        nc.vector.memset(w1_plane_raw[:].bitcast(I32), 0)
         nc.vector.memset(tab_plane[:].bitcast(I32), 0)
+        nc.vector.memset(w1_plane_raw[:].bitcast(I32), 0)
         nc.vector.memset(wc_plane[:].bitcast(I32), 0)
 
         warm_in = sb("warm_in", [P, 8], F32)
         warm_out = sb("warm_out", [P, 8], F32)
-        nc.gpsimd.memset(warm_in[:], 0.0)
+        nc.vector.memset(warm_in[:], 0.0)
         nc.scalar.activation(warm_out[:], warm_in[:], GELU)
         ident = sb("ident", [P, P], F32)
         make_identity(nc, ident[:])
 
+        bias = sb("bias", [P, PACK], F32)
+        gain_sb = sb("gain_sb", [P, PACK], F32)
         nc.sync.dma_start(picks[:], offs)
+        nc.sync.dma_start(places[:], offs2)
+        nc.sync.dma_start(bias[:], b1.rearrange("(p i) -> p i", i=PACK))
+        nc.sync.dma_start(gain_sb[:], gain.rearrange("(p i) -> p i", i=PACK))
         nc.sync.dma_start(
             w1_raw[:].bitcast(I32).rearrange("p (a w) -> p a w", a=PASSES1),
             w1_words.bitcast(I32).rearrange("a p w -> p a w"),
         )
         for q in range(QUADS):
             nc.sync.dma_start(
-                w1_plane_raw[32 * q : 32 * q + 4, :].bitcast(I32).rearrange("r (a w) -> r a w", a=PASSES1),
-                w1_scales[:, 4 * q : 4 * q + 4, :].bitcast(I32).rearrange("a r w -> r a w"),
-            )
-        for q in range(QUADS):
-            nc.sync.dma_start(
                 tab_plane[32 * q : 32 * q + 4, :].bitcast(I32).rearrange("r (a w) -> r a w", a=PASSES1),
                 tab_scales[:, 4 * q : 4 * q + 4, :].bitcast(I32).rearrange("a r w -> r a w"),
             )
+        for q in range(QUADS):
+            nc.sync.dma_start(
+                w1_plane_raw[32 * q : 32 * q + 4, :].bitcast(I32).rearrange("r (a w) -> r a w", a=PASSES1),
+                w1_scales[:, 4 * q : 4 * q + 4, :].bitcast(I32).rearrange("a r w -> r a w"),
+            )
         for a in range(PASSES1):
             nc.sync.dma_start(tab_codes[a][:].bitcast(I32), tab_words[a].rearrange("p t i -> p (t i)").bitcast(I32))
-        nc.sync.dma_start(places[:], offs2)
         wgs_sb = sb("wgs_sb", [P, S], F32)
         nc.sync.dma_start(wgs_sb[:], wgs)
-        bias = sb("bias", [P, PACK], F32)
-        gain_sb = sb("gain_sb", [P, PACK], F32)
-        nc.sync.dma_start(bias[:], b1.rearrange("(p i) -> p i", i=PACK))
-        nc.sync.dma_start(gain_sb[:], gain.rearrange("(p i) -> p i", i=PACK))
         heat_rows = heat.rearrange("(p i) m -> p i m", i=PACK)
         cond_rows = cond.rearrange("(p i) m -> p i m", i=PACK)
         heat_sb = [sb("heat%d" % i, [P, T2], F32) for i in range(PACK)]
@@ -94,6 +94,8 @@ def tile_list_heating_loop_balance_kernel(
         for i in range(PACK):
             nc.sync.dma_start(cond_sb[i][:], cond_rows[:, i, :])
             nc.sync.dma_start(heat_sb[i][:], heat_rows[:, i, :])
+            if i == 0:
+                nc.sync.dma_start(wv_raw[:], wv.rearrange("(p j) c -> p j c", j=PACK))
             if i == 1:
                 for q in range(QUADS):
                     nc.sync.dma_start(
@@ -104,20 +106,36 @@ def tile_list_heating_loop_balance_kernel(
                     nc.sync.dma_start(
                         wc_codes[a][:].bitcast(I32), wc_words[a].rearrange("p c i -> p (c i)").bitcast(I32)
                     )
-        nc.sync.dma_start(wv_raw[:], wv.rearrange("(p j) c -> p j c", j=PACK))
 
-        w1_plane = sb("w1_plane", [P, PASSES1 * H], U8)
-        nc.vector.tensor_copy(
-            w1_plane[:].rearrange("p (a i m) -> p a i m", a=PASSES1, i=PACK),
-            w1_plane_raw[:].rearrange("p (a m i) -> p a i m", a=PASSES1, i=PACK),
-        )
-        w1_codes = sb("w1_codes", [P, PASSES1 * 2 * H], U8)
-        for a in range(PASSES1):
-            cols = slice(a * 2 * H, (a + 1) * 2 * H)
+        w1_codes, w1_plane = {}, {}
+
+        def deal_w1(name, first, count, codes_tag=None, plane_tag=None):
+            plane = sb(name + "_plane", [P, count * PASSES1 * P], U8, tag=plane_tag)
+            codes = sb(name + "_codes", [P, count * PASSES1 * 2 * P], U8, tag=codes_tag)
             nc.vector.tensor_copy(
-                w1_codes[:, cols].bitcast(U16).rearrange("p (i m) -> p i m", i=PACK),
-                w1_raw[:, cols].bitcast(U16).rearrange("p (m i) -> p i m", i=PACK),
+                plane[:].rearrange("p (i c) -> p i c", i=count),
+                w1_plane_raw[:].rearrange("p (c i) -> p i c", i=PACK)[:, first : first + count, :],
             )
+            nc.vector.tensor_copy(
+                codes[:].bitcast(U16).rearrange("p (i c) -> p i c", i=count),
+                w1_raw[:].bitcast(U16).rearrange("p (c i) -> p i c", i=PACK)[:, first : first + count, :],
+            )
+            for k in range(count):
+                w1_plane[first + k] = plane[:, k * PASSES1 * P : (k + 1) * PASSES1 * P]
+                w1_codes[first + k] = codes[:, 2 * k * PASSES1 * P : 2 * (k + 1) * PASSES1 * P]
+
+        def first_product(i, a):
+            nc.tensor.matmul_mx(
+                out=d[i][:],
+                lhsT=w1_codes[i][:, 2 * a * P : 2 * (a + 1) * P].bitcast(FP4X4),
+                lhsT_scale=w1_plane[i][:, a * P : (a + 1) * P],
+                rhs=v_codes[a][:].bitcast(FP8X4),
+                rhs_scale=v_plane[a][:],
+                start=(a == 0),
+                stop=(a == PASSES1 - 1),
+            )
+
+        deal_w1("w1_first", 0, 1)
         v_plane = [sb("v_plane%d" % a, [P, S], U8) for a in range(PASSES1)]
         v_codes = [sb("v_codes%d" % a, [P, S], U32) for a in range(PASSES1)]
         for a in range(PASSES1):
@@ -126,19 +144,13 @@ def tile_list_heating_loop_balance_kernel(
         d = [bank(4 + (i + 3) % PACK, "d%d" % i, [P, S]) for i in range(PACK)]
         for a in range(PASSES1):
             nc.vector.tensor_copy(v_codes[a][:], tab_codes[a][:].indirect(picks[:]))
-            for i in range(PACK):
-                c0 = a * H + i * P
-                nc.tensor.matmul_mx(
-                    out=d[i][:],
-                    lhsT=w1_codes[:, 2 * c0 : 2 * (c0 + P)].bitcast(FP4X4),
-                    lhsT_scale=w1_plane[:, c0 : c0 + P],
-                    rhs=v_codes[a][:].bitcast(FP8X4),
-                    rhs_scale=v_plane[a][:],
-                    start=(a == 0),
-                    stop=(a == PASSES1 - 1),
-                )
+            first_product(0, a)
+        deal_w1("w1_rest", 1, PACK - 1, codes_tag="tab_codes2", plane_tag="tab_codes1")
+        for i in range(1, PACK):
+            for a in range(PASSES1):
+                first_product(i, a)
         nc.vector.tensor_scalar(neg_gain[:], gain_sb[:], -1.0, None, MULT)
-        tenants = ["w1_raw", "tab_plane", "tab_codes0", "tab_codes1"]
+        tenants = ["tab_plane", "tab_codes0", "w1_plane_raw", "w1_raw"]
         pages = [sb("page%d" % i, [P, T2], F32, tag=tenants[i]) for i in range(PACK)]
         for i in range(PACK):
             nc.gpsimd.memset(pages[i][:], 0.0)
@@ -167,19 +179,21 @@ def tile_list_heating_loop_balance_kernel(
             )
 
         def couple(i):
-            nc.vector.tensor_tensor(
-                zc[i][:].rearrange("p (u q e) -> p u q e", u=2, e=2),
-                z_pair[i // 2][:, i % 2, :].rearrange("p (q u e) -> p u q e", u=2, e=2),
-                cond_sb[i][:].rearrange("p (q u e) -> p u q e", u=2, e=2),
-                MULT,
-            )
+            for a in range(PASSES2):
+                cols = slice(a * 512, (a + 1) * 512)
+                nc.vector.tensor_tensor(
+                    zc[i][:, cols].rearrange("p (u q e) -> p u q e", u=2, e=2),
+                    z_pair[i // 2][:, i % 2, cols].rearrange("p (q u e) -> p u q e", u=2, e=2),
+                    cond_sb[i][:, cols].rearrange("p (q u e) -> p u q e", u=2, e=2),
+                    MULT,
+                )
             turned = bank(7, "turned%d" % i, [P, 2 * PASSES2, P])
             words = zc[i][:].bitcast(F32)
             for b in range(2 * PASSES2):
                 nc.tensor.transpose(turned[:, b, :], words[:, b * P : (b + 1) * P], ident[:])
             nc.scalar.copy(
                 zct[i][:].bitcast(F32).rearrange("q (a n u) -> q a n u", a=PASSES2, u=2),
-                turned[:].rearrange("q (u a) n -> q a n u", u=2),
+                turned[:].rearrange("q (a u) n -> q a n u", u=2),
             )
 
         def quantize_zc(i):
@@ -225,15 +239,23 @@ def tile_list_heating_loop_balance_kernel(
                 stop=last,
             )
 
-        whole = slice(0, T2)
+        def halves(i):
+            remainder(i, slice(0, T2 // 2))
+            remainder(i, slice(T2 // 2, T2))
+
         scatter(0)
-        remainder(0, whole)
+        halves(0)
         couple(0)
         scatter(1)
+        nc.scalar.copy(
+            wv_round[:].rearrange("p (t m j) -> p m t j", t=PACK, j=PACK),
+            wv_raw[:].rearrange("p j (m t) -> p m t j", t=PACK),
+        )
         quantize_zc(0)
         for c in range(CHUNKS):
             right(0, c, True, False)
-        remainder(1, whole)
+        nc.vector.quantize_mx(out=wv_codes[:].bitcast(FP8X4), scales=wv_plane[:], in_=wv_round[:])
+        halves(1)
         couple(1)
         scatter(2)
         for c in range(CHUNKS):
@@ -241,28 +263,22 @@ def tile_list_heating_loop_balance_kernel(
         quantize_zc(1)
         for c in range(CHUNKS):
             right(1, c, False, False)
-        remainder(2, whole)
+        halves(2)
         couple(2)
         scatter(3)
-        nc.scalar.copy(
-            wv_round[:].rearrange("p (t m j) -> p m j t", t=PACK, j=PACK),
-            wv_raw[:].rearrange("p j (m t) -> p m j t", t=PACK),
-        )
         quantize_zc(2)
-        nc.vector.quantize_mx(out=wv_codes[:].bitcast(FP8X4), scales=wv_plane[:], in_=wv_round[:])
         for c in range(CHUNKS - 1):
             right(2, c, True, False)
-        remainder(3, slice(0, T2 // 2))
-        remainder(3, slice(T2 // 2, T2))
+        halves(3)
         round_z(1, 0, False)
         round_z(1, 1, False)
         couple(3)
         right(2, CHUNKS - 1, True, False)
-        round_z(1, 2, True)
-        round_z(1, 3, True)
         quantize_z(0)
         quantize_z(1)
+        round_z(1, 2, True)
         quantize_zc(3)
+        round_z(1, 3, True)
         quantize_z(2)
         quantize_z(3)
 

@@ -50,7 +50,8 @@ def tile_list_heating_loop_balance_kernel(
         tab_codes = [sb("tab_codes%d" % a, [P, T], U32) for a in range(PASSES1)]
         wc_plane = sb("wc_plane", [P, T2], U8)
 
-        nc.vector.memset(tab_plane[:].bitcast(I32), 0)
+        nc.gpsimd.memset(tab_plane[:, :T].bitcast(I32), 0)
+        nc.vector.memset(tab_plane[:, T:].bitcast(I32), 0)
         nc.vector.memset(w1_plane_raw[:].bitcast(I32), 0)
         nc.vector.memset(wc_plane[:].bitcast(I32), 0)
 
@@ -64,9 +65,7 @@ def tile_list_heating_loop_balance_kernel(
         bias = sb("bias", [P, PACK], F32)
         gain_sb = sb("gain_sb", [P, PACK], F32)
         nc.sync.dma_start(picks[:], offs)
-        nc.sync.dma_start(places[:], offs2)
         nc.sync.dma_start(bias[:], b1.rearrange("(p i) -> p i", i=PACK))
-        nc.sync.dma_start(gain_sb[:], gain.rearrange("(p i) -> p i", i=PACK))
         nc.sync.dma_start(
             w1_raw[:].bitcast(I32).rearrange("p (a w) -> p a w", a=PASSES1),
             w1_words.bitcast(I32).rearrange("a p w -> p a w"),
@@ -76,15 +75,18 @@ def tile_list_heating_loop_balance_kernel(
                 tab_plane[32 * q : 32 * q + 4, :].bitcast(I32).rearrange("r (a w) -> r a w", a=PASSES1),
                 tab_scales[:, 4 * q : 4 * q + 4, :].bitcast(I32).rearrange("a r w -> r a w"),
             )
-        for q in range(QUADS):
-            nc.sync.dma_start(
-                w1_plane_raw[32 * q : 32 * q + 4, :].bitcast(I32).rearrange("r (a w) -> r a w", a=PASSES1),
-                w1_scales[:, 4 * q : 4 * q + 4, :].bitcast(I32).rearrange("a r w -> r a w"),
-            )
         for a in range(PASSES1):
+            if a == PASSES1 - 1:
+                for q in range(QUADS):
+                    nc.sync.dma_start(
+                        w1_plane_raw[32 * q : 32 * q + 4, :].bitcast(I32).rearrange("r (a w) -> r a w", a=PASSES1),
+                        w1_scales[:, 4 * q : 4 * q + 4, :].bitcast(I32).rearrange("a r w -> r a w"),
+                    )
             nc.sync.dma_start(tab_codes[a][:].bitcast(I32), tab_words[a].rearrange("p t i -> p (t i)").bitcast(I32))
         wgs_sb = sb("wgs_sb", [P, S], F32)
+        nc.sync.dma_start(places[:], offs2)
         nc.sync.dma_start(wgs_sb[:], wgs)
+        nc.sync.dma_start(gain_sb[:], gain.rearrange("(p i) -> p i", i=PACK))
         heat_rows = heat.rearrange("(p i) m -> p i m", i=PACK)
         cond_rows = cond.rearrange("(p i) m -> p i m", i=PACK)
         heat_sb = [sb("heat%d" % i, [P, T2], F32) for i in range(PACK)]
@@ -107,27 +109,26 @@ def tile_list_heating_loop_balance_kernel(
                         wc_codes[a][:].bitcast(I32), wc_words[a].rearrange("p c i -> p (c i)").bitcast(I32)
                     )
 
-        w1_codes, w1_plane = {}, {}
+        w1_codes = sb("w1_codes", [P, PACK, PASSES1 * 2 * P], U8)
+        nc.vector.tensor_copy(
+            w1_codes[:].rearrange("p i b -> p (i b)").bitcast(U16).rearrange("p (i c) -> p i c", i=PACK),
+            w1_raw[:].bitcast(U16).rearrange("p (c i) -> p i c", i=PACK),
+        )
+        w1_plane = {}
 
-        def deal_w1(name, first, count, codes_tag=None, plane_tag=None):
-            plane = sb(name + "_plane", [P, count * PASSES1 * P], U8, tag=plane_tag)
-            codes = sb(name + "_codes", [P, count * PASSES1 * 2 * P], U8, tag=codes_tag)
+        def deal_plane(name, first, count, tag=None):
+            plane = sb(name, [P, count * PASSES1 * P], U8, tag=tag)
             nc.vector.tensor_copy(
-                plane[:].rearrange("p (i c) -> p i c", i=count),
-                w1_plane_raw[:].rearrange("p (c i) -> p i c", i=PACK)[:, first : first + count, :],
-            )
-            nc.vector.tensor_copy(
-                codes[:].bitcast(U16).rearrange("p (i c) -> p i c", i=count),
-                w1_raw[:].bitcast(U16).rearrange("p (c i) -> p i c", i=PACK)[:, first : first + count, :],
+                plane[:].rearrange("p (i h c) -> p h i c", i=count, h=2),
+                w1_plane_raw[:].rearrange("p (h c i) -> p h i c", i=PACK, h=2)[:, :, first : first + count, :],
             )
             for k in range(count):
                 w1_plane[first + k] = plane[:, k * PASSES1 * P : (k + 1) * PASSES1 * P]
-                w1_codes[first + k] = codes[:, 2 * k * PASSES1 * P : 2 * (k + 1) * PASSES1 * P]
 
         def first_product(i, a):
             nc.tensor.matmul_mx(
                 out=d[i][:],
-                lhsT=w1_codes[i][:, 2 * a * P : 2 * (a + 1) * P].bitcast(FP4X4),
+                lhsT=w1_codes[:, i, 2 * a * P : 2 * (a + 1) * P].bitcast(FP4X4),
                 lhsT_scale=w1_plane[i][:, a * P : (a + 1) * P],
                 rhs=v_codes[a][:].bitcast(FP8X4),
                 rhs_scale=v_plane[a][:],
@@ -135,7 +136,7 @@ def tile_list_heating_loop_balance_kernel(
                 stop=(a == PASSES1 - 1),
             )
 
-        deal_w1("w1_first", 0, 1)
+        deal_plane("w1_plane_first", 0, 1)
         v_plane = [sb("v_plane%d" % a, [P, S], U8) for a in range(PASSES1)]
         v_codes = [sb("v_codes%d" % a, [P, S], U32) for a in range(PASSES1)]
         for a in range(PASSES1):
@@ -145,12 +146,12 @@ def tile_list_heating_loop_balance_kernel(
         for a in range(PASSES1):
             nc.vector.tensor_copy(v_codes[a][:], tab_codes[a][:].indirect(picks[:]))
             first_product(0, a)
-        deal_w1("w1_rest", 1, PACK - 1, codes_tag="tab_codes2", plane_tag="tab_codes1")
+        deal_plane("w1_plane_rest", 1, PACK - 1, tag="tab_codes2")
         for i in range(1, PACK):
             for a in range(PASSES1):
                 first_product(i, a)
         nc.vector.tensor_scalar(neg_gain[:], gain_sb[:], -1.0, None, MULT)
-        tenants = ["tab_plane", "tab_codes0", "w1_plane_raw", "w1_raw"]
+        tenants = ["tab_plane", "tab_codes0", "tab_codes1", "w1_plane_raw"]
         pages = [sb("page%d" % i, [P, T2], F32, tag=tenants[i]) for i in range(PACK)]
         for i in range(PACK):
             nc.gpsimd.memset(pages[i][:], 0.0)
@@ -163,7 +164,6 @@ def tile_list_heating_loop_balance_kernel(
         zct = [sb("zct%d" % i, [P, T2], BF16) for i in range(PACK)]
         zc_codes = [sb("zc_codes%d" % i, [P, PASSES2 * P], U32) for i in range(PACK)]
         zc_plane = [sb("zc_plane%d" % i, [P, PASSES2 * P], U8) for i in range(PACK)]
-        wv_round = sb("wv_round", [P, N * PACK], BF16)
         wv_codes = sb("wv_codes", [P, N], U32)
         wv_plane = sb("wv_plane", [P, N], U8)
         acc = {}
@@ -181,16 +181,12 @@ def tile_list_heating_loop_balance_kernel(
         def couple(i):
             for a in range(PASSES2):
                 cols = slice(a * 512, (a + 1) * 512)
-                nc.vector.tensor_tensor(
-                    zc[i][:, cols].rearrange("p (u q e) -> p u q e", u=2, e=2),
-                    z_pair[i // 2][:, i % 2, cols].rearrange("p (q u e) -> p u q e", u=2, e=2),
-                    cond_sb[i][:, cols].rearrange("p (q u e) -> p u q e", u=2, e=2),
-                    MULT,
-                )
+                nc.vector.tensor_tensor(zc[i][:, cols], z_pair[i // 2][:, i % 2, cols], cond_sb[i][:, cols], MULT)
             turned = bank(7, "turned%d" % i, [P, 2 * PASSES2, P])
             words = zc[i][:].bitcast(F32)
-            for b in range(2 * PASSES2):
-                nc.tensor.transpose(turned[:, b, :], words[:, b * P : (b + 1) * P], ident[:])
+            for a in range(PASSES2):
+                for u in range(2):
+                    nc.tensor.transpose(turned[:, 2 * a + u, :], words[:, 2 * P * a + u : 2 * P * (a + 1) : 2], ident[:])
             nc.scalar.copy(
                 zct[i][:].bitcast(F32).rearrange("q (a n u) -> q a n u", a=PASSES2, u=2),
                 turned[:].rearrange("q (a u) n -> q a n u", u=2),
@@ -247,6 +243,7 @@ def tile_list_heating_loop_balance_kernel(
         halves(0)
         couple(0)
         scatter(1)
+        wv_round = sb("wv_round", [P, N * PACK], BF16, tag="zc0")
         nc.scalar.copy(
             wv_round[:].rearrange("p (t m j) -> p m t j", t=PACK, j=PACK),
             wv_raw[:].rearrange("p j (m t) -> p m t j", t=PACK),
@@ -254,8 +251,8 @@ def tile_list_heating_loop_balance_kernel(
         quantize_zc(0)
         for c in range(CHUNKS):
             right(0, c, True, False)
-        nc.vector.quantize_mx(out=wv_codes[:].bitcast(FP8X4), scales=wv_plane[:], in_=wv_round[:])
         halves(1)
+        nc.vector.quantize_mx(out=wv_codes[:].bitcast(FP8X4), scales=wv_plane[:], in_=wv_round[:])
         couple(1)
         scatter(2)
         for c in range(CHUNKS):

@@ -15,7 +15,8 @@ U8 = mybir.dt.uint8
 FP8X4 = mybir.dt.float8_e4m3fn_x4
 FP4X4 = mybir.dt.float4_e2m1fn_x4
 MULT = mybir.AluOpType.mult
-ADD = mybir.AluOpType.add
+SUBTRACT = mybir.AluOpType.subtract
+COPY = mybir.ActivationFunctionType.Copy
 GELU = mybir.ActivationFunctionType.Gelu_apprx_tanh
 
 P = 128
@@ -55,10 +56,6 @@ def tile_list_heating_loop_balance_kernel(
         nc.vector.memset(w1_plane_raw[:].bitcast(I32), 0)
         nc.vector.memset(wc_plane[:].bitcast(I32), 0)
 
-        warm_in = sb("warm_in", [P, 8], F32)
-        warm_out = sb("warm_out", [P, 8], F32)
-        nc.vector.memset(warm_in[:], 0.0)
-        nc.scalar.activation(warm_out[:], warm_in[:], GELU)
         ident = sb("ident", [P, P], F32)
         make_identity(nc, ident[:])
 
@@ -76,7 +73,7 @@ def tile_list_heating_loop_balance_kernel(
                 tab_scales[:, 4 * q : 4 * q + 4, :].bitcast(I32).rearrange("a r w -> r a w"),
             )
         for a in range(PASSES1):
-            if a == PASSES1 - 1:
+            if a == 1:
                 for q in range(QUADS):
                     nc.sync.dma_start(
                         w1_plane_raw[32 * q : 32 * q + 4, :].bitcast(I32).rearrange("r (a w) -> r a w", a=PASSES1),
@@ -93,21 +90,22 @@ def tile_list_heating_loop_balance_kernel(
         cond_sb = [sb("cond%d" % i, [P, T2], F32) for i in range(PACK)]
         wc_codes = [sb("wc_codes%d" % a, [P, T2], U32) for a in range(PASSES2)]
         wv_raw = sb("wv_raw", [P, PACK, N], F32)
-        for i in range(PACK):
-            nc.sync.dma_start(cond_sb[i][:], cond_rows[:, i, :])
+        nc.sync.dma_start(heat_sb[0][:], heat_rows[:, 0, :])
+        nc.sync.dma_start(cond_sb[0][:], cond_rows[:, 0, :])
+        nc.sync.dma_start(wv_raw[:], wv.rearrange("(p j) c -> p j c", j=PACK))
+        nc.sync.dma_start(heat_sb[1][:], heat_rows[:, 1, :])
+        nc.sync.dma_start(cond_sb[1][:], cond_rows[:, 1, :])
+        for q in range(QUADS):
+            nc.sync.dma_start(
+                wc_plane[32 * q : 32 * q + 4 * PASSES2, :].bitcast(I32),
+                wc_scales[:, 4 * q : 4 * q + 4, :].bitcast(I32),
+            )
+        for a in range(PASSES2):
+            nc.sync.dma_start(wc_codes[a][:].bitcast(I32), wc_words[a].rearrange("p c i -> p (c i)").bitcast(I32))
+        for i in range(2, PACK):
             nc.sync.dma_start(heat_sb[i][:], heat_rows[:, i, :])
-            if i == 0:
-                nc.sync.dma_start(wv_raw[:], wv.rearrange("(p j) c -> p j c", j=PACK))
-            if i == 1:
-                for q in range(QUADS):
-                    nc.sync.dma_start(
-                        wc_plane[32 * q : 32 * q + 4 * PASSES2, :].bitcast(I32),
-                        wc_scales[:, 4 * q : 4 * q + 4, :].bitcast(I32),
-                    )
-                for a in range(PASSES2):
-                    nc.sync.dma_start(
-                        wc_codes[a][:].bitcast(I32), wc_words[a].rearrange("p c i -> p (c i)").bitcast(I32)
-                    )
+        for i in (3, 2):
+            nc.sync.dma_start(cond_sb[i][:], cond_rows[:, i, :])
 
         w1_codes = sb("w1_codes", [P, PACK, PASSES1 * 2 * P], U8)
         nc.vector.tensor_copy(
@@ -116,14 +114,10 @@ def tile_list_heating_loop_balance_kernel(
         )
         w1_plane = {}
 
-        def deal_plane(name, first, count, tag=None):
-            plane = sb(name, [P, count * PASSES1 * P], U8, tag=tag)
-            nc.vector.tensor_copy(
-                plane[:].rearrange("p (i h c) -> p h i c", i=count, h=2),
-                w1_plane_raw[:].rearrange("p (h c i) -> p h i c", i=PACK, h=2)[:, :, first : first + count, :],
-            )
-            for k in range(count):
-                w1_plane[first + k] = plane[:, k * PASSES1 * P : (k + 1) * PASSES1 * P]
+        def deal_plane(u, tag=None):
+            plane = sb("w1_plane%d" % u, [P, 2, PASSES1 * P], U8, tag=tag)
+            nc.vector.tensor_copy(plane[:], w1_plane_raw[:].rearrange("p (c i) -> p i c", i=PACK)[:, 2 * u : 2 * u + 2, :])
+            w1_plane[2 * u], w1_plane[2 * u + 1] = plane[:, 0, :], plane[:, 1, :]
 
         def first_product(i, a):
             nc.tensor.matmul_mx(
@@ -136,54 +130,59 @@ def tile_list_heating_loop_balance_kernel(
                 stop=(a == PASSES1 - 1),
             )
 
-        deal_plane("w1_plane_first", 0, 1)
         v_plane = [sb("v_plane%d" % a, [P, S], U8) for a in range(PASSES1)]
         v_codes = [sb("v_codes%d" % a, [P, S], U32) for a in range(PASSES1)]
         for a in range(PASSES1):
             nc.vector.tensor_copy(v_plane[a][:], tab_plane[:, a * T : (a + 1) * T].indirect(picks[:]))
-        neg_gain = sb("neg_gain", [P, PACK], F32)
         d = [bank(4 + (i + 3) % PACK, "d%d" % i, [P, S]) for i in range(PACK)]
         for a in range(PASSES1):
             nc.vector.tensor_copy(v_codes[a][:], tab_codes[a][:].indirect(picks[:]))
-            first_product(0, a)
-        deal_plane("w1_plane_rest", 1, PACK - 1, tag="tab_codes2")
-        for i in range(1, PACK):
+            if a == 0:
+                deal_plane(0)
+            for i in range(2):
+                first_product(i, a)
+        deal_plane(1, tag="tab_codes2")
+        for i in range(2, PACK):
             for a in range(PASSES1):
                 first_product(i, a)
-        nc.vector.tensor_scalar(neg_gain[:], gain_sb[:], -1.0, None, MULT)
-        tenants = ["tab_plane", "tab_codes0", "tab_codes1", "w1_plane_raw"]
-        pages = [sb("page%d" % i, [P, T2], F32, tag=tenants[i]) for i in range(PACK)]
-        for i in range(PACK):
-            nc.gpsimd.memset(pages[i][:], 0.0)
 
-        z_pair = [sb("z_pair%d" % u, [P, 2, T2], F32) for u in range(2)]
         z_round = [sb("z_round%d" % c, [P, CHUNK, PACK], BF16) for c in range(CHUNKS)]
         z_codes = [sb("z_codes%d" % c, [P, CHUNK], U32) for c in range(CHUNKS)]
         z_plane = [sb("z_plane%d" % c, [P, CHUNK], U8) for c in range(CHUNKS)]
-        zc = [sb("zc%d" % i, [P, T2], BF16) for i in range(PACK)]
         zct = [sb("zct%d" % i, [P, T2], BF16) for i in range(PACK)]
         zc_codes = [sb("zc_codes%d" % i, [P, PASSES2 * P], U32) for i in range(PACK)]
-        zc_plane = [sb("zc_plane%d" % i, [P, PASSES2 * P], U8) for i in range(PACK)]
-        wv_codes = sb("wv_codes", [P, N], U32)
+        zc_plane = {}
         wv_plane = sb("wv_plane", [P, N], U8)
         acc = {}
+        pages, z = {}, {}
+
+        def clear(i, tag=None):
+            pages[i] = sb("page%d" % i, [P, T2], F32, tag=tag)
+            nc.gpsimd.memset(pages[i][:], 0.0)
 
         def scatter(i):
-            act = sb("act%d" % i, [P, S], F32, tag="heat%d" % (i - 1) if i else None)
-            nc.scalar.activation(act[:], d[i][:], GELU, bias=bias[:, i : i + 1])
-            nc.vector.tensor_tensor(pages[i][:].indirect(places[:]), act[:], wgs_sb[:], MULT)
+            nc.vector.tensor_copy(pages[i][:].indirect(places[:]), weighted[i][:])
 
-        def remainder(i, cols):
-            nc.vector.scalar_tensor_tensor(
-                z_pair[i // 2][:, i % 2, cols], pages[i][:, cols], neg_gain[:, i : i + 1], heat_sb[i][:, cols], MULT, ADD
-            )
+        def weigh(i):
+            act = sb("act%d" % i, [P, S], F32)
+            out = sb("weighted%d" % i, [P, S], F32)
+            nc.scalar.activation(act[:], d[i][:], GELU, bias=bias[:, i : i + 1])
+            if i == 0:
+                nc.vector.scalar_tensor_tensor(out[:], act[:], gain_sb[:, 0:1], wgs_sb[:], MULT, MULT)
+            else:
+                h = sb("h%d" % i, [P, S], F32)
+                nc.scalar.activation(h[:], act[:], COPY, scale=gain_sb[:, i : i + 1])
+                nc.gpsimd.tensor_tensor(out[:], h[:], wgs_sb[:], MULT)
+            return out
+
+        def remainder(engine, i, cols):
+            engine.tensor_tensor(z[i][:, cols], heat_sb[i][:, cols], pages[i][:, cols], SUBTRACT)
 
         def couple(i):
-            for a in range(PASSES2):
-                cols = slice(a * 512, (a + 1) * 512)
-                nc.vector.tensor_tensor(zc[i][:, cols], z_pair[i // 2][:, i % 2, cols], cond_sb[i][:, cols], MULT)
+            zc = sb("zc%d" % i, [P, T2], BF16)
+            nc.vector.tensor_tensor(zc[:], z[i], cond_sb[i][:], MULT)
             turned = bank(7, "turned%d" % i, [P, 2 * PASSES2, P])
-            words = zc[i][:].bitcast(F32)
+            words = zc[:].bitcast(F32)
             for a in range(PASSES2):
                 for u in range(2):
                     nc.tensor.transpose(turned[:, 2 * a + u, :], words[:, 2 * P * a + u : 2 * P * (a + 1) : 2], ident[:])
@@ -192,16 +191,12 @@ def tile_list_heating_loop_balance_kernel(
                 turned[:].rearrange("q (a u) n -> q a n u", u=2),
             )
 
-        def quantize_zc(i):
+        def quantize_zc(i, tag=None):
+            zc_plane[i] = sb("zc_plane%d" % i, [P, PASSES2 * P], U8, tag=tag)
             nc.vector.quantize_mx(out=zc_codes[i][:].bitcast(FP8X4), scales=zc_plane[i][:], in_=zct[i][:])
 
-        def round_z(u, c, on_vector):
-            dst = z_round[c][:, :, 2 * u : 2 * u + 2]
-            src = z_pair[u][:, :, c * CHUNK : (c + 1) * CHUNK].rearrange("p e m -> p m e")
-            if on_vector:
-                nc.vector.tensor_copy(dst, src)
-            else:
-                nc.scalar.copy(dst, src)
+        def round_z(copy, c, slots, rows):
+            copy(z_round[c][:, :, slots], rows[:, :, c * CHUNK : (c + 1) * CHUNK].rearrange("p e m -> p m e"))
 
         def quantize_z(c):
             nc.vector.quantize_mx(
@@ -235,49 +230,72 @@ def tile_list_heating_loop_balance_kernel(
                 stop=last,
             )
 
-        def halves(i):
-            remainder(i, slice(0, T2 // 2))
-            remainder(i, slice(T2 // 2, T2))
-
+        halves = [slice(0, T2 // 2), slice(T2 // 2, T2)]
+        whole = slice(0, T2)
+        clear(0)
+        clear(1)
+        weighted = [weigh(i) for i in range(PACK)]
         scatter(0)
-        halves(0)
-        couple(0)
         scatter(1)
-        wv_round = sb("wv_round", [P, N * PACK], BF16, tag="zc0")
+        z[0] = sb("z0", [P, T2], F32, tag="h3")[:]
+        remainder(nc.gpsimd, 0, whole)
+        clear(2, tag="heat0")
+        couple(0)
+        for c in range(CHUNKS):
+            round_z(nc.scalar.copy, c, slice(0, 1), z[0].unsqueeze(1))
+        scatter(2)
+        z[1] = sb("z1", [P, T2], F32, tag="cond0")[:]
+        remainder(nc.gpsimd, 1, whole)
+        clear(3, tag="heat1")
+        wv_round = sb("wv_round", [P, N * PACK], BF16)
         nc.scalar.copy(
             wv_round[:].rearrange("p (t m j) -> p m t j", t=PACK, j=PACK),
             wv_raw[:].rearrange("p j (m t) -> p m t j", t=PACK),
         )
-        quantize_zc(0)
+        wv_codes = sb("wv_codes", [P, N], U32, tag="weighted2")
+        nc.vector.quantize_mx(out=wv_codes[:].bitcast(FP8X4), scales=wv_plane[:], in_=wv_round[:])
+        quantize_zc(0, tag="wv_round")
         for c in range(CHUNKS):
             right(0, c, True, False)
-        halves(1)
-        nc.vector.quantize_mx(out=wv_codes[:].bitcast(FP8X4), scales=wv_plane[:], in_=wv_round[:])
         couple(1)
-        scatter(2)
         for c in range(CHUNKS):
-            round_z(0, c, False)
-        quantize_zc(1)
+            round_z(nc.scalar.copy, c, slice(1, 2), z[1].unsqueeze(1))
+        scatter(3)
+        z_last = sb("z_last", [P, 2, T2], F32, tag="cond1")
+        z[2], z[3] = z_last[:, 0, :], z_last[:, 1, :]
+        remainder(nc.gpsimd, 2, whole)
+        for cols in halves:
+            remainder(nc.vector, 3, cols)
+        quantize_zc(1, tag="weighted3")
         for c in range(CHUNKS):
             right(1, c, False, False)
-        halves(2)
-        couple(2)
-        scatter(3)
-        quantize_zc(2)
-        for c in range(CHUNKS - 1):
-            right(2, c, True, False)
-        halves(3)
-        round_z(1, 0, False)
-        round_z(1, 1, False)
+        round_z(nc.scalar.copy, 0, slice(2, 4), z_last[:])
+        round_z(nc.scalar.copy, 1, slice(2, 4), z_last[:])
         couple(3)
-        right(2, CHUNKS - 1, True, False)
+        couple(2)
         quantize_z(0)
         quantize_z(1)
-        round_z(1, 2, True)
         quantize_zc(3)
-        round_z(1, 3, True)
+        round_z(nc.vector.tensor_copy, 2, slice(2, 4), z_last[:])
+        round_z(nc.vector.tensor_copy, 3, slice(2, 4), z_last[:])
+        quantize_zc(2)
         quantize_z(2)
         quantize_z(3)
+        for c in range(CHUNKS - 1):
+            right(3, c, True, False)
+        for c in range(CHUNKS):
+            left(0, c, False)
+            left(1, c, True)
+            if c == CHUNKS - 1:
+                right(3, c, True, False)
+            if c < 2:
+                left(2, c, False)
+                left(3, c, False)
+                right(2, c, False, True)
+            else:
+                right(2, c, False, False)
+                left(2, c, False)
+                left(3, c, True)
 
         y = [sb("y%d" % c, [P, PACK, CHUNK], F32) for c in range(CHUNKS)]
         y_round = [sb("y_round%d" % c, [P, CHUNK * PACK], BF16) for c in range(CHUNKS)]
@@ -285,22 +303,28 @@ def tile_list_heating_loop_balance_kernel(
         y_plane = sb("y_plane", [P, T2], U8)
         out_rows = out_0.rearrange("(p i) m -> p i m", i=PACK)
         out_words = out_1[0].rearrange("p m t -> p (m t)").bitcast(I32)
-        for c in range(CHUNKS):
+
+        def empty(u, c):
             cols = slice(c * CHUNK, (c + 1) * CHUNK)
-            left(0, c, False)
-            left(1, c, True)
-            left(2, c, False)
-            left(3, c, False)
-            right(3, c, False, True)
-            for u in range(2):
-                nc.scalar.copy(y[c][:, 2 * u : 2 * u + 2, :], acc[u, c][:])
-                nc.sync.dma_start(out_rows[:, 2 * u : 2 * u + 2, cols], y[c][:, 2 * u : 2 * u + 2, :])
-            nc.vector.tensor_copy(
+            nc.scalar.copy(y[c][:, 2 * u : 2 * u + 2, :], acc[u, c][:])
+            nc.sync.dma_start(out_rows[:, 2 * u : 2 * u + 2, cols], y[c][:, 2 * u : 2 * u + 2, :])
+
+        def weave(c, copy):
+            copy(
                 y_round[c][:].rearrange("p (m j i) -> p m i j", j=4, i=PACK),
                 y[c][:].rearrange("p i (m j) -> p m i j", j=4),
             )
+
+        def quantize_y(c):
+            cols = slice(c * CHUNK, (c + 1) * CHUNK)
             nc.vector.quantize_mx(out=y_codes[:, cols].bitcast(FP8X4), scales=y_plane[:, cols], in_=y_round[c][:])
             nc.sync.dma_start(out_words[:, cols], y_codes[:, cols].bitcast(I32))
+
+        for c in range(CHUNKS):
+            empty(0, c)
+            empty(1, c)
+            weave(c, nc.vector.tensor_copy)
+            quantize_y(c)
         for q in range(QUADS):
             nc.sync.dma_start(
                 out_2[0, 4 * q : 4 * q + 4, :].bitcast(I32), y_plane[32 * q : 32 * q + 4, :].bitcast(I32)

@@ -154,7 +154,7 @@ def tile_list_heating_loop_balance_kernel(
         zc_plane = {}
         wv_plane = sb("wv_plane", [P, N], U8)
         acc = {}
-        pages, z = {}, {}
+        pages, z, act, weighted = {}, {}, {}, {}
 
         def clear(i, tag=None):
             pages[i] = sb("page%d" % i, [P, T2], F32, tag=tag)
@@ -163,25 +163,27 @@ def tile_list_heating_loop_balance_kernel(
         def scatter(i):
             nc.vector.tensor_copy(pages[i][:].indirect(places[:]), weighted[i][:])
 
-        def weigh(i):
-            act = sb("act%d" % i, [P, S], F32)
-            out = sb("weighted%d" % i, [P, S], F32)
-            nc.scalar.activation(act[:], d[i][:], GELU, bias=bias[:, i : i + 1])
-            if i == 0:
-                nc.vector.scalar_tensor_tensor(out[:], act[:], gain_sb[:, 0:1], wgs_sb[:], MULT, MULT)
-            else:
-                h = sb("h%d" % i, [P, S], F32)
-                nc.scalar.activation(h[:], act[:], COPY, scale=gain_sb[:, i : i + 1])
-                nc.gpsimd.tensor_tensor(out[:], h[:], wgs_sb[:], MULT)
-            return out
+        def gelu(i):
+            act[i] = sb("act%d" % i, [P, S], F32)
+            nc.scalar.activation(act[i][:], d[i][:], GELU, bias=bias[:, i : i + 1])
+
+        def weigh_on_vector(i, tag=None):
+            weighted[i] = sb("weighted%d" % i, [P, S], F32, tag=tag)
+            nc.vector.scalar_tensor_tensor(weighted[i][:], act[i][:], gain_sb[:, i : i + 1], wgs_sb[:], MULT, MULT)
+
+        def weigh_on_gpsimd(i):
+            h = sb("h%d" % i, [P, S], F32)
+            weighted[i] = sb("weighted%d" % i, [P, S], F32)
+            nc.scalar.activation(h[:], act[i][:], COPY, scale=gain_sb[:, i : i + 1])
+            nc.gpsimd.tensor_tensor(weighted[i][:], h[:], wgs_sb[:], MULT)
 
         def remainder(engine, i, cols):
             engine.tensor_tensor(z[i][:, cols], heat_sb[i][:, cols], pages[i][:, cols], SUBTRACT)
 
-        def couple(i):
+        def couple(i, b=7):
             zc = sb("zc%d" % i, [P, T2], BF16)
             nc.vector.tensor_tensor(zc[:], z[i], cond_sb[i][:], MULT)
-            turned = bank(7, "turned%d" % i, [P, 2 * PASSES2, P])
+            turned = bank(b, "turned%d" % i, [P, 2 * PASSES2, P])
             words = zc[:].bitcast(F32)
             for a in range(PASSES2):
                 for u in range(2):
@@ -234,10 +236,16 @@ def tile_list_heating_loop_balance_kernel(
         whole = slice(0, T2)
         clear(0)
         clear(1)
-        weighted = [weigh(i) for i in range(PACK)]
+        clear(3, tag="tab_plane")
+        gelu(0)
+        weigh_on_vector(0)
+        for i in (1, 2):
+            gelu(i)
+            weigh_on_gpsimd(i)
+        gelu(3)
         scatter(0)
         scatter(1)
-        z[0] = sb("z0", [P, T2], F32, tag="h3")[:]
+        z[0] = sb("z0", [P, T2], F32, tag="h2")[:]
         remainder(nc.gpsimd, 0, whole)
         clear(2, tag="heat0")
         couple(0)
@@ -246,7 +254,6 @@ def tile_list_heating_loop_balance_kernel(
         scatter(2)
         z[1] = sb("z1", [P, T2], F32, tag="cond0")[:]
         remainder(nc.gpsimd, 1, whole)
-        clear(3, tag="heat1")
         wv_round = sb("wv_round", [P, N * PACK], BF16)
         nc.scalar.copy(
             wv_round[:].rearrange("p (t m j) -> p m t j", t=PACK, j=PACK),
@@ -260,23 +267,24 @@ def tile_list_heating_loop_balance_kernel(
         couple(1)
         for c in range(CHUNKS):
             round_z(nc.scalar.copy, c, slice(1, 2), z[1].unsqueeze(1))
+        weigh_on_vector(3, tag="cond1")
         scatter(3)
-        z_last = sb("z_last", [P, 2, T2], F32, tag="cond1")
+        z_last = sb("z_last", [P, 2, T2], F32, tag="act3")
         z[2], z[3] = z_last[:, 0, :], z_last[:, 1, :]
         remainder(nc.gpsimd, 2, whole)
         for cols in halves:
             remainder(nc.vector, 3, cols)
-        quantize_zc(1, tag="weighted3")
+        quantize_zc(1, tag="cond1")
         for c in range(CHUNKS):
             right(1, c, False, False)
         round_z(nc.scalar.copy, 0, slice(2, 4), z_last[:])
         round_z(nc.scalar.copy, 1, slice(2, 4), z_last[:])
-        couple(3)
+        round_z(nc.scalar.copy, 2, slice(2, 4), z_last[:])
+        couple(3, b=6)
         couple(2)
         quantize_z(0)
         quantize_z(1)
         quantize_zc(3)
-        round_z(nc.vector.tensor_copy, 2, slice(2, 4), z_last[:])
         round_z(nc.vector.tensor_copy, 3, slice(2, 4), z_last[:])
         quantize_zc(2)
         quantize_z(2)
@@ -323,7 +331,12 @@ def tile_list_heating_loop_balance_kernel(
         for c in range(CHUNKS):
             empty(0, c)
             empty(1, c)
-            weave(c, nc.vector.tensor_copy)
+        weave(0, nc.vector.tensor_copy)
+        weave(1, nc.vector.tensor_copy)
+        quantize_y(0)
+        weave(2, nc.vector.tensor_copy)
+        weave(3, nc.scalar.copy)
+        for c in range(1, CHUNKS):
             quantize_y(c)
         for q in range(QUADS):
             nc.sync.dma_start(

@@ -24,6 +24,12 @@ PACK = 4
 QUADS = 4
 PASSES1 = K // 512
 PASSES2 = T2 // 512
+KIB = 1024
+ROW0 = P - 16 * PASSES1
+TAB_AT = [0, 12 * KIB, 30 * KIB]
+W1_AT = 8 * KIB
+ROWS_AT = 11 * KIB
+V_AT = [44 * KIB, 52 * KIB, 60 * KIB]
 CHUNK = 256
 CHUNKS = T2 // CHUNK
 
@@ -43,53 +49,100 @@ def tile_list_heating_loop_balance_kernel(
         def bank(b, name, shape):
             return psum.tile(shape, F32, name=name, tag="bank%d" % b)
 
+        shared = ctx.enter_context(tc.tile_pool(name="shared", bufs=1))
+
+        def at(name, shape, dtype, offset):
+            return shared.tile(shape, dtype, name=name, tag=name, align_bytes=64, offset=offset)
+
         picks = keep.tile([P, S // 16], U16, name="picks")
         places = keep.tile([P, S // 16], U16, name="places")
-        w1_plane_raw = sb("w1_plane_raw", [P, PASSES1 * H], U8)
-        tab_plane = sb("tab_plane", [P, PASSES1 * T], U8)
-        w1_raw = sb("w1_raw", [P, PASSES1 * 2 * H], U8)
-        tab_codes = [sb("tab_codes%d" % a, [P, T], U32) for a in range(PASSES1)]
-        wc_plane = sb("wc_plane", [P, T2], U8)
+        tab_rows = sb("tab_rows", [P, T], U8)
+        w1_rows = sb("w1_rows", [P, H], U8)
+        tab_codes = [at("tab_codes%d" % a, [P, T], U32, TAB_AT[a]) for a in range(PASSES1)]
+        w1_raw = at("w1_raw", [P, PASSES1 * 2 * H], U8, W1_AT)
+        both_rows = at("both_rows", [P, S + H], U8, ROWS_AT)
+        v_codes = [at("v_codes%d" % a, [P, S], U32, V_AT[a]) for a in range(PASSES1)]
+        planes = sb("planes", [P, PASSES1 * (S + H)], U8)
 
-        nc.gpsimd.memset(tab_plane[:, :T].bitcast(I32), 0)
-        nc.vector.memset(tab_plane[:, T:].bitcast(I32), 0)
-        nc.vector.memset(w1_plane_raw[:].bitcast(I32), 0)
-        nc.vector.memset(wc_plane[:].bitcast(I32), 0)
+        nc.gpsimd.memset(w1_rows[:ROW0, :].bitcast(I32), 0)
+        nc.gpsimd.memset(tab_rows[:ROW0, :].bitcast(I32), 0)
+        nc.vector.memset(planes[:].bitcast(I32), 0)
 
         ident = sb("ident", [P, P], F32)
         make_identity(nc, ident[:])
 
         bias = sb("bias", [P, PACK], F32)
         gain_sb = sb("gain_sb", [P, PACK], F32)
-        nc.sync.dma_start(picks[:], offs)
-        nc.sync.dma_start(bias[:], b1.rearrange("(p i) -> p i", i=PACK))
-        nc.sync.dma_start(
-            w1_raw[:].bitcast(I32).rearrange("p (a w) -> p a w", a=PASSES1),
-            w1_words.bitcast(I32).rearrange("a p w -> p a w"),
-        )
-        for q in range(QUADS):
-            nc.sync.dma_start(
-                tab_plane[32 * q : 32 * q + 4, :].bitcast(I32).rearrange("r (a w) -> r a w", a=PASSES1),
-                tab_scales[:, 4 * q : 4 * q + 4, :].bitcast(I32).rearrange("a r w -> r a w"),
-            )
-        for a in range(PASSES1):
-            if a == 1:
-                for q in range(QUADS):
-                    nc.sync.dma_start(
-                        w1_plane_raw[32 * q : 32 * q + 4, :].bitcast(I32).rearrange("r (a w) -> r a w", a=PASSES1),
-                        w1_scales[:, 4 * q : 4 * q + 4, :].bitcast(I32).rearrange("a r w -> r a w"),
-                    )
-            nc.sync.dma_start(tab_codes[a][:].bitcast(I32), tab_words[a].rearrange("p t i -> p (t i)").bitcast(I32))
         wgs_sb = sb("wgs_sb", [P, S], F32)
-        nc.sync.dma_start(places[:], offs2)
+        nc.sync.dma_start(picks[:], offs)
+        for a in range(PASSES1):
+            nc.scalar.dma_start(tab_rows[ROW0 + a : P : PASSES1, :].bitcast(I32), tab_scales[a].bitcast(I32))
+            nc.sync.dma_start(w1_rows[ROW0 + a : P : PASSES1, :].bitcast(I32), w1_scales[a].bitcast(I32))
+        for a in range(PASSES1):
+            nc.sync.dma_start(tab_codes[a][:].bitcast(I32), tab_words[a].rearrange("p t i -> p (t i)").bitcast(I32))
+            if a == 0:
+                nc.sync.dma_start(bias[:], b1.rearrange("(p i) -> p i", i=PACK))
+                nc.sync.dma_start(gain_sb[:], gain.rearrange("(p i) -> p i", i=PACK))
+                nc.sync.dma_start(
+                    w1_raw[:].bitcast(I32).rearrange("p (a w) -> p a w", a=PASSES1),
+                    w1_words.bitcast(I32).rearrange("a p w -> p a w"),
+                )
         nc.sync.dma_start(wgs_sb[:], wgs)
-        nc.sync.dma_start(gain_sb[:], gain.rearrange("(p i) -> p i", i=PACK))
+        nc.sync.dma_start(places[:], offs2)
+
+        v_rows = sb("v_rows", [P, S], U8)
+        nc.vector.tensor_copy(
+            both_rows[:, S:].rearrange("p (i c) -> p i c", i=PACK), w1_rows[:].rearrange("p (c i) -> p i c", i=PACK)
+        )
+        nc.vector.tensor_copy(v_rows[:], tab_rows[:].indirect(picks[:]))
+        nc.vector.tensor_copy(both_rows[:, :S].bitcast(I32), v_rows[:].bitcast(I32))
+        for q in range(QUADS):
+            first = ROW0 + 4 * PASSES1 * q
+            nc.scalar.dma_start(
+                planes[32 * q : 32 * q + 4, :].bitcast(I32), both_rows[first : first + 4 * PASSES1, :].bitcast(I32)
+            )
+        w1_codes = []
+
+        def deal_words(u, pair):
+            nc.vector.tensor_copy(
+                pair[:].bitcast(U16).rearrange("p (i c) -> p i c", i=2),
+                w1_raw[:].bitcast(U16).rearrange("p (c i) -> p i c", i=PACK)[:, 2 * u : 2 * u + 2, :],
+            )
+            w1_codes.extend([pair[:, : PASSES1 * 2 * P], pair[:, PASSES1 * 2 * P :]])
+
+        for a in range(PASSES1):
+            nc.vector.tensor_copy(v_codes[a][:], tab_codes[a][:].indirect(picks[:]))
+            if a == 0:
+                deal_words(0, sb("w1_pair0", [P, PASSES1 * 4 * P], U8))
+        deal_words(1, at("w1_pair1", [P, PASSES1 * 4 * P], U8, TAB_AT[2] + KIB))
+        d = [bank(4 + (i + 3) % PACK, "d%d" % i, [P, S]) for i in range(PACK)]
+
+        def first_product(i, a):
+            plane = planes[:, a * (S + H) : (a + 1) * (S + H)]
+            nc.tensor.matmul_mx(
+                out=d[i][:],
+                lhsT=w1_codes[i][:, 2 * a * P : 2 * (a + 1) * P].bitcast(FP4X4),
+                lhsT_scale=plane[:, S + i * P : S + (i + 1) * P],
+                rhs=v_codes[a][:].bitcast(FP8X4),
+                rhs_scale=plane[:, :S],
+                start=(a == 0),
+                stop=(a == PASSES1 - 1),
+            )
+
+        for i in range(PACK):
+            for a in range(PASSES1):
+                first_product(i, a)
+
+        heat_at = [TAB_AT[1] + 3 * KIB, TAB_AT[2] + 3 * KIB, V_AT[1] - 3 * KIB, V_AT[1] + KIB]
+        cond_at = [TAB_AT[1] + 7 * KIB, TAB_AT[2] + 7 * KIB, V_AT[2] + KIB, V_AT[2] - 3 * KIB]
+        heat_sb = [at("heat%d" % i, [P, T2], F32, heat_at[i]) for i in range(PACK)]
+        cond_sb = [at("cond%d" % i, [P, T2], F32, cond_at[i]) for i in range(PACK)]
+        wc_codes = [at("wc_codes%d" % a, [P, T2], U32, V_AT[0] - 3 * KIB + 4 * KIB * a) for a in range(PASSES2)]
+        wv_raw = at("wv_raw", [P, PACK, N], F32, TAB_AT[2] - 7 * KIB)
+        wc_plane = at("wc_plane", [P, T2], U8, ROWS_AT)
+        nc.gpsimd.memset(wc_plane[:].bitcast(I32), 0)
         heat_rows = heat.rearrange("(p i) m -> p i m", i=PACK)
         cond_rows = cond.rearrange("(p i) m -> p i m", i=PACK)
-        heat_sb = [sb("heat%d" % i, [P, T2], F32) for i in range(PACK)]
-        cond_sb = [sb("cond%d" % i, [P, T2], F32) for i in range(PACK)]
-        wc_codes = [sb("wc_codes%d" % a, [P, T2], U32) for a in range(PASSES2)]
-        wv_raw = sb("wv_raw", [P, PACK, N], F32)
         nc.sync.dma_start(heat_sb[0][:], heat_rows[:, 0, :])
         nc.sync.dma_start(cond_sb[0][:], cond_rows[:, 0, :])
         nc.sync.dma_start(wv_raw[:], wv.rearrange("(p j) c -> p j c", j=PACK))
@@ -107,44 +160,12 @@ def tile_list_heating_loop_balance_kernel(
         for i in (3, 2):
             nc.sync.dma_start(cond_sb[i][:], cond_rows[:, i, :])
 
-        w1_codes = sb("w1_codes", [P, PACK, PASSES1 * 2 * P], U8)
-        nc.vector.tensor_copy(
-            w1_codes[:].rearrange("p i b -> p (i b)").bitcast(U16).rearrange("p (i c) -> p i c", i=PACK),
-            w1_raw[:].bitcast(U16).rearrange("p (c i) -> p i c", i=PACK),
-        )
-        w1_plane = {}
+        left_by = {"heat0": heat_at[0], "cond0": cond_at[0], "cond1": cond_at[1]}
 
-        def deal_plane(u, tag=None):
-            plane = sb("w1_plane%d" % u, [P, 2, PASSES1 * P], U8, tag=tag)
-            nc.vector.tensor_copy(plane[:], w1_plane_raw[:].rearrange("p (c i) -> p i c", i=PACK)[:, 2 * u : 2 * u + 2, :])
-            w1_plane[2 * u], w1_plane[2 * u + 1] = plane[:, 0, :], plane[:, 1, :]
-
-        def first_product(i, a):
-            nc.tensor.matmul_mx(
-                out=d[i][:],
-                lhsT=w1_codes[:, i, 2 * a * P : 2 * (a + 1) * P].bitcast(FP4X4),
-                lhsT_scale=w1_plane[i][:, a * P : (a + 1) * P],
-                rhs=v_codes[a][:].bitcast(FP8X4),
-                rhs_scale=v_plane[a][:],
-                start=(a == 0),
-                stop=(a == PASSES1 - 1),
-            )
-
-        v_plane = [sb("v_plane%d" % a, [P, S], U8) for a in range(PASSES1)]
-        v_codes = [sb("v_codes%d" % a, [P, S], U32) for a in range(PASSES1)]
-        for a in range(PASSES1):
-            nc.vector.tensor_copy(v_plane[a][:], tab_plane[:, a * T : (a + 1) * T].indirect(picks[:]))
-        d = [bank(4 + (i + 3) % PACK, "d%d" % i, [P, S]) for i in range(PACK)]
-        for a in range(PASSES1):
-            nc.vector.tensor_copy(v_codes[a][:], tab_codes[a][:].indirect(picks[:]))
-            if a == 0:
-                deal_plane(0)
-            for i in range(2):
-                first_product(i, a)
-        deal_plane(1, tag="tab_codes2")
-        for i in range(2, PACK):
-            for a in range(PASSES1):
-                first_product(i, a)
+        def after(name, shape, dtype, tag=None):
+            if tag in left_by:
+                return at(name, shape, dtype, left_by[tag])
+            return sb(name, shape, dtype, tag=tag)
 
         z_round = [sb("z_round%d" % c, [P, CHUNK, PACK], BF16) for c in range(CHUNKS)]
         z_codes = [sb("z_codes%d" % c, [P, CHUNK], U32) for c in range(CHUNKS)]
@@ -157,7 +178,7 @@ def tile_list_heating_loop_balance_kernel(
         pages, z, act, weighted = {}, {}, {}, {}
 
         def clear(i, tag=None):
-            pages[i] = sb("page%d" % i, [P, T2], F32, tag=tag)
+            pages[i] = after("page%d" % i, [P, T2], F32, tag=tag)
             nc.gpsimd.memset(pages[i][:], 0.0)
 
         def scatter(i):
@@ -168,7 +189,7 @@ def tile_list_heating_loop_balance_kernel(
             nc.scalar.activation(act[i][:], d[i][:], GELU, bias=bias[:, i : i + 1])
 
         def weigh_on_vector(i, tag=None):
-            weighted[i] = sb("weighted%d" % i, [P, S], F32, tag=tag)
+            weighted[i] = after("weighted%d" % i, [P, S], F32, tag=tag)
             nc.vector.scalar_tensor_tensor(weighted[i][:], act[i][:], gain_sb[:, i : i + 1], wgs_sb[:], MULT, MULT)
 
         def weigh_on_gpsimd(i):
@@ -194,7 +215,7 @@ def tile_list_heating_loop_balance_kernel(
             )
 
         def quantize_zc(i, tag=None):
-            zc_plane[i] = sb("zc_plane%d" % i, [P, PASSES2 * P], U8, tag=tag)
+            zc_plane[i] = after("zc_plane%d" % i, [P, PASSES2 * P], U8, tag=tag)
             nc.vector.quantize_mx(out=zc_codes[i][:].bitcast(FP8X4), scales=zc_plane[i][:], in_=zct[i][:])
 
         def round_z(copy, c, slots, rows):
@@ -236,7 +257,7 @@ def tile_list_heating_loop_balance_kernel(
         whole = slice(0, T2)
         clear(0)
         clear(1)
-        clear(3, tag="tab_plane")
+        clear(3, tag="tab_rows")
         gelu(0)
         weigh_on_vector(0)
         for i in (1, 2):
@@ -252,7 +273,7 @@ def tile_list_heating_loop_balance_kernel(
         for c in range(CHUNKS):
             round_z(nc.scalar.copy, c, slice(0, 1), z[0].unsqueeze(1))
         scatter(2)
-        z[1] = sb("z1", [P, T2], F32, tag="cond0")[:]
+        z[1] = after("z1", [P, T2], F32, tag="cond0")[:]
         remainder(nc.gpsimd, 1, whole)
         wv_round = sb("wv_round", [P, N * PACK], BF16)
         nc.scalar.copy(

@@ -29,7 +29,8 @@ ROW0 = P - 16 * PASSES1
 TAB_AT = [0, 12 * KIB, 30 * KIB]
 W1_AT = 8 * KIB
 ROWS_AT = 11 * KIB
-V_AT = [44 * KIB, 52 * KIB, 60 * KIB]
+V_AT = [48 * KIB, 56 * KIB, 64 * KIB]
+WEIGHTED_AT = 70 * KIB
 CHUNK = 256
 CHUNKS = T2 // CHUNK
 
@@ -136,7 +137,8 @@ def tile_list_heating_loop_balance_kernel(
         heat_at = [TAB_AT[1] + 3 * KIB, TAB_AT[2] + 3 * KIB, V_AT[1] - 3 * KIB, V_AT[1] + KIB]
         cond_at = [TAB_AT[1] + 7 * KIB, TAB_AT[2] + 7 * KIB, V_AT[2] + KIB, V_AT[2] - 3 * KIB]
         heat_sb = [at("heat%d" % i, [P, T2], F32, heat_at[i]) for i in range(PACK)]
-        cond_sb = [at("cond%d" % i, [P, T2], F32, cond_at[i]) for i in range(PACK)]
+        z_last = at("z_last", [P, 2, T2], F32, cond_at[1])
+        cond_sb = [z_last[:, 0, :] if i == 1 else at("cond%d" % i, [P, T2], F32, cond_at[i])[:] for i in range(PACK)]
         wc_codes = [at("wc_codes%d" % a, [P, T2], U32, V_AT[0] - 3 * KIB + 4 * KIB * a) for a in range(PASSES2)]
         wv_raw = at("wv_raw", [P, PACK, N], F32, TAB_AT[2] - 7 * KIB)
         wc_plane = at("wc_plane", [P, T2], U8, ROWS_AT)
@@ -144,10 +146,10 @@ def tile_list_heating_loop_balance_kernel(
         heat_rows = heat.rearrange("(p i) m -> p i m", i=PACK)
         cond_rows = cond.rearrange("(p i) m -> p i m", i=PACK)
         nc.sync.dma_start(heat_sb[0][:], heat_rows[:, 0, :])
-        nc.sync.dma_start(cond_sb[0][:], cond_rows[:, 0, :])
+        nc.sync.dma_start(cond_sb[0], cond_rows[:, 0, :])
         nc.sync.dma_start(wv_raw[:], wv.rearrange("(p j) c -> p j c", j=PACK))
         nc.sync.dma_start(heat_sb[1][:], heat_rows[:, 1, :])
-        nc.sync.dma_start(cond_sb[1][:], cond_rows[:, 1, :])
+        nc.sync.dma_start(cond_sb[1], cond_rows[:, 1, :])
         for q in range(QUADS):
             nc.sync.dma_start(
                 wc_plane[32 * q : 32 * q + 4 * PASSES2, :].bitcast(I32),
@@ -158,9 +160,15 @@ def tile_list_heating_loop_balance_kernel(
         for i in range(2, PACK):
             nc.sync.dma_start(heat_sb[i][:], heat_rows[:, i, :])
         for i in (3, 2):
-            nc.sync.dma_start(cond_sb[i][:], cond_rows[:, i, :])
+            nc.sync.dma_start(cond_sb[i], cond_rows[:, i, :])
 
-        left_by = {"heat0": heat_at[0], "cond0": cond_at[0], "cond1": cond_at[1]}
+        left_by = {
+            "heat0": heat_at[0],
+            "cond0": cond_at[0],
+            "weighted2": WEIGHTED_AT,
+            "weighted2 low": WEIGHTED_AT - KIB,
+            "weighted2 high": WEIGHTED_AT + KIB,
+        }
 
         def after(name, shape, dtype, tag=None):
             if tag in left_by:
@@ -194,7 +202,7 @@ def tile_list_heating_loop_balance_kernel(
 
         def weigh_on_gpsimd(i):
             h = sb("h%d" % i, [P, S], F32)
-            weighted[i] = sb("weighted%d" % i, [P, S], F32)
+            weighted[i] = after("weighted%d" % i, [P, S], F32, tag="weighted%d" % i)
             nc.scalar.activation(h[:], act[i][:], COPY, scale=gain_sb[:, i : i + 1])
             nc.gpsimd.tensor_tensor(weighted[i][:], h[:], wgs_sb[:], MULT)
 
@@ -203,7 +211,7 @@ def tile_list_heating_loop_balance_kernel(
 
         def couple(i, b=7):
             zc = sb("zc%d" % i, [P, T2], BF16)
-            nc.vector.tensor_tensor(zc[:], z[i], cond_sb[i][:], MULT)
+            nc.vector.tensor_tensor(zc[:], z[i], cond_sb[i], MULT)
             turned = bank(b, "turned%d" % i, [P, 2 * PASSES2, P])
             words = zc[:].bitcast(F32)
             for a in range(PASSES2):
@@ -280,7 +288,8 @@ def tile_list_heating_loop_balance_kernel(
             wv_round[:].rearrange("p (t m j) -> p m t j", t=PACK, j=PACK),
             wv_raw[:].rearrange("p j (m t) -> p m t j", t=PACK),
         )
-        wv_codes = sb("wv_codes", [P, N], U32, tag="weighted2")
+        weigh_on_vector(3, tag="weighted2 low")
+        wv_codes = after("wv_codes", [P, N], U32, tag="weighted2 high")
         nc.vector.quantize_mx(out=wv_codes[:].bitcast(FP8X4), scales=wv_plane[:], in_=wv_round[:])
         quantize_zc(0, tag="wv_round")
         for c in range(CHUNKS):
@@ -288,14 +297,12 @@ def tile_list_heating_loop_balance_kernel(
         couple(1)
         for c in range(CHUNKS):
             round_z(nc.scalar.copy, c, slice(1, 2), z[1].unsqueeze(1))
-        weigh_on_vector(3, tag="cond1")
         scatter(3)
-        z_last = sb("z_last", [P, 2, T2], F32, tag="act3")
         z[2], z[3] = z_last[:, 0, :], z_last[:, 1, :]
         remainder(nc.gpsimd, 2, whole)
         for cols in halves:
             remainder(nc.vector, 3, cols)
-        quantize_zc(1, tag="cond1")
+        quantize_zc(1, tag="weighted2 low")
         for c in range(CHUNKS):
             right(1, c, False, False)
         round_z(nc.scalar.copy, 0, slice(2, 4), z_last[:])

@@ -111,35 +111,45 @@ def tile_list_heating_loop_balance_kernel(
             )
             w1_codes.extend([pair[:, : PASSES1 * 2 * P], pair[:, PASSES1 * 2 * P :]])
 
-        for a in range(PASSES1):
+        entries = [slice(0, S // 2), slice(S // 2, S)]
+        for a in range(PASSES1 - 1):
             nc.vector.tensor_copy(v_codes[a][:], tab_codes[a][:].indirect(picks[:]))
             if a == 0:
                 deal_words(0, sb("w1_pair0", [P, PASSES1 * 4 * P], U8))
+        for e in entries:
+            nc.vector.tensor_copy(v_codes[-1][:, e], tab_codes[-1][:].indirect(picks[:, e.start // 16 : e.stop // 16]))
         deal_words(1, at("w1_pair1", [P, PASSES1 * 4 * P], U8, TAB_AT[2] + KIB))
-        d = [bank(4 + (i + 3) % PACK, "d%d" % i, [P, S]) for i in range(PACK)]
+        d = {i: bank(3 + i, "d%d" % i, [P, S]) for i in range(1, PACK)}
+        d_first = [bank(e, "d0_%d" % e, [P, S // 2]) for e in range(2)]
 
-        def first_product(i, a):
+        def first_product(out, i, a, cols, start, stop):
             plane = planes[:, a * (S + H) : (a + 1) * (S + H)]
             nc.tensor.matmul_mx(
-                out=d[i][:],
+                out=out,
                 lhsT=w1_codes[i][:, 2 * a * P : 2 * (a + 1) * P].bitcast(FP4X4),
                 lhsT_scale=plane[:, S + i * P : S + (i + 1) * P],
-                rhs=v_codes[a][:].bitcast(FP8X4),
-                rhs_scale=plane[:, :S],
-                start=(a == 0),
-                stop=(a == PASSES1 - 1),
+                rhs=v_codes[a][:, cols].bitcast(FP8X4),
+                rhs_scale=plane[:, cols],
+                start=start,
+                stop=stop,
             )
 
-        for i in range(PACK):
+        for e in range(2):
             for a in range(PASSES1):
-                first_product(i, a)
+                for n in range(2):
+                    cols = slice(entries[e].start + n * P, entries[e].start + (n + 1) * P)
+                    out = d_first[e][:, n * P : (n + 1) * P]
+                    first_product(out, 0, a, cols, (a, n) == (0, 0), (a, n) == (PASSES1 - 1, 1))
+        for i in range(1, PACK):
+            for a in range(PASSES1):
+                first_product(d[i][:], i, a, slice(0, S), a == 0, a == PASSES1 - 1)
 
-        heat_at = [TAB_AT[1] + 3 * KIB, TAB_AT[2] + 3 * KIB, V_AT[1] - 3 * KIB, V_AT[1] + KIB]
+        heat_at = [TAB_AT[1] + 3 * KIB, TAB_AT[2] + 3 * KIB, V_AT[0] - 3 * KIB, V_AT[1] + KIB]
         cond_at = [TAB_AT[1] + 7 * KIB, TAB_AT[2] + 7 * KIB, V_AT[2] + KIB, V_AT[2] - 3 * KIB]
         heat_sb = [at("heat%d" % i, [P, T2], F32, heat_at[i]) for i in range(PACK)]
         z_last = at("z_last", [P, 2, T2], F32, cond_at[1])
         cond_sb = [z_last[:, 0, :] if i == 1 else at("cond%d" % i, [P, T2], F32, cond_at[i])[:] for i in range(PACK)]
-        wc_codes = [at("wc_codes%d" % a, [P, T2], U32, V_AT[0] - 3 * KIB + 4 * KIB * a) for a in range(PASSES2)]
+        wc_codes = [at("wc_codes%d" % a, [P, T2], U32, V_AT[0] + KIB + 4 * KIB * a) for a in range(PASSES2)]
         wv_raw = at("wv_raw", [P, PACK, N], F32, TAB_AT[2] - 7 * KIB)
         wc_plane = at("wc_plane", [P, T2], U8, ROWS_AT)
         nc.gpsimd.memset(wc_plane[:].bitcast(I32), 0)
@@ -150,6 +160,7 @@ def tile_list_heating_loop_balance_kernel(
         nc.sync.dma_start(wv_raw[:], wv.rearrange("(p j) c -> p j c", j=PACK))
         nc.sync.dma_start(heat_sb[1][:], heat_rows[:, 1, :])
         nc.sync.dma_start(cond_sb[1], cond_rows[:, 1, :])
+        nc.sync.dma_start(heat_sb[2][:], heat_rows[:, 2, :])
         for q in range(QUADS):
             nc.sync.dma_start(
                 wc_plane[32 * q : 32 * q + 4 * PASSES2, :].bitcast(I32),
@@ -157,13 +168,11 @@ def tile_list_heating_loop_balance_kernel(
             )
         for a in range(PASSES2):
             nc.sync.dma_start(wc_codes[a][:].bitcast(I32), wc_words[a].rearrange("p c i -> p (c i)").bitcast(I32))
-        for i in range(2, PACK):
-            nc.sync.dma_start(heat_sb[i][:], heat_rows[:, i, :])
+        nc.sync.dma_start(heat_sb[3][:], heat_rows[:, 3, :])
         for i in (3, 2):
             nc.sync.dma_start(cond_sb[i], cond_rows[:, i, :])
 
         left_by = {
-            "heat0": heat_at[0],
             "cond0": cond_at[0],
             "weighted2": WEIGHTED_AT,
             "weighted2 low": WEIGHTED_AT - KIB,
@@ -183,14 +192,14 @@ def tile_list_heating_loop_balance_kernel(
         zc_plane = {}
         wv_plane = sb("wv_plane", [P, N], U8)
         acc = {}
-        pages, z, act, weighted = {}, {}, {}, {}
+        pages, z, act, weighted, zc_rows = {}, {}, {}, {}, {}
 
         def clear(i, tag=None):
             pages[i] = after("page%d" % i, [P, T2], F32, tag=tag)
             nc.gpsimd.memset(pages[i][:], 0.0)
 
         def scatter(i):
-            nc.vector.tensor_copy(pages[i][:].indirect(places[:]), weighted[i][:])
+            nc.vector.tensor_copy(pages[i % 2][:].indirect(places[:]), weighted[i][:])
 
         def gelu(i):
             act[i] = sb("act%d" % i, [P, S], F32)
@@ -207,11 +216,15 @@ def tile_list_heating_loop_balance_kernel(
             nc.gpsimd.tensor_tensor(weighted[i][:], h[:], wgs_sb[:], MULT)
 
         def remainder(engine, i, cols):
-            engine.tensor_tensor(z[i][:, cols], heat_sb[i][:, cols], pages[i][:, cols], SUBTRACT)
+            engine.tensor_tensor(z[i][:, cols], heat_sb[i][:, cols], pages[i % 2][:, cols], SUBTRACT)
 
-        def couple(i, b=7):
-            zc = sb("zc%d" % i, [P, T2], BF16)
-            nc.vector.tensor_tensor(zc[:], z[i], cond_sb[i], MULT)
+        def couple(i, cols):
+            if i not in zc_rows:
+                zc_rows[i] = sb("zc%d" % i, [P, T2], BF16)
+            nc.vector.tensor_tensor(zc_rows[i][:, cols], z[i][:, cols], cond_sb[i][:, cols], MULT)
+
+        def turn(i, b=7):
+            zc = zc_rows[i]
             turned = bank(b, "turned%d" % i, [P, 2 * PASSES2, P])
             words = zc[:].bitcast(F32)
             for a in range(PASSES2):
@@ -250,14 +263,16 @@ def tile_list_heating_loop_balance_kernel(
                     stop=(last and a == PASSES2 - 1),
                 )
 
-        def left(i, c, last):
+        def left(i, c, first, last):
+            if first:
+                acc[i // 2, c] = bank(4 * (i // 2) + c, "acc%d_%d" % (i // 2, c), [P, 2, CHUNK])
             nc.tensor.matmul_mx(
                 out=acc[i // 2, c][:, i % 2, :],
                 lhsT=wv_codes[:, i * P : (i + 1) * P].bitcast(FP8X4),
                 lhsT_scale=wv_plane[:, i * P : (i + 1) * P],
                 rhs=z_codes[c][:].bitcast(FP8X4),
                 rhs_scale=z_plane[c][:],
-                start=False,
+                start=first,
                 stop=last,
             )
 
@@ -265,19 +280,24 @@ def tile_list_heating_loop_balance_kernel(
         whole = slice(0, T2)
         clear(0)
         clear(1)
-        clear(3, tag="tab_rows")
-        gelu(0)
-        weigh_on_vector(0)
+        act[0] = sb("act0", [P, S], F32)
+        weighted[0] = sb("weighted0", [P, S], F32)
+        for e, cols in enumerate(entries):
+            nc.scalar.activation(act[0][:, cols], d_first[e][:], GELU, bias=bias[:, 0:1])
+            nc.vector.scalar_tensor_tensor(
+                weighted[0][:, cols], act[0][:, cols], gain_sb[:, 0:1], wgs_sb[:, cols], MULT, MULT
+            )
         for i in (1, 2):
             gelu(i)
             weigh_on_gpsimd(i)
         gelu(3)
-        scatter(0)
+        for cols in entries:
+            nc.vector.tensor_copy(pages[0][:].indirect(places[:, cols.start // 16 : cols.stop // 16]), weighted[0][:, cols])
         scatter(1)
         z[0] = sb("z0", [P, T2], F32, tag="h2")[:]
         remainder(nc.gpsimd, 0, whole)
-        clear(2, tag="heat0")
-        couple(0)
+        couple(0, whole)
+        turn(0)
         for c in range(CHUNKS):
             round_z(nc.scalar.copy, c, slice(0, 1), z[0].unsqueeze(1))
         scatter(2)
@@ -294,44 +314,16 @@ def tile_list_heating_loop_balance_kernel(
         quantize_zc(0, tag="wv_round")
         for c in range(CHUNKS):
             right(0, c, True, False)
-        couple(1)
+        couple(1, whole)
+        turn(1)
         for c in range(CHUNKS):
             round_z(nc.scalar.copy, c, slice(1, 2), z[1].unsqueeze(1))
         scatter(3)
         z[2], z[3] = z_last[:, 0, :], z_last[:, 1, :]
         remainder(nc.gpsimd, 2, whole)
-        for cols in halves:
-            remainder(nc.vector, 3, cols)
         quantize_zc(1, tag="weighted2 low")
         for c in range(CHUNKS):
             right(1, c, False, False)
-        round_z(nc.scalar.copy, 0, slice(2, 4), z_last[:])
-        round_z(nc.scalar.copy, 1, slice(2, 4), z_last[:])
-        round_z(nc.scalar.copy, 2, slice(2, 4), z_last[:])
-        couple(3, b=6)
-        couple(2)
-        quantize_z(0)
-        quantize_z(1)
-        quantize_zc(3)
-        round_z(nc.vector.tensor_copy, 3, slice(2, 4), z_last[:])
-        quantize_zc(2)
-        quantize_z(2)
-        quantize_z(3)
-        for c in range(CHUNKS - 1):
-            right(3, c, True, False)
-        for c in range(CHUNKS):
-            left(0, c, False)
-            left(1, c, True)
-            if c == CHUNKS - 1:
-                right(3, c, True, False)
-            if c < 2:
-                left(2, c, False)
-                left(3, c, False)
-                right(2, c, False, True)
-            else:
-                right(2, c, False, False)
-                left(2, c, False)
-                left(3, c, True)
 
         y = [sb("y%d" % c, [P, PACK, CHUNK], F32) for c in range(CHUNKS)]
         y_round = [sb("y_round%d" % c, [P, CHUNK * PACK], BF16) for c in range(CHUNKS)]
@@ -356,8 +348,34 @@ def tile_list_heating_loop_balance_kernel(
             nc.vector.quantize_mx(out=y_codes[:, cols].bitcast(FP8X4), scales=y_plane[:, cols], in_=y_round[c][:])
             nc.sync.dma_start(out_words[:, cols], y_codes[:, cols].bitcast(I32))
 
-        for c in range(CHUNKS):
+        def close_low(c):
+            left(0, c, False, False)
+            left(1, c, False, True)
             empty(0, c)
+
+        for cols in halves:
+            remainder(nc.vector, 3, cols)
+        for c in range(2):
+            round_z(nc.scalar.copy, c, slice(2, 4), z_last[:])
+        for c in range(2):
+            couple(3, halves[c])
+            quantize_z(c)
+            close_low(c)
+        round_z(nc.scalar.copy, 2, slice(2, 4), z_last[:])
+        turn(3, b=6)
+        round_z(nc.vector.tensor_copy, 3, slice(2, 4), z_last[:])
+        for c in range(2, CHUNKS):
+            quantize_z(c)
+            close_low(c)
+        couple(2, whole)
+        turn(2)
+        quantize_zc(3)
+        quantize_zc(2)
+        for c in range(CHUNKS):
+            left(2, c, True, False)
+            left(3, c, False, False)
+            right(3, c, False, False)
+            right(2, c, False, True)
             empty(1, c)
         weave(0, nc.vector.tensor_copy)
         weave(1, nc.vector.tensor_copy)

@@ -235,6 +235,15 @@ def tile_list_heating_loop_balance_kernel(
                 turned[:].rearrange("q (a u) n -> q a n u", u=2),
             )
 
+        def turn_in_lower_banks(i):
+            words = zc_rows[i][:].bitcast(F32)
+            target = zct[i][:].bitcast(F32).rearrange("q (a n u) -> q a n u", a=PASSES2, u=2)
+            for a in range(PASSES2):
+                turned = [bank(2 * a + u, "turned%d_%d_%d" % (i, a, u), [P, P]) for u in range(2)]
+                for u in range(2):
+                    nc.tensor.transpose(turned[u][:], words[:, 2 * P * a + u : 2 * P * (a + 1) : 2], ident[:])
+                    nc.scalar.copy(target[:, a, :, u], turned[u][:])
+
         def quantize_zc(i, tag=None):
             zc_plane[i] = after("zc_plane%d" % i, [P, PASSES2 * P], U8, tag=tag)
             nc.vector.quantize_mx(out=zc_codes[i][:].bitcast(FP8X4), scales=zc_plane[i][:], in_=zct[i][:])
@@ -312,10 +321,10 @@ def tile_list_heating_loop_balance_kernel(
         wv_codes = after("wv_codes", [P, N], U32, tag="weighted2 high")
         nc.vector.quantize_mx(out=wv_codes[:].bitcast(FP8X4), scales=wv_plane[:], in_=wv_round[:])
         quantize_zc(0, tag="wv_round")
+        couple(1, whole)
+        turn_in_lower_banks(1)
         for c in range(CHUNKS):
             right(0, c, True, False)
-        couple(1, whole)
-        turn(1)
         for c in range(CHUNKS):
             round_z(nc.scalar.copy, c, slice(1, 2), z[1].unsqueeze(1))
         scatter(3)
@@ -357,34 +366,36 @@ def tile_list_heating_loop_balance_kernel(
             remainder(nc.vector, 3, cols)
         for c in range(2):
             round_z(nc.scalar.copy, c, slice(2, 4), z_last[:])
-        for c in range(2):
-            couple(3, halves[c])
-            quantize_z(c)
-            close_low(c)
-        round_z(nc.scalar.copy, 2, slice(2, 4), z_last[:])
+        couple(3, halves[0])
+        quantize_z(0)
+        close_low(0)
+        couple(3, halves[1])
         turn(3, b=6)
-        round_z(nc.vector.tensor_copy, 3, slice(2, 4), z_last[:])
-        for c in range(2, CHUNKS):
-            quantize_z(c)
-            close_low(c)
         couple(2, whole)
         turn(2)
+        round_z(nc.scalar.copy, 2, slice(2, 4), z_last[:])
+        quantize_z(1)
         quantize_zc(3)
+        round_z(nc.vector.tensor_copy, 3, slice(2, 4), z_last[:])
         quantize_zc(2)
+        close_low(1)
+        for c in range(2, CHUNKS):
+            quantize_z(c)
         for c in range(CHUNKS):
             left(2, c, True, False)
             left(3, c, False, False)
             right(3, c, False, False)
             right(2, c, False, True)
             empty(1, c)
+            if c < 2:
+                close_low(c + 2)
         weave(0, nc.vector.tensor_copy)
         weave(1, nc.vector.tensor_copy)
         quantize_y(0)
         weave(2, nc.vector.tensor_copy)
-        weave(3, nc.scalar.copy)
+        weave(3, nc.vector.tensor_copy)
         for c in range(1, CHUNKS):
             quantize_y(c)
         for q in range(QUADS):
-            nc.sync.dma_start(
-                out_2[0, 4 * q : 4 * q + 4, :].bitcast(I32), y_plane[32 * q : 32 * q + 4, :].bitcast(I32)
-            )
+            queue = nc.scalar if q < 2 else nc.sync
+            queue.dma_start(out_2[0, 4 * q : 4 * q + 4, :].bitcast(I32), y_plane[32 * q : 32 * q + 4, :].bitcast(I32))

@@ -29,8 +29,9 @@ ROW0 = P - 16 * PASSES1
 TAB_AT = [0, 12 * KIB, 30 * KIB]
 W1_AT = 8 * KIB
 ROWS_AT = 11 * KIB
-V_AT = [48 * KIB, 56 * KIB, 64 * KIB]
-WEIGHTED_AT = 70 * KIB
+V_AT = [49 * KIB, 57 * KIB, 65 * KIB]
+WEIGHTED_AT = 71 * KIB
+SHARE = 192
 CHUNK = 256
 CHUNKS = T2 // CHUNK
 
@@ -144,9 +145,12 @@ def tile_list_heating_loop_balance_kernel(
             for a in range(PASSES1):
                 first_product(d[i][:], i, a, slice(0, S), a == 0, a == PASSES1 - 1)
 
-        heat_at = [TAB_AT[1] + 3 * KIB, TAB_AT[2] + 3 * KIB, V_AT[0] - 3 * KIB, V_AT[1] + KIB]
-        cond_at = [TAB_AT[1] + 7 * KIB, TAB_AT[2] + 7 * KIB, V_AT[2] + KIB, V_AT[2] - 3 * KIB]
-        heat_sb = [at("heat%d" % i, [P, T2], F32, heat_at[i]) for i in range(PACK)]
+        heat_at = [TAB_AT[1] + 3 * KIB, TAB_AT[2] + 3 * KIB + KIB // 2, V_AT[0] - 3 * KIB, V_AT[1] + KIB]
+        cond_at = [TAB_AT[1] + 7 * KIB, TAB_AT[2] + 7 * KIB + KIB // 2, V_AT[2] + KIB, V_AT[2] - 3 * KIB]
+        heat1_and_more = at("heat1_and_more", [P, S // 2 + T2], F32, heat_at[1] - KIB)
+        heat_sb = [
+            heat1_and_more[:, S // 2 :] if i == 1 else at("heat%d" % i, [P, T2], F32, heat_at[i])[:] for i in range(PACK)
+        ]
         z_last = at("z_last", [P, 2, T2], F32, cond_at[1])
         cond_sb = [z_last[:, 0, :] if i == 1 else at("cond%d" % i, [P, T2], F32, cond_at[i])[:] for i in range(PACK)]
         wc_codes = [at("wc_codes%d" % a, [P, T2], U32, V_AT[0] + KIB + 4 * KIB * a) for a in range(PASSES2)]
@@ -155,12 +159,12 @@ def tile_list_heating_loop_balance_kernel(
         nc.gpsimd.memset(wc_plane[:].bitcast(I32), 0)
         heat_rows = heat.rearrange("(p i) m -> p i m", i=PACK)
         cond_rows = cond.rearrange("(p i) m -> p i m", i=PACK)
-        nc.sync.dma_start(heat_sb[0][:], heat_rows[:, 0, :])
+        nc.sync.dma_start(heat_sb[0], heat_rows[:, 0, :])
         nc.sync.dma_start(cond_sb[0], cond_rows[:, 0, :])
         nc.sync.dma_start(wv_raw[:], wv.rearrange("(p j) c -> p j c", j=PACK))
-        nc.sync.dma_start(heat_sb[1][:], heat_rows[:, 1, :])
+        nc.sync.dma_start(heat_sb[1], heat_rows[:, 1, :])
         nc.sync.dma_start(cond_sb[1], cond_rows[:, 1, :])
-        nc.sync.dma_start(heat_sb[2][:], heat_rows[:, 2, :])
+        nc.sync.dma_start(heat_sb[2], heat_rows[:, 2, :])
         for q in range(QUADS):
             nc.sync.dma_start(
                 wc_plane[32 * q : 32 * q + 4 * PASSES2, :].bitcast(I32),
@@ -168,14 +172,14 @@ def tile_list_heating_loop_balance_kernel(
             )
         for a in range(PASSES2):
             nc.sync.dma_start(wc_codes[a][:].bitcast(I32), wc_words[a].rearrange("p c i -> p (c i)").bitcast(I32))
-        nc.sync.dma_start(heat_sb[3][:], heat_rows[:, 3, :])
+        nc.sync.dma_start(heat_sb[3], heat_rows[:, 3, :])
         for i in (3, 2):
             nc.sync.dma_start(cond_sb[i], cond_rows[:, i, :])
 
         left_by = {
             "cond0": cond_at[0],
             "weighted2": WEIGHTED_AT,
-            "weighted2 low": WEIGHTED_AT - KIB,
+            "weighted2 low": WEIGHTED_AT,
             "weighted2 high": WEIGHTED_AT + KIB,
         }
 
@@ -199,7 +203,7 @@ def tile_list_heating_loop_balance_kernel(
             nc.gpsimd.memset(pages[i][:], 0.0)
 
         def scatter(i):
-            nc.vector.tensor_copy(pages[i % 2][:].indirect(places[:]), weighted[i][:])
+            nc.vector.tensor_copy(pages[i % 2][:].indirect(places[:]), weighted[i][:, :])
 
         def gelu(i):
             act[i] = sb("act%d" % i, [P, S], F32)
@@ -300,6 +304,10 @@ def tile_list_heating_loop_balance_kernel(
             gelu(i)
             weigh_on_gpsimd(i)
         gelu(3)
+        h_last = sb("h3", [P, S], F32)
+        nc.scalar.activation(h_last[:], act[3][:], COPY, scale=gain_sb[:, 3:4])
+        weighted[3] = heat1_and_more[:, :S]
+        nc.gpsimd.tensor_tensor(weighted[3][:, entries[0]], h_last[:, entries[0]], wgs_sb[:, entries[0]], MULT)
         for cols in entries:
             nc.vector.tensor_copy(pages[0][:].indirect(places[:, cols.start // 16 : cols.stop // 16]), weighted[0][:, cols])
         scatter(1)
@@ -312,15 +320,15 @@ def tile_list_heating_loop_balance_kernel(
         scatter(2)
         z[1] = after("z1", [P, T2], F32, tag="cond0")[:]
         remainder(nc.gpsimd, 1, whole)
+        nc.gpsimd.tensor_tensor(weighted[3][:, entries[1]], h_last[:, entries[1]], wgs_sb[:, entries[1]], MULT)
         wv_round = sb("wv_round", [P, N * PACK], BF16)
         nc.scalar.copy(
             wv_round[:].rearrange("p (t m j) -> p m t j", t=PACK, j=PACK),
             wv_raw[:].rearrange("p j (m t) -> p m t j", t=PACK),
         )
-        weigh_on_vector(3, tag="weighted2 low")
         wv_codes = after("wv_codes", [P, N], U32, tag="weighted2 high")
         nc.vector.quantize_mx(out=wv_codes[:].bitcast(FP8X4), scales=wv_plane[:], in_=wv_round[:])
-        quantize_zc(0, tag="wv_round")
+        quantize_zc(0, tag="weighted2 low")
         couple(1, whole)
         turn_in_lower_banks(1)
         for c in range(CHUNKS):
@@ -330,7 +338,7 @@ def tile_list_heating_loop_balance_kernel(
         scatter(3)
         z[2], z[3] = z_last[:, 0, :], z_last[:, 1, :]
         remainder(nc.gpsimd, 2, whole)
-        quantize_zc(1, tag="weighted2 low")
+        quantize_zc(1, tag="page0")
         for c in range(CHUNKS):
             right(1, c, False, False)
 

@@ -151,8 +151,7 @@ def tile_list_heating_loop_balance_kernel(
         heat_sb = [
             heat1_and_more[:, S // 2 :] if i == 1 else at("heat%d" % i, [P, T2], F32, heat_at[i])[:] for i in range(PACK)
         ]
-        z_last = at("z_last", [P, 2, T2], F32, cond_at[1])
-        cond_sb = [z_last[:, 0, :] if i == 1 else at("cond%d" % i, [P, T2], F32, cond_at[i])[:] for i in range(PACK)]
+        cond_sb = [at("cond%d" % i, [P, T2], F32, cond_at[i])[:] for i in range(PACK)]
         wc_codes = [at("wc_codes%d" % a, [P, T2], U32, V_AT[0] + KIB + 4 * KIB * a) for a in range(PASSES2)]
         wv_raw = at("wv_raw", [P, PACK, N], F32, TAB_AT[2] - 7 * KIB)
         wc_plane = at("wc_plane", [P, T2], U8, ROWS_AT)
@@ -178,9 +177,9 @@ def tile_list_heating_loop_balance_kernel(
 
         left_by = {
             "cond0": cond_at[0],
-            "weighted2": WEIGHTED_AT,
-            "weighted2 low": WEIGHTED_AT,
-            "weighted2 high": WEIGHTED_AT + KIB,
+            "h3": WEIGHTED_AT,
+            "h3 low": WEIGHTED_AT,
+            "h3 high": WEIGHTED_AT + KIB,
         }
 
         def after(name, shape, dtype, tag=None):
@@ -227,13 +226,27 @@ def tile_list_heating_loop_balance_kernel(
                 zc_rows[i] = sb("zc%d" % i, [P, T2], BF16)
             nc.vector.tensor_tensor(zc_rows[i][:, cols], z[i][:, cols], cond_sb[i][:, cols], MULT)
 
+        def couple_sorted(i, a):
+            if i not in zc_rows:
+                zc_rows[i] = sb("zc%d" % i, [P, T2], BF16)
+            nc.vector.tensor_tensor(
+                zc_rows[i][:, halves[a]].rearrange("p (u q e) -> p u q e", u=2, e=2),
+                z[i][:, halves[a]].rearrange("p (q u e) -> p u q e", u=2, e=2),
+                cond_sb[i][:, halves[a]].rearrange("p (q u e) -> p u q e", u=2, e=2),
+                MULT,
+            )
+
         def turn(i, b=7):
             zc = zc_rows[i]
             turned = bank(b, "turned%d" % i, [P, 2 * PASSES2, P])
             words = zc[:].bitcast(F32)
             for a in range(PASSES2):
                 for u in range(2):
-                    nc.tensor.transpose(turned[:, 2 * a + u, :], words[:, 2 * P * a + u : 2 * P * (a + 1) : 2], ident[:])
+                    if i < 2:
+                        block = words[:, 2 * P * a + u : 2 * P * (a + 1) : 2]
+                    else:
+                        block = words[:, P * (2 * a + u) : P * (2 * a + u + 1)]
+                    nc.tensor.transpose(turned[:, 2 * a + u, :], block, ident[:])
             nc.scalar.copy(
                 zct[i][:].bitcast(F32).rearrange("q (a n u) -> q a n u", a=PASSES2, u=2),
                 turned[:].rearrange("q (a u) n -> q a n u", u=2),
@@ -304,7 +317,7 @@ def tile_list_heating_loop_balance_kernel(
             gelu(i)
             weigh_on_gpsimd(i)
         gelu(3)
-        h_last = sb("h3", [P, S], F32)
+        h_last = after("h3", [P, S], F32, tag="h3")
         nc.scalar.activation(h_last[:], act[3][:], COPY, scale=gain_sb[:, 3:4])
         weighted[3] = heat1_and_more[:, :S]
         nc.gpsimd.tensor_tensor(weighted[3][:, entries[0]], h_last[:, entries[0]], wgs_sb[:, entries[0]], MULT)
@@ -321,15 +334,16 @@ def tile_list_heating_loop_balance_kernel(
         z[1] = after("z1", [P, T2], F32, tag="cond0")[:]
         remainder(nc.gpsimd, 1, whole)
         nc.gpsimd.tensor_tensor(weighted[3][:, entries[1]], h_last[:, entries[1]], wgs_sb[:, entries[1]], MULT)
-        wv_round = sb("wv_round", [P, N * PACK], BF16)
+        z_last = sb("z_last", [P, 2, T2], F32)
+        wv_round = z_last[:, 0, :].bitcast(BF16)
         nc.scalar.copy(
-            wv_round[:].rearrange("p (t m j) -> p m t j", t=PACK, j=PACK),
+            wv_round.rearrange("p (t m j) -> p m t j", t=PACK, j=PACK),
             wv_raw[:].rearrange("p j (m t) -> p m t j", t=PACK),
         )
-        wv_codes = after("wv_codes", [P, N], U32, tag="weighted2 high")
-        nc.vector.quantize_mx(out=wv_codes[:].bitcast(FP8X4), scales=wv_plane[:], in_=wv_round[:])
-        quantize_zc(0, tag="weighted2 low")
         couple(1, whole)
+        quantize_zc(0, tag="h3 low")
+        wv_codes = after("wv_codes", [P, N], U32, tag="h3 high")
+        nc.vector.quantize_mx(out=wv_codes[:].bitcast(FP8X4), scales=wv_plane[:], in_=wv_round)
         turn_in_lower_banks(1)
         for c in range(CHUNKS):
             right(0, c, True, False)
@@ -349,37 +363,39 @@ def tile_list_heating_loop_balance_kernel(
         out_rows = out_0.rearrange("(p i) m -> p i m", i=PACK)
         out_words = out_1[0].rearrange("p m t -> p (m t)").bitcast(I32)
 
-        def empty(u, c):
+        def empty(u, c, copy=nc.scalar.copy):
             cols = slice(c * CHUNK, (c + 1) * CHUNK)
-            nc.scalar.copy(y[c][:, 2 * u : 2 * u + 2, :], acc[u, c][:])
+            copy(y[c][:, 2 * u : 2 * u + 2, :], acc[u, c][:])
             nc.sync.dma_start(out_rows[:, 2 * u : 2 * u + 2, cols], y[c][:, 2 * u : 2 * u + 2, :])
 
-        def weave(c, copy):
+        def weave(c, copy, first=0, count=CHUNK):
             copy(
-                y_round[c][:].rearrange("p (m j i) -> p m i j", j=4, i=PACK),
-                y[c][:].rearrange("p i (m j) -> p m i j", j=4),
+                y_round[c][:, PACK * first : PACK * (first + count)].rearrange("p (m j i) -> p m i j", j=4, i=PACK),
+                y[c][:, :, first : first + count].rearrange("p i (m j) -> p m i j", j=4),
             )
 
         def quantize_y(c):
             cols = slice(c * CHUNK, (c + 1) * CHUNK)
             nc.vector.quantize_mx(out=y_codes[:, cols].bitcast(FP8X4), scales=y_plane[:, cols], in_=y_round[c][:])
-            nc.sync.dma_start(out_words[:, cols], y_codes[:, cols].bitcast(I32))
+            if c % 2 == 1:
+                nc.sync.dma_start(out_words[:, halves[c // 2]], y_codes[:, halves[c // 2]].bitcast(I32))
 
         def close_low(c):
             left(0, c, False, False)
             left(1, c, False, True)
             empty(0, c)
 
-        for cols in halves:
+        for cols in (slice(0, CHUNK), slice(CHUNK, 2 * CHUNK), halves[1]):
             remainder(nc.vector, 3, cols)
         for c in range(2):
             round_z(nc.scalar.copy, c, slice(2, 4), z_last[:])
-        couple(3, halves[0])
+        couple_sorted(3, 0)
         quantize_z(0)
         close_low(0)
-        couple(3, halves[1])
+        couple_sorted(3, 1)
         turn(3, b=6)
-        couple(2, whole)
+        for a in range(PASSES2):
+            couple_sorted(2, a)
         turn(2)
         round_z(nc.scalar.copy, 2, slice(2, 4), z_last[:])
         quantize_z(1)
@@ -394,14 +410,15 @@ def tile_list_heating_loop_balance_kernel(
             left(3, c, False, False)
             right(3, c, False, False)
             right(2, c, False, True)
-            empty(1, c)
+            empty(1, c, nc.vector.tensor_copy if c == 0 else nc.scalar.copy)
             if c < 2:
                 close_low(c + 2)
         weave(0, nc.vector.tensor_copy)
         weave(1, nc.vector.tensor_copy)
         quantize_y(0)
         weave(2, nc.vector.tensor_copy)
-        weave(3, nc.vector.tensor_copy)
+        weave(3, nc.scalar.copy, 0, CHUNK // 4)
+        weave(3, nc.vector.tensor_copy, CHUNK // 4, CHUNK - CHUNK // 4)
         for c in range(1, CHUNKS):
             quantize_y(c)
         for q in range(QUADS):

@@ -28,7 +28,7 @@ KIB = 1024
 ROW0 = P - 16 * PASSES1
 TAB_AT = [0, 12 * KIB, 30 * KIB]
 W1_AT = 8 * KIB
-ROWS_AT = 11 * KIB
+ROWS_AT = 78 * KIB
 V_AT = [49 * KIB, 57 * KIB, 65 * KIB]
 WEIGHTED_AT = 71 * KIB
 SHARE = 192
@@ -73,8 +73,8 @@ def tile_list_heating_loop_balance_kernel(
         ident = sb("ident", [P, P], F32)
         make_identity(nc, ident[:])
 
-        bias = sb("bias", [P, PACK], F32)
-        gain_sb = sb("gain_sb", [P, PACK], F32)
+        vectors = sb("vectors", [P, H], F32)
+        nc.gpsimd.memset(vectors[: P - 2, :], 0.0)
         wgs_sb = sb("wgs_sb", [P, S], F32)
         nc.sync.dma_start(picks[:], offs)
         for a in range(PASSES1):
@@ -83,8 +83,8 @@ def tile_list_heating_loop_balance_kernel(
         for a in range(PASSES1):
             nc.sync.dma_start(tab_codes[a][:].bitcast(I32), tab_words[a].rearrange("p t i -> p (t i)").bitcast(I32))
             if a == 0:
-                nc.sync.dma_start(bias[:], b1.rearrange("(p i) -> p i", i=PACK))
-                nc.sync.dma_start(gain_sb[:], gain.rearrange("(p i) -> p i", i=PACK))
+                nc.sync.dma_start(vectors[P - 2 : P - 1, :], b1.unsqueeze(0))
+                nc.sync.dma_start(vectors[P - 1 : P, :], gain.unsqueeze(0))
                 nc.sync.dma_start(
                     w1_raw[:].bitcast(I32).rearrange("p (a w) -> p a w", a=PASSES1),
                     w1_words.bitcast(I32).rearrange("a p w -> p a w"),
@@ -103,6 +103,12 @@ def tile_list_heating_loop_balance_kernel(
             nc.scalar.dma_start(
                 planes[32 * q : 32 * q + 4, :].bitcast(I32), both_rows[first : first + 4 * PASSES1, :].bitcast(I32)
             )
+        turned_vectors = bank(2, "turned_vectors", [P, PACK, P])
+        for i in range(PACK):
+            nc.tensor.transpose(turned_vectors[:, i, :], vectors[:, i:H:PACK], ident[:])
+        per_row = sb("per_row", [P, 2, PACK], F32)
+        nc.vector.tensor_copy(per_row[:], turned_vectors[:, :, P - 2 :].rearrange("p i v -> p v i"))
+        bias, gain_sb = per_row[:, 0, :], per_row[:, 1, :]
         w1_codes = []
 
         def deal_words(u, pair):
@@ -154,7 +160,7 @@ def tile_list_heating_loop_balance_kernel(
         cond_sb = [at("cond%d" % i, [P, T2], F32, cond_at[i])[:] for i in range(PACK)]
         wc_codes = [at("wc_codes%d" % a, [P, T2], U32, V_AT[0] + KIB + 4 * KIB * a) for a in range(PASSES2)]
         wv_raw = at("wv_raw", [P, PACK, N], F32, TAB_AT[2] - 7 * KIB)
-        wc_plane = at("wc_plane", [P, T2], U8, ROWS_AT)
+        wc_plane = at("wc_plane", [P, T2], U8, ROWS_AT + KIB // 2)
         nc.gpsimd.memset(wc_plane[:].bitcast(I32), 0)
         heat_rows = heat.rearrange("(p i) m -> p i m", i=PACK)
         cond_rows = cond.rearrange("(p i) m -> p i m", i=PACK)
@@ -177,6 +183,7 @@ def tile_list_heating_loop_balance_kernel(
 
         left_by = {
             "cond0": cond_at[0],
+            "both_rows": ROWS_AT - 2 * KIB + KIB // 4,
             "h3": WEIGHTED_AT,
             "h3 low": WEIGHTED_AT,
             "h3 high": WEIGHTED_AT + KIB,
@@ -306,7 +313,7 @@ def tile_list_heating_loop_balance_kernel(
         whole = slice(0, T2)
         clear(0)
         clear(1)
-        act[0] = sb("act0", [P, S], F32)
+        act[0] = after("act0", [P, S], F32, tag="both_rows")
         weighted[0] = sb("weighted0", [P, S], F32)
         for e, cols in enumerate(entries):
             nc.scalar.activation(act[0][:, cols], d_first[e][:], GELU, bias=bias[:, 0:1])

@@ -401,15 +401,15 @@ def tile_list_heating_loop_balance_kernel(
         close_low(0)
         couple_sorted(3, 1)
         turn(3, b=6)
+        quantize_z(1)
+        round_z(nc.scalar.copy, 2, slice(2, 4), z_last[:])
         for a in range(PASSES2):
             couple_sorted(2, a)
         turn(2)
-        round_z(nc.scalar.copy, 2, slice(2, 4), z_last[:])
-        quantize_z(1)
+        close_low(1)
         quantize_zc(3)
         round_z(nc.vector.tensor_copy, 3, slice(2, 4), z_last[:])
         quantize_zc(2)
-        close_low(1)
         for c in range(2, CHUNKS):
             quantize_z(c)
         for c in range(CHUNKS):

@@ -59,7 +59,7 @@ def tile_list_heating_loop_balance_kernel(
         picks = keep.tile([P, S // 16], U16, name="picks")
         places = keep.tile([P, S // 16], U16, name="places")
         tab_rows = sb("tab_rows", [P, T], U8)
-        w1_rows = sb("w1_rows", [P, H], U8)
+        w1_rows = at("w1_rows", [P, H], U8, ROWS_AT - 2 * KIB)
         tab_codes = [at("tab_codes%d" % a, [P, T], U32, TAB_AT[a]) for a in range(PASSES1)]
         w1_raw = at("w1_raw", [P, PASSES1 * 2 * H], U8, W1_AT)
         both_rows = at("both_rows", [P, S + H], U8, ROWS_AT)
@@ -109,23 +109,29 @@ def tile_list_heating_loop_balance_kernel(
         per_row = sb("per_row", [P, 2, PACK], F32)
         nc.vector.tensor_copy(per_row[:], turned_vectors[:, :, P - 2 :].rearrange("p i v -> p v i"))
         bias, gain_sb = per_row[:, 0, :], per_row[:, 1, :]
-        w1_codes = []
+        w1_codes = {}
+        w1_dealt = w1_raw[:].bitcast(U16).rearrange("p (a c i) -> p i a c", a=PASSES1, i=PACK)
 
-        def deal_words(u, pair):
+        def deal_words(slices, passes, dealt):
+            count = passes.stop - passes.start
             nc.vector.tensor_copy(
-                pair[:].bitcast(U16).rearrange("p (i c) -> p i c", i=2),
-                w1_raw[:].bitcast(U16).rearrange("p (c i) -> p i c", i=PACK)[:, 2 * u : 2 * u + 2, :],
+                dealt[:].bitcast(U16).rearrange("p (i a c) -> p i a c", a=count, c=P), w1_dealt[:, slices, passes, :]
             )
-            w1_codes.extend([pair[:, : PASSES1 * 2 * P], pair[:, PASSES1 * 2 * P :]])
+            for i in range(slices.start, slices.stop):
+                for a in range(passes.start, passes.stop):
+                    first = 2 * P * ((i - slices.start) * count + a - passes.start)
+                    w1_codes[i, a] = dealt[:, first : first + 2 * P]
 
         entries = [slice(0, S // 2), slice(S // 2, S)]
         for a in range(PASSES1 - 1):
             nc.vector.tensor_copy(v_codes[a][:], tab_codes[a][:].indirect(picks[:]))
             if a == 0:
-                deal_words(0, sb("w1_pair0", [P, PASSES1 * 4 * P], U8))
+                deal_words(slice(0, 1), slice(0, PASSES1), sb("w1_first", [P, PASSES1 * 2 * P], U8))
+                deal_words(slice(1, 2), slice(0, 1), sb("w1_early", [P, 1 * 2 * P], U8))
         for e in entries:
             nc.vector.tensor_copy(v_codes[-1][:, e], tab_codes[-1][:].indirect(picks[:, e.start // 16 : e.stop // 16]))
-        deal_words(1, at("w1_pair1", [P, PASSES1 * 4 * P], U8, TAB_AT[2] + KIB))
+        deal_words(slice(1, 2), slice(1, PASSES1), at("w1_late", [P, (PASSES1 - 1) * 2 * P], U8, TAB_AT[2] + 7 * KIB))
+        deal_words(slice(2, PACK), slice(0, PASSES1), at("w1_pair", [P, PASSES1 * 4 * P], U8, TAB_AT[2] + KIB))
         d = {i: bank(3 + i, "d%d" % i, [P, S]) for i in range(1, PACK)}
         d_first = [bank(e, "d0_%d" % e, [P, S // 2]) for e in range(2)]
 
@@ -133,7 +139,7 @@ def tile_list_heating_loop_balance_kernel(
             plane = planes[:, a * (S + H) : (a + 1) * (S + H)]
             nc.tensor.matmul_mx(
                 out=out,
-                lhsT=w1_codes[i][:, 2 * a * P : 2 * (a + 1) * P].bitcast(FP4X4),
+                lhsT=w1_codes[i, a].bitcast(FP4X4),
                 lhsT_scale=plane[:, S + i * P : S + (i + 1) * P],
                 rhs=v_codes[a][:, cols].bitcast(FP8X4),
                 rhs_scale=plane[:, cols],
@@ -183,7 +189,7 @@ def tile_list_heating_loop_balance_kernel(
 
         left_by = {
             "cond0": cond_at[0],
-            "both_rows": ROWS_AT - 2 * KIB + KIB // 4,
+            "both_rows": ROWS_AT - 2 * KIB,
             "h3": WEIGHTED_AT,
             "h3 low": WEIGHTED_AT,
             "h3 high": WEIGHTED_AT + KIB,

@@ -337,6 +337,7 @@ def tile_list_heating_loop_balance_kernel(
         for cols in entries:
             nc.vector.tensor_copy(pages[0][:].indirect(places[:, cols.start // 16 : cols.stop // 16]), weighted[0][:, cols])
         scatter(1)
+        scatter(1)
         z[0] = sb("z0", [P, T2], F32, tag="h2")[:]
         remainder(nc.gpsimd, 0, whole)
         couple(0, whole)

@@ -26,12 +26,14 @@ PASSES1 = K // 512
 PASSES2 = T2 // 512
 KIB = 1024
 ROW0 = P - 16 * PASSES1
-TAB_AT = [0, 12 * KIB, 30 * KIB]
-W1_AT = 8 * KIB
+EARLY = PASSES1 - 1
+ROW_LAST = P - 16
+TAB_AT = [8 * KIB, 26 * KIB, 40 * KIB]
+W1_AT = 19 * KIB
+ACT_LAST_AT = 81 * KIB
 ROWS_AT = 78 * KIB
 V_AT = [49 * KIB, 57 * KIB, 65 * KIB]
 WEIGHTED_AT = 71 * KIB
-SHARE = 192
 CHUNK = 256
 CHUNKS = T2 // CHUNK
 
@@ -64,7 +66,7 @@ def tile_list_heating_loop_balance_kernel(
         w1_raw = at("w1_raw", [P, PASSES1 * 2 * H], U8, W1_AT)
         both_rows = at("both_rows", [P, S + H], U8, ROWS_AT)
         v_codes = [at("v_codes%d" % a, [P, S], U32, V_AT[a]) for a in range(PASSES1)]
-        planes = sb("planes", [P, PASSES1 * (S + H)], U8)
+        planes = sb("planes", [P, EARLY * (S + H)], U8)
 
         nc.gpsimd.memset(w1_rows[:ROW0, :].bitcast(I32), 0)
         nc.gpsimd.memset(tab_rows[:ROW0, :].bitcast(I32), 0)
@@ -75,22 +77,20 @@ def tile_list_heating_loop_balance_kernel(
 
         vectors = sb("vectors", [P, H], F32)
         nc.gpsimd.memset(vectors[: P - 2, :], 0.0)
-        wgs_sb = sb("wgs_sb", [P, S], F32)
         nc.sync.dma_start(picks[:], offs)
-        for a in range(PASSES1):
-            nc.scalar.dma_start(tab_rows[ROW0 + a : P : PASSES1, :].bitcast(I32), tab_scales[a].bitcast(I32))
-            nc.sync.dma_start(w1_rows[ROW0 + a : P : PASSES1, :].bitcast(I32), w1_scales[a].bitcast(I32))
+        for queue, rows, scales in ((nc.scalar, tab_rows, tab_scales), (nc.sync, w1_rows, w1_scales)):
+            queue.dma_start(rows[ROW0:ROW_LAST, :].bitcast(I32), scales[:EARLY].bitcast(I32).rearrange("a q w -> q a w"))
+            queue.dma_start(rows[ROW_LAST:, :].bitcast(I32), scales[EARLY].bitcast(I32))
         for a in range(PASSES1):
             nc.sync.dma_start(tab_codes[a][:].bitcast(I32), tab_words[a].rearrange("p t i -> p (t i)").bitcast(I32))
             if a == 0:
                 nc.sync.dma_start(vectors[P - 2 : P - 1, :], b1.unsqueeze(0))
                 nc.sync.dma_start(vectors[P - 1 : P, :], gain.unsqueeze(0))
+                nc.sync.dma_start(places[:], offs2)
                 nc.sync.dma_start(
                     w1_raw[:].bitcast(I32).rearrange("p (a w) -> p a w", a=PASSES1),
                     w1_words.bitcast(I32).rearrange("a p w -> p a w"),
                 )
-        nc.sync.dma_start(wgs_sb[:], wgs)
-        nc.sync.dma_start(places[:], offs2)
 
         v_rows = sb("v_rows", [P, S], U8)
         nc.vector.tensor_copy(
@@ -99,9 +99,9 @@ def tile_list_heating_loop_balance_kernel(
         nc.vector.tensor_copy(v_rows[:], tab_rows[:].indirect(picks[:]))
         nc.vector.tensor_copy(both_rows[:, :S].bitcast(I32), v_rows[:].bitcast(I32))
         for q in range(QUADS):
-            first = ROW0 + 4 * PASSES1 * q
+            first = ROW0 + 4 * EARLY * q
             nc.scalar.dma_start(
-                planes[32 * q : 32 * q + 4, :].bitcast(I32), both_rows[first : first + 4 * PASSES1, :].bitcast(I32)
+                planes[32 * q : 32 * q + 4, :].bitcast(I32), both_rows[first : first + 4 * EARLY, :].bitcast(I32)
             )
         turned_vectors = bank(2, "turned_vectors", [P, PACK, P])
         for i in range(PACK):
@@ -109,37 +109,42 @@ def tile_list_heating_loop_balance_kernel(
         per_row = sb("per_row", [P, 2, PACK], F32)
         nc.vector.tensor_copy(per_row[:], turned_vectors[:, :, P - 2 :].rearrange("p i v -> p v i"))
         bias, gain_sb = per_row[:, 0, :], per_row[:, 1, :]
-        w1_codes = {}
-        w1_dealt = w1_raw[:].bitcast(U16).rearrange("p (a c i) -> p i a c", a=PASSES1, i=PACK)
-
-        def deal_words(slices, passes, dealt):
-            count = passes.stop - passes.start
-            nc.vector.tensor_copy(
-                dealt[:].bitcast(U16).rearrange("p (i a c) -> p i a c", a=count, c=P), w1_dealt[:, slices, passes, :]
-            )
-            for i in range(slices.start, slices.stop):
-                for a in range(passes.start, passes.stop):
-                    first = 2 * P * ((i - slices.start) * count + a - passes.start)
-                    w1_codes[i, a] = dealt[:, first : first + 2 * P]
-
         entries = [slice(0, S // 2), slice(S // 2, S)]
-        for a in range(PASSES1 - 1):
-            nc.vector.tensor_copy(v_codes[a][:], tab_codes[a][:].indirect(picks[:]))
-            if a == 0:
-                deal_words(slice(0, 1), slice(0, PASSES1), sb("w1_first", [P, PASSES1 * 2 * P], U8))
-                deal_words(slice(1, 2), slice(0, 1), sb("w1_early", [P, 1 * 2 * P], U8))
+        nc.vector.tensor_copy(v_codes[0][:], tab_codes[0][:].indirect(picks[:]))
+
+        wv_raw = at("wv_raw", [P, PACK, N], F32, TAB_AT[0] - 8 * KIB + 64)
+        wgs_sb = at("wgs_sb", [P, S], F32, TAB_AT[0] + 64)
+        heat_at = [TAB_AT[0] + 2 * KIB + 64, TAB_AT[1] - 3 * KIB, TAB_AT[1] + 5 * KIB, TAB_AT[2] - 3 * KIB - KIB // 2]
+        cond_at = [TAB_AT[0] + 6 * KIB + 64, TAB_AT[1] + KIB, V_AT[2] + KIB, V_AT[2] - 3 * KIB]
+        heat_rows = heat.rearrange("(p i) m -> p i m", i=PACK)
+        cond_rows = cond.rearrange("(p i) m -> p i m", i=PACK)
+        heat_first = at("heat0", [P, T2], F32, heat_at[0])
+        cond_first = at("cond0", [P, T2], F32, cond_at[0])
+        nc.sync.dma_start(wgs_sb[:], wgs)
+        nc.sync.dma_start(heat_first[:], heat_rows[:, 0, :])
+        nc.sync.dma_start(cond_first[:], cond_rows[:, 0, :])
+        nc.sync.dma_start(wv_raw[:], wv.rearrange("(p j) c -> p j c", j=PACK))
+
+        w1_dealt = sb("w1_dealt", [P, PACK, PASSES1, 2 * P], U8)
+        nc.vector.tensor_copy(
+            w1_dealt[:].bitcast(U16), w1_raw[:].bitcast(U16).rearrange("p (a c i) -> p i a c", a=PASSES1, i=PACK)
+        )
+        last_plane = at("last_plane", [P, S + H], U8, W1_AT)
+        nc.gpsimd.memset(last_plane[:].bitcast(I32), 0)
+        for q in range(QUADS):
+            first = ROW_LAST + 4 * q
+            nc.scalar.dma_start(last_plane[32 * q : 32 * q + 4, :].bitcast(I32), both_rows[first : first + 4, :].bitcast(I32))
+        nc.vector.tensor_copy(v_codes[1][:], tab_codes[1][:].indirect(picks[:]))
         for e in entries:
             nc.vector.tensor_copy(v_codes[-1][:, e], tab_codes[-1][:].indirect(picks[:, e.start // 16 : e.stop // 16]))
-        deal_words(slice(1, 2), slice(1, PASSES1), at("w1_late", [P, (PASSES1 - 1) * 2 * P], U8, TAB_AT[2] + 7 * KIB))
-        deal_words(slice(2, PACK), slice(0, PASSES1), at("w1_pair", [P, PASSES1 * 4 * P], U8, TAB_AT[2] + KIB))
         d = {i: bank(3 + i, "d%d" % i, [P, S]) for i in range(1, PACK)}
         d_first = [bank(e, "d0_%d" % e, [P, S // 2]) for e in range(2)]
 
         def first_product(out, i, a, cols, start, stop):
-            plane = planes[:, a * (S + H) : (a + 1) * (S + H)]
+            plane = planes[:, a * (S + H) : (a + 1) * (S + H)] if a < EARLY else last_plane[:]
             nc.tensor.matmul_mx(
                 out=out,
-                lhsT=w1_codes[i, a].bitcast(FP4X4),
+                lhsT=w1_dealt[:, i, a, :].bitcast(FP4X4),
                 lhsT_scale=plane[:, S + i * P : S + (i + 1) * P],
                 rhs=v_codes[a][:, cols].bitcast(FP8X4),
                 rhs_scale=plane[:, cols],
@@ -147,32 +152,22 @@ def tile_list_heating_loop_balance_kernel(
                 stop=stop,
             )
 
-        for e in range(2):
-            for a in range(PASSES1):
+        for a in range(PASSES1):
+            for e in range(2):
                 for n in range(2):
                     cols = slice(entries[e].start + n * P, entries[e].start + (n + 1) * P)
                     out = d_first[e][:, n * P : (n + 1) * P]
                     first_product(out, 0, a, cols, (a, n) == (0, 0), (a, n) == (PASSES1 - 1, 1))
-        for i in range(1, PACK):
-            for a in range(PASSES1):
+            for i in range(1, PACK):
                 first_product(d[i][:], i, a, slice(0, S), a == 0, a == PASSES1 - 1)
 
-        heat_at = [TAB_AT[1] + 3 * KIB, TAB_AT[2] + 3 * KIB + KIB // 2, V_AT[0] - 3 * KIB, V_AT[1] + KIB]
-        cond_at = [TAB_AT[1] + 7 * KIB, TAB_AT[2] + 7 * KIB + KIB // 2, V_AT[2] + KIB, V_AT[2] - 3 * KIB]
         heat1_and_more = at("heat1_and_more", [P, S // 2 + T2], F32, heat_at[1] - KIB)
-        heat_sb = [
-            heat1_and_more[:, S // 2 :] if i == 1 else at("heat%d" % i, [P, T2], F32, heat_at[i])[:] for i in range(PACK)
-        ]
-        cond_sb = [at("cond%d" % i, [P, T2], F32, cond_at[i])[:] for i in range(PACK)]
-        wc_codes = [at("wc_codes%d" % a, [P, T2], U32, V_AT[0] + KIB + 4 * KIB * a) for a in range(PASSES2)]
-        wv_raw = at("wv_raw", [P, PACK, N], F32, TAB_AT[2] - 7 * KIB)
+        heat_sb = [heat_first[:], heat1_and_more[:, S // 2 :]]
+        heat_sb.extend(at("heat%d" % i, [P, T2], F32, heat_at[i])[:] for i in range(2, PACK))
+        cond_sb = [cond_first[:]] + [at("cond%d" % i, [P, T2], F32, cond_at[i])[:] for i in range(1, PACK)]
+        wc_codes = [at("wc_codes%d" % a, [P, T2], U32, TAB_AT[2] + KIB // 2 + 4 * KIB * a) for a in range(PASSES2)]
         wc_plane = at("wc_plane", [P, T2], U8, ROWS_AT + KIB // 2)
         nc.gpsimd.memset(wc_plane[:].bitcast(I32), 0)
-        heat_rows = heat.rearrange("(p i) m -> p i m", i=PACK)
-        cond_rows = cond.rearrange("(p i) m -> p i m", i=PACK)
-        nc.sync.dma_start(heat_sb[0], heat_rows[:, 0, :])
-        nc.sync.dma_start(cond_sb[0], cond_rows[:, 0, :])
-        nc.sync.dma_start(wv_raw[:], wv.rearrange("(p j) c -> p j c", j=PACK))
         nc.sync.dma_start(heat_sb[1], heat_rows[:, 1, :])
         nc.sync.dma_start(cond_sb[1], cond_rows[:, 1, :])
         nc.sync.dma_start(heat_sb[2], heat_rows[:, 2, :])
@@ -218,12 +213,8 @@ def tile_list_heating_loop_balance_kernel(
             nc.vector.tensor_copy(pages[i % 2][:].indirect(places[:]), weighted[i][:, :])
 
         def gelu(i):
-            act[i] = sb("act%d" % i, [P, S], F32)
+            act[i] = at("act3", [P, S], F32, ACT_LAST_AT) if i == 3 else sb("act%d" % i, [P, S], F32)
             nc.scalar.activation(act[i][:], d[i][:], GELU, bias=bias[:, i : i + 1])
-
-        def weigh_on_vector(i, tag=None):
-            weighted[i] = after("weighted%d" % i, [P, S], F32, tag=tag)
-            nc.vector.scalar_tensor_tensor(weighted[i][:], act[i][:], gain_sb[:, i : i + 1], wgs_sb[:], MULT, MULT)
 
         def weigh_on_gpsimd(i):
             h = sb("h%d" % i, [P, S], F32)
@@ -337,7 +328,6 @@ def tile_list_heating_loop_balance_kernel(
         for cols in entries:
             nc.vector.tensor_copy(pages[0][:].indirect(places[:, cols.start // 16 : cols.stop // 16]), weighted[0][:, cols])
         scatter(1)
-        scatter(1)
         z[0] = sb("z0", [P, T2], F32, tag="h2")[:]
         remainder(nc.gpsimd, 0, whole)
         couple(0, whole)
@@ -348,7 +338,7 @@ def tile_list_heating_loop_balance_kernel(
         z[1] = after("z1", [P, T2], F32, tag="cond0")[:]
         remainder(nc.gpsimd, 1, whole)
         nc.gpsimd.tensor_tensor(weighted[3][:, entries[1]], h_last[:, entries[1]], wgs_sb[:, entries[1]], MULT)
-        z_last = sb("z_last", [P, 2, T2], F32)
+        z_last = at("z_last", [P, 2, T2], F32, ACT_LAST_AT + KIB)
         wv_round = z_last[:, 0, :].bitcast(BF16)
         nc.scalar.copy(
             wv_round.rearrange("p (t m j) -> p m t j", t=PACK, j=PACK),

@@ -28,12 +28,11 @@ KIB = 1024
 ROW0 = P - 16 * PASSES1
 EARLY = PASSES1 - 1
 ROW_LAST = P - 16
-TAB_AT = [8 * KIB, 26 * KIB, 40 * KIB]
-W1_AT = 19 * KIB
+TAB_AT = [0, 20 * KIB, 40 * KIB]
 ACT_LAST_AT = 81 * KIB
 ROWS_AT = 78 * KIB
-V_AT = [49 * KIB, 57 * KIB, 65 * KIB]
-WEIGHTED_AT = 71 * KIB
+V_AT = [54 * KIB, 62 * KIB, 70 * KIB]
+WEIGHTED_AT = 92 * KIB
 CHUNK = 256
 CHUNKS = T2 // CHUNK
 
@@ -61,16 +60,18 @@ def tile_list_heating_loop_balance_kernel(
         picks = keep.tile([P, S // 16], U16, name="picks")
         places = keep.tile([P, S // 16], U16, name="places")
         tab_rows = sb("tab_rows", [P, T], U8)
-        w1_rows = at("w1_rows", [P, H], U8, ROWS_AT - 2 * KIB)
+        w1_rows = at("w1_rows", [P, H], U8, ROWS_AT - 3 * KIB)
         tab_codes = [at("tab_codes%d" % a, [P, T], U32, TAB_AT[a]) for a in range(PASSES1)]
-        w1_raw = at("w1_raw", [P, PASSES1 * 2 * H], U8, W1_AT)
+        w1_raw = sb("w1_raw", [P, PASSES1 * 2 * H], U8)
         both_rows = at("both_rows", [P, S + H], U8, ROWS_AT)
         v_codes = [at("v_codes%d" % a, [P, S], U32, V_AT[a]) for a in range(PASSES1)]
         planes = sb("planes", [P, EARLY * (S + H)], U8)
+        last_plane = sb("last_plane", [P, S + H], U8)
 
         nc.gpsimd.memset(w1_rows[:ROW0, :].bitcast(I32), 0)
         nc.gpsimd.memset(tab_rows[:ROW0, :].bitcast(I32), 0)
         nc.vector.memset(planes[:].bitcast(I32), 0)
+        nc.vector.memset(last_plane[:].bitcast(I32), 0)
 
         ident = sb("ident", [P, P], F32)
         make_identity(nc, ident[:])
@@ -81,8 +82,12 @@ def tile_list_heating_loop_balance_kernel(
         for queue, rows, scales in ((nc.scalar, tab_rows, tab_scales), (nc.sync, w1_rows, w1_scales)):
             queue.dma_start(rows[ROW0:ROW_LAST, :].bitcast(I32), scales[:EARLY].bitcast(I32).rearrange("a q w -> q a w"))
             queue.dma_start(rows[ROW_LAST:, :].bitcast(I32), scales[EARLY].bitcast(I32))
-        for a in range(PASSES1):
-            nc.sync.dma_start(tab_codes[a][:].bitcast(I32), tab_words[a].rearrange("p t i -> p (t i)").bitcast(I32))
+
+        def load_table(queue, a):
+            queue.dma_start(tab_codes[a][:].bitcast(I32), tab_words[a].rearrange("p t i -> p (t i)").bitcast(I32))
+
+        for a in range(EARLY):
+            load_table(nc.sync, a)
             if a == 0:
                 nc.sync.dma_start(vectors[P - 2 : P - 1, :], b1.unsqueeze(0))
                 nc.sync.dma_start(vectors[P - 1 : P, :], gain.unsqueeze(0))
@@ -100,9 +105,15 @@ def tile_list_heating_loop_balance_kernel(
         nc.vector.tensor_copy(both_rows[:, :S].bitcast(I32), v_rows[:].bitcast(I32))
         for q in range(QUADS):
             first = ROW0 + 4 * EARLY * q
-            nc.scalar.dma_start(
+            nc.sync.dma_start(
                 planes[32 * q : 32 * q + 4, :].bitcast(I32), both_rows[first : first + 4 * EARLY, :].bitcast(I32)
             )
+        load_table(nc.sync, EARLY)
+        for q in range(QUADS):
+            first = ROW_LAST + 4 * q
+            nc.sync.dma_start(last_plane[32 * q : 32 * q + 4, :].bitcast(I32), both_rows[first : first + 4, :].bitcast(I32))
+        wgs_sb = sb("wgs_sb", [P, S], F32)
+        nc.sync.dma_start(wgs_sb[:], wgs)
         turned_vectors = bank(2, "turned_vectors", [P, PACK, P])
         for i in range(PACK):
             nc.tensor.transpose(turned_vectors[:, i, :], vectors[:, i:H:PACK], ident[:])
@@ -111,32 +122,13 @@ def tile_list_heating_loop_balance_kernel(
         bias, gain_sb = per_row[:, 0, :], per_row[:, 1, :]
         entries = [slice(0, S // 2), slice(S // 2, S)]
         nc.vector.tensor_copy(v_codes[0][:], tab_codes[0][:].indirect(picks[:]))
-
-        wv_raw = at("wv_raw", [P, PACK, N], F32, TAB_AT[0] - 8 * KIB + 64)
-        wgs_sb = at("wgs_sb", [P, S], F32, TAB_AT[0] + 64)
-        heat_at = [TAB_AT[0] + 2 * KIB + 64, TAB_AT[1] - 3 * KIB, TAB_AT[1] + 5 * KIB, TAB_AT[2] - 3 * KIB - KIB // 2]
-        cond_at = [TAB_AT[0] + 6 * KIB + 64, TAB_AT[1] + KIB, V_AT[2] + KIB, V_AT[2] - 3 * KIB]
-        heat_rows = heat.rearrange("(p i) m -> p i m", i=PACK)
-        cond_rows = cond.rearrange("(p i) m -> p i m", i=PACK)
-        heat_first = at("heat0", [P, T2], F32, heat_at[0])
-        cond_first = at("cond0", [P, T2], F32, cond_at[0])
-        nc.sync.dma_start(wgs_sb[:], wgs)
-        nc.sync.dma_start(heat_first[:], heat_rows[:, 0, :])
-        nc.sync.dma_start(cond_first[:], cond_rows[:, 0, :])
-        nc.sync.dma_start(wv_raw[:], wv.rearrange("(p j) c -> p j c", j=PACK))
-
-        w1_dealt = sb("w1_dealt", [P, PACK, PASSES1, 2 * P], U8)
-        nc.vector.tensor_copy(
-            w1_dealt[:].bitcast(U16), w1_raw[:].bitcast(U16).rearrange("p (a c i) -> p i a c", a=PASSES1, i=PACK)
-        )
-        last_plane = at("last_plane", [P, S + H], U8, W1_AT)
-        nc.gpsimd.memset(last_plane[:].bitcast(I32), 0)
-        for q in range(QUADS):
-            first = ROW_LAST + 4 * q
-            nc.scalar.dma_start(last_plane[32 * q : 32 * q + 4, :].bitcast(I32), both_rows[first : first + 4, :].bitcast(I32))
+        w1_slices = w1_raw[:].bitcast(U16).rearrange("p (a c i) -> p i a c", a=PASSES1, i=PACK)
+        w1_dealt = [sb("w1_low", [P, 2, PASSES1, 2 * P], U8), at("w1_high", [P, 2, PASSES1, 2 * P], U8, ROWS_AT - KIB)]
+        nc.vector.tensor_copy(w1_dealt[0][:].bitcast(U16), w1_slices[:, 0:2])
         nc.vector.tensor_copy(v_codes[1][:], tab_codes[1][:].indirect(picks[:]))
         for e in entries:
             nc.vector.tensor_copy(v_codes[-1][:, e], tab_codes[-1][:].indirect(picks[:, e.start // 16 : e.stop // 16]))
+        nc.vector.tensor_copy(w1_dealt[1][:].bitcast(U16), w1_slices[:, 2:4])
         d = {i: bank(3 + i, "d%d" % i, [P, S]) for i in range(1, PACK)}
         d_first = [bank(e, "d0_%d" % e, [P, S // 2]) for e in range(2)]
 
@@ -144,7 +136,7 @@ def tile_list_heating_loop_balance_kernel(
             plane = planes[:, a * (S + H) : (a + 1) * (S + H)] if a < EARLY else last_plane[:]
             nc.tensor.matmul_mx(
                 out=out,
-                lhsT=w1_dealt[:, i, a, :].bitcast(FP4X4),
+                lhsT=w1_dealt[i // 2][:, i % 2, a, :].bitcast(FP4X4),
                 lhsT_scale=plane[:, S + i * P : S + (i + 1) * P],
                 rhs=v_codes[a][:, cols].bitcast(FP8X4),
                 rhs_scale=plane[:, cols],
@@ -158,16 +150,27 @@ def tile_list_heating_loop_balance_kernel(
                     cols = slice(entries[e].start + n * P, entries[e].start + (n + 1) * P)
                     out = d_first[e][:, n * P : (n + 1) * P]
                     first_product(out, 0, a, cols, (a, n) == (0, 0), (a, n) == (PASSES1 - 1, 1))
-            for i in range(1, PACK):
+            first_product(d[1][:], 1, a, slice(0, S), a == 0, a == PASSES1 - 1)
+        for i in range(2, PACK):
+            for a in range(PASSES1):
                 first_product(d[i][:], i, a, slice(0, S), a == 0, a == PASSES1 - 1)
 
+        heat_at = [TAB_AT[1] + KIB // 2, TAB_AT[2] - 3 * KIB, V_AT[0] - 3 * KIB, V_AT[1] + KIB]
+        cond_at = [TAB_AT[1] + 4 * KIB + KIB // 2, TAB_AT[2] + KIB, V_AT[2] + KIB, V_AT[2] - 3 * KIB]
         heat1_and_more = at("heat1_and_more", [P, S // 2 + T2], F32, heat_at[1] - KIB)
-        heat_sb = [heat_first[:], heat1_and_more[:, S // 2 :]]
-        heat_sb.extend(at("heat%d" % i, [P, T2], F32, heat_at[i])[:] for i in range(2, PACK))
-        cond_sb = [cond_first[:]] + [at("cond%d" % i, [P, T2], F32, cond_at[i])[:] for i in range(1, PACK)]
-        wc_codes = [at("wc_codes%d" % a, [P, T2], U32, TAB_AT[2] + KIB // 2 + 4 * KIB * a) for a in range(PASSES2)]
+        heat_sb = [
+            heat1_and_more[:, S // 2 :] if i == 1 else at("heat%d" % i, [P, T2], F32, heat_at[i])[:] for i in range(PACK)
+        ]
+        cond_sb = [at("cond%d" % i, [P, T2], F32, cond_at[i])[:] for i in range(PACK)]
+        wc_codes = [at("wc_codes%d" % a, [P, T2], U32, V_AT[0] + KIB + 4 * KIB * a) for a in range(PASSES2)]
+        wv_raw = at("wv_raw", [P, PACK, N], F32, TAB_AT[1] - 7 * KIB - KIB // 2)
         wc_plane = at("wc_plane", [P, T2], U8, ROWS_AT + KIB // 2)
         nc.gpsimd.memset(wc_plane[:].bitcast(I32), 0)
+        heat_rows = heat.rearrange("(p i) m -> p i m", i=PACK)
+        cond_rows = cond.rearrange("(p i) m -> p i m", i=PACK)
+        nc.sync.dma_start(heat_sb[0], heat_rows[:, 0, :])
+        nc.sync.dma_start(cond_sb[0], cond_rows[:, 0, :])
+        nc.sync.dma_start(wv_raw[:], wv.rearrange("(p j) c -> p j c", j=PACK))
         nc.sync.dma_start(heat_sb[1], heat_rows[:, 1, :])
         nc.sync.dma_start(cond_sb[1], cond_rows[:, 1, :])
         nc.sync.dma_start(heat_sb[2], heat_rows[:, 2, :])
@@ -184,7 +187,7 @@ def tile_list_heating_loop_balance_kernel(
 
         left_by = {
             "cond0": cond_at[0],
-            "both_rows": ROWS_AT - 2 * KIB,
+            "both_rows": ROWS_AT - 3 * KIB,
             "h3": WEIGHTED_AT,
             "h3 low": WEIGHTED_AT,
             "h3 high": WEIGHTED_AT + KIB,

@@ -33,6 +33,7 @@ ACT_LAST_AT = 81 * KIB
 ROWS_AT = 78 * KIB
 V_AT = [54 * KIB, 62 * KIB, 70 * KIB]
 WEIGHTED_AT = 92 * KIB
+ZC_AT = 96 * KIB
 CHUNK = 256
 CHUNKS = T2 // CHUNK
 
@@ -161,15 +162,16 @@ def tile_list_heating_loop_balance_kernel(
         heat_sb = [
             heat1_and_more[:, S // 2 :] if i == 1 else at("heat%d" % i, [P, T2], F32, heat_at[i])[:] for i in range(PACK)
         ]
-        cond_sb = [at("cond%d" % i, [P, T2], F32, cond_at[i])[:] for i in range(PACK)]
+        z_first = at("z_first", [P, 2, T2], F32, cond_at[0])
+        cond_sb = [z_first[:, 1, :]] + [at("cond%d" % i, [P, T2], F32, cond_at[i])[:] for i in range(1, PACK)]
         wc_codes = [at("wc_codes%d" % a, [P, T2], U32, V_AT[0] + KIB + 4 * KIB * a) for a in range(PASSES2)]
         wv_raw = at("wv_raw", [P, PACK, N], F32, TAB_AT[1] - 7 * KIB - KIB // 2)
         wc_plane = at("wc_plane", [P, T2], U8, ROWS_AT + KIB // 2)
         nc.gpsimd.memset(wc_plane[:].bitcast(I32), 0)
         heat_rows = heat.rearrange("(p i) m -> p i m", i=PACK)
         cond_rows = cond.rearrange("(p i) m -> p i m", i=PACK)
-        nc.sync.dma_start(heat_sb[0], heat_rows[:, 0, :])
         nc.sync.dma_start(cond_sb[0], cond_rows[:, 0, :])
+        nc.sync.dma_start(heat_sb[0], heat_rows[:, 0, :])
         nc.sync.dma_start(wv_raw[:], wv.rearrange("(p j) c -> p j c", j=PACK))
         nc.sync.dma_start(heat_sb[1], heat_rows[:, 1, :])
         nc.sync.dma_start(cond_sb[1], cond_rows[:, 1, :])
@@ -181,12 +183,11 @@ def tile_list_heating_loop_balance_kernel(
             )
         for a in range(PASSES2):
             nc.sync.dma_start(wc_codes[a][:].bitcast(I32), wc_words[a].rearrange("p c i -> p (c i)").bitcast(I32))
+        nc.sync.dma_start(cond_sb[3], cond_rows[:, 3, :])
         nc.sync.dma_start(heat_sb[3], heat_rows[:, 3, :])
-        for i in (3, 2):
-            nc.sync.dma_start(cond_sb[i], cond_rows[:, i, :])
+        nc.sync.dma_start(cond_sb[2], cond_rows[:, 2, :])
 
         left_by = {
-            "cond0": cond_at[0],
             "both_rows": ROWS_AT - 3 * KIB,
             "h3": WEIGHTED_AT,
             "h3 low": WEIGHTED_AT,
@@ -198,7 +199,7 @@ def tile_list_heating_loop_balance_kernel(
                 return at(name, shape, dtype, left_by[tag])
             return sb(name, shape, dtype, tag=tag)
 
-        z_round = [sb("z_round%d" % c, [P, CHUNK, PACK], BF16) for c in range(CHUNKS)]
+        z_round = {c: sb("z_round%d" % c, [P, CHUNK, PACK], BF16) for c in range(2)}
         z_codes = [sb("z_codes%d" % c, [P, CHUNK], U32) for c in range(CHUNKS)]
         z_plane = [sb("z_plane%d" % c, [P, CHUNK], U8) for c in range(CHUNKS)]
         zct = [sb("zct%d" % i, [P, T2], BF16) for i in range(PACK)]
@@ -220,7 +221,7 @@ def tile_list_heating_loop_balance_kernel(
             nc.scalar.activation(act[i][:], d[i][:], GELU, bias=bias[:, i : i + 1])
 
         def weigh_on_gpsimd(i):
-            h = sb("h%d" % i, [P, S], F32)
+            h = z_first[:, 0, :S] if i == 2 else sb("h%d" % i, [P, S], F32)
             weighted[i] = after("weighted%d" % i, [P, S], F32, tag="weighted%d" % i)
             nc.scalar.activation(h[:], act[i][:], COPY, scale=gain_sb[:, i : i + 1])
             nc.gpsimd.tensor_tensor(weighted[i][:], h[:], wgs_sb[:], MULT)
@@ -274,6 +275,12 @@ def tile_list_heating_loop_balance_kernel(
 
         def round_z(copy, c, slots, rows):
             copy(z_round[c][:, :, slots], rows[:, :, c * CHUNK : (c + 1) * CHUNK].rearrange("p e m -> p m e"))
+
+        def round_pair(c, slots, rows):
+            nc.scalar.copy(
+                z_round[c][:, :, slots].rearrange("p (m j) e -> p m e j", j=2),
+                rows[:, :, c * CHUNK : (c + 1) * CHUNK].rearrange("p e (m j) -> p m e j", j=2),
+            )
 
         def quantize_z(c):
             nc.vector.quantize_mx(
@@ -331,14 +338,11 @@ def tile_list_heating_loop_balance_kernel(
         for cols in entries:
             nc.vector.tensor_copy(pages[0][:].indirect(places[:, cols.start // 16 : cols.stop // 16]), weighted[0][:, cols])
         scatter(1)
-        z[0] = sb("z0", [P, T2], F32, tag="h2")[:]
+        z[0], z[1] = z_first[:, 0, :], z_first[:, 1, :]
         remainder(nc.gpsimd, 0, whole)
         couple(0, whole)
         turn(0)
-        for c in range(CHUNKS):
-            round_z(nc.scalar.copy, c, slice(0, 1), z[0].unsqueeze(1))
         scatter(2)
-        z[1] = after("z1", [P, T2], F32, tag="cond0")[:]
         remainder(nc.gpsimd, 1, whole)
         nc.gpsimd.tensor_tensor(weighted[3][:, entries[1]], h_last[:, entries[1]], wgs_sb[:, entries[1]], MULT)
         z_last = at("z_last", [P, 2, T2], F32, ACT_LAST_AT + KIB)
@@ -347,6 +351,7 @@ def tile_list_heating_loop_balance_kernel(
             wv_round.rearrange("p (t m j) -> p m t j", t=PACK, j=PACK),
             wv_raw[:].rearrange("p j (m t) -> p m t j", t=PACK),
         )
+        zc_rows[1] = at("zc1", [P, T2], BF16, ZC_AT)
         couple(1, whole)
         quantize_zc(0, tag="h3 low")
         wv_codes = after("wv_codes", [P, N], U32, tag="h3 high")
@@ -355,7 +360,9 @@ def tile_list_heating_loop_balance_kernel(
         for c in range(CHUNKS):
             right(0, c, True, False)
         for c in range(CHUNKS):
-            round_z(nc.scalar.copy, c, slice(1, 2), z[1].unsqueeze(1))
+            if c >= 2:
+                z_round[c] = at("z_round%d" % c, [P, CHUNK, PACK], BF16, ZC_AT + (2 * c - 5) * KIB)
+            round_pair(c, slice(0, 2), z_first[:])
         scatter(3)
         z[2], z[3] = z_last[:, 0, :], z_last[:, 1, :]
         remainder(nc.gpsimd, 2, whole)
@@ -390,43 +397,56 @@ def tile_list_heating_loop_balance_kernel(
         def close_low(c):
             left(0, c, False, False)
             left(1, c, False, True)
-            empty(0, c)
+
+        def open_high(c):
+            left(2, c, True, False)
+            left(3, c, False, False)
 
         for cols in (slice(0, CHUNK), slice(CHUNK, 2 * CHUNK), halves[1]):
             remainder(nc.vector, 3, cols)
         for c in range(2):
-            round_z(nc.scalar.copy, c, slice(2, 4), z_last[:])
+            round_pair(c, slice(2, 4), z_last[:])
         couple_sorted(3, 0)
         quantize_z(0)
         close_low(0)
+        open_high(0)
+        empty(0, 0)
         couple_sorted(3, 1)
         turn(3, b=6)
         quantize_z(1)
-        round_z(nc.scalar.copy, 2, slice(2, 4), z_last[:])
+        close_low(1)
+        open_high(1)
+        round_pair(2, slice(2, 4), z_last[:])
         for a in range(PASSES2):
             couple_sorted(2, a)
         turn(2)
-        close_low(1)
+        empty(0, 1)
         quantize_zc(3)
         round_z(nc.vector.tensor_copy, 3, slice(2, 4), z_last[:])
+        quantize_z(2)
         quantize_zc(2)
-        for c in range(2, CHUNKS):
-            quantize_z(c)
-        for c in range(CHUNKS):
-            left(2, c, True, False)
-            left(3, c, False, False)
+        quantize_z(3)
+        right(3, 0, False, False)
+        close_low(2)
+        empty(0, 2)
+        right(2, 0, False, True)
+        empty(1, 0, nc.vector.tensor_copy)
+        close_low(3)
+        empty(0, 3)
+        for c in range(1, CHUNKS):
+            if c >= 2:
+                open_high(c)
             right(3, c, False, False)
             right(2, c, False, True)
-            empty(1, c, nc.vector.tensor_copy if c == 0 else nc.scalar.copy)
-            if c < 2:
-                close_low(c + 2)
+            empty(1, c)
         weave(0, nc.vector.tensor_copy)
         weave(1, nc.vector.tensor_copy)
         quantize_y(0)
         weave(2, nc.vector.tensor_copy)
+        quantize_y(1)
         weave(3, nc.scalar.copy, 0, CHUNK // 4)
         weave(3, nc.vector.tensor_copy, CHUNK // 4, CHUNK - CHUNK // 4)
-        for c in range(1, CHUNKS):
+        for c in range(2, CHUNKS):
             quantize_y(c)
         for q in range(QUADS):
             queue = nc.scalar if q < 2 else nc.sync

@@ -170,8 +170,8 @@ def tile_list_heating_loop_balance_kernel(
         nc.gpsimd.memset(wc_plane[:].bitcast(I32), 0)
         heat_rows = heat.rearrange("(p i) m -> p i m", i=PACK)
         cond_rows = cond.rearrange("(p i) m -> p i m", i=PACK)
-        nc.sync.dma_start(cond_sb[0], cond_rows[:, 0, :])
         nc.sync.dma_start(heat_sb[0], heat_rows[:, 0, :])
+        nc.sync.dma_start(cond_sb[0], cond_rows[:, 0, :])
         nc.sync.dma_start(wv_raw[:], wv.rearrange("(p j) c -> p j c", j=PACK))
         nc.sync.dma_start(heat_sb[1], heat_rows[:, 1, :])
         nc.sync.dma_start(cond_sb[1], cond_rows[:, 1, :])
@@ -183,8 +183,8 @@ def tile_list_heating_loop_balance_kernel(
             )
         for a in range(PASSES2):
             nc.sync.dma_start(wc_codes[a][:].bitcast(I32), wc_words[a].rearrange("p c i -> p (c i)").bitcast(I32))
-        nc.sync.dma_start(cond_sb[3], cond_rows[:, 3, :])
         nc.sync.dma_start(heat_sb[3], heat_rows[:, 3, :])
+        nc.sync.dma_start(cond_sb[3], cond_rows[:, 3, :])
         nc.sync.dma_start(cond_sb[2], cond_rows[:, 2, :])
 
         left_by = {
@@ -276,12 +276,6 @@ def tile_list_heating_loop_balance_kernel(
         def round_z(copy, c, slots, rows):
             copy(z_round[c][:, :, slots], rows[:, :, c * CHUNK : (c + 1) * CHUNK].rearrange("p e m -> p m e"))
 
-        def round_pair(c, slots, rows):
-            nc.scalar.copy(
-                z_round[c][:, :, slots].rearrange("p (m j) e -> p m e j", j=2),
-                rows[:, :, c * CHUNK : (c + 1) * CHUNK].rearrange("p e (m j) -> p m e j", j=2),
-            )
-
         def quantize_z(c):
             nc.vector.quantize_mx(
                 out=z_codes[c][:].bitcast(FP8X4), scales=z_plane[c][:], in_=z_round[c][:].rearrange("p m i -> p (m i)")
@@ -362,7 +356,7 @@ def tile_list_heating_loop_balance_kernel(
         for c in range(CHUNKS):
             if c >= 2:
                 z_round[c] = at("z_round%d" % c, [P, CHUNK, PACK], BF16, ZC_AT + (2 * c - 5) * KIB)
-            round_pair(c, slice(0, 2), z_first[:])
+            round_z(nc.scalar.copy, c, slice(0, 2), z_first[:])
         scatter(3)
         z[2], z[3] = z_last[:, 0, :], z_last[:, 1, :]
         remainder(nc.gpsimd, 2, whole)
@@ -405,7 +399,7 @@ def tile_list_heating_loop_balance_kernel(
         for cols in (slice(0, CHUNK), slice(CHUNK, 2 * CHUNK), halves[1]):
             remainder(nc.vector, 3, cols)
         for c in range(2):
-            round_pair(c, slice(2, 4), z_last[:])
+            round_z(nc.scalar.copy, c, slice(2, 4), z_last[:])
         couple_sorted(3, 0)
         quantize_z(0)
         close_low(0)
@@ -416,7 +410,7 @@ def tile_list_heating_loop_balance_kernel(
         quantize_z(1)
         close_low(1)
         open_high(1)
-        round_pair(2, slice(2, 4), z_last[:])
+        round_z(nc.scalar.copy, 2, slice(2, 4), z_last[:])
         for a in range(PASSES2):
             couple_sorted(2, a)
         turn(2)

@@ -26,14 +26,11 @@ PASSES1 = K // 512
 PASSES2 = T2 // 512
 KIB = 1024
 ROW0 = P - 16 * PASSES1
-EARLY = PASSES1 - 1
-ROW_LAST = P - 16
-TAB_AT = [0, 20 * KIB, 40 * KIB]
+TAB_AT = [0, 12 * KIB, 30 * KIB]
 ACT_LAST_AT = 81 * KIB
-ROWS_AT = 78 * KIB
-V_AT = [54 * KIB, 62 * KIB, 70 * KIB]
-WEIGHTED_AT = 92 * KIB
 ZC_AT = 96 * KIB
+ROWS_AT = 78 * KIB
+V_AT = [49 * KIB, 57 * KIB, 65 * KIB]
 CHUNK = 256
 CHUNKS = T2 // CHUNK
 
@@ -61,42 +58,38 @@ def tile_list_heating_loop_balance_kernel(
         picks = keep.tile([P, S // 16], U16, name="picks")
         places = keep.tile([P, S // 16], U16, name="places")
         tab_rows = sb("tab_rows", [P, T], U8)
-        w1_rows = at("w1_rows", [P, H], U8, ROWS_AT - 3 * KIB)
+        w1_rows = at("w1_rows", [P, H], U8, ROWS_AT - 2 * KIB)
         tab_codes = [at("tab_codes%d" % a, [P, T], U32, TAB_AT[a]) for a in range(PASSES1)]
         w1_raw = sb("w1_raw", [P, PASSES1 * 2 * H], U8)
         both_rows = at("both_rows", [P, S + H], U8, ROWS_AT)
         v_codes = [at("v_codes%d" % a, [P, S], U32, V_AT[a]) for a in range(PASSES1)]
-        planes = sb("planes", [P, EARLY * (S + H)], U8)
-        last_plane = sb("last_plane", [P, S + H], U8)
+        planes = sb("planes", [P, PASSES1 * (S + H)], U8)
 
         nc.gpsimd.memset(w1_rows[:ROW0, :].bitcast(I32), 0)
         nc.gpsimd.memset(tab_rows[:ROW0, :].bitcast(I32), 0)
         nc.vector.memset(planes[:].bitcast(I32), 0)
-        nc.vector.memset(last_plane[:].bitcast(I32), 0)
 
         ident = sb("ident", [P, P], F32)
         make_identity(nc, ident[:])
 
         vectors = sb("vectors", [P, H], F32)
         nc.gpsimd.memset(vectors[: P - 2, :], 0.0)
+        wgs_sb = sb("wgs_sb", [P, S], F32)
         nc.sync.dma_start(picks[:], offs)
-        for queue, rows, scales in ((nc.scalar, tab_rows, tab_scales), (nc.sync, w1_rows, w1_scales)):
-            queue.dma_start(rows[ROW0:ROW_LAST, :].bitcast(I32), scales[:EARLY].bitcast(I32).rearrange("a q w -> q a w"))
-            queue.dma_start(rows[ROW_LAST:, :].bitcast(I32), scales[EARLY].bitcast(I32))
-
-        def load_table(queue, a):
-            queue.dma_start(tab_codes[a][:].bitcast(I32), tab_words[a].rearrange("p t i -> p (t i)").bitcast(I32))
-
-        for a in range(EARLY):
-            load_table(nc.sync, a)
+        for a in range(PASSES1):
+            nc.scalar.dma_start(tab_rows[ROW0 + a : P : PASSES1, :].bitcast(I32), tab_scales[a].bitcast(I32))
+            nc.sync.dma_start(w1_rows[ROW0 + a : P : PASSES1, :].bitcast(I32), w1_scales[a].bitcast(I32))
+        for a in range(PASSES1):
+            nc.sync.dma_start(tab_codes[a][:].bitcast(I32), tab_words[a].rearrange("p t i -> p (t i)").bitcast(I32))
             if a == 0:
                 nc.sync.dma_start(vectors[P - 2 : P - 1, :], b1.unsqueeze(0))
                 nc.sync.dma_start(vectors[P - 1 : P, :], gain.unsqueeze(0))
-                nc.sync.dma_start(places[:], offs2)
                 nc.sync.dma_start(
                     w1_raw[:].bitcast(I32).rearrange("p (a w) -> p a w", a=PASSES1),
                     w1_words.bitcast(I32).rearrange("a p w -> p a w"),
                 )
+        nc.sync.dma_start(wgs_sb[:], wgs)
+        nc.sync.dma_start(places[:], offs2)
 
         v_rows = sb("v_rows", [P, S], U8)
         nc.vector.tensor_copy(
@@ -104,40 +97,50 @@ def tile_list_heating_loop_balance_kernel(
         )
         nc.vector.tensor_copy(v_rows[:], tab_rows[:].indirect(picks[:]))
         nc.vector.tensor_copy(both_rows[:, :S].bitcast(I32), v_rows[:].bitcast(I32))
-        for q in range(QUADS):
-            first = ROW0 + 4 * EARLY * q
-            nc.sync.dma_start(
-                planes[32 * q : 32 * q + 4, :].bitcast(I32), both_rows[first : first + 4 * EARLY, :].bitcast(I32)
+        for q in (0, 2, 1, 3):
+            first = ROW0 + 4 * PASSES1 * q
+            nc.scalar.dma_start(
+                planes[32 * q : 32 * q + 4, :].bitcast(I32), both_rows[first : first + 4 * PASSES1, :].bitcast(I32)
             )
-        load_table(nc.sync, EARLY)
-        for q in range(QUADS):
-            first = ROW_LAST + 4 * q
-            nc.sync.dma_start(last_plane[32 * q : 32 * q + 4, :].bitcast(I32), both_rows[first : first + 4, :].bitcast(I32))
-        wgs_sb = sb("wgs_sb", [P, S], F32)
-        nc.sync.dma_start(wgs_sb[:], wgs)
         turned_vectors = bank(2, "turned_vectors", [P, PACK, P])
         for i in range(PACK):
             nc.tensor.transpose(turned_vectors[:, i, :], vectors[:, i:H:PACK], ident[:])
         per_row = sb("per_row", [P, 2, PACK], F32)
         nc.vector.tensor_copy(per_row[:], turned_vectors[:, :, P - 2 :].rearrange("p i v -> p v i"))
         bias, gain_sb = per_row[:, 0, :], per_row[:, 1, :]
+        minus_gain = sb("minus_gain", [P, 1], F32)
+        nc.vector.tensor_scalar_mul(minus_gain[:], turned_vectors[:, 1, P - 1 :], -1.0)
+        w1_codes = {}
+        w1_dealt = w1_raw[:].bitcast(U16).rearrange("p (a c i) -> p i a c", a=PASSES1, i=PACK)
+
+        def deal_words(slices, passes, dealt):
+            count = passes.stop - passes.start
+            nc.vector.tensor_copy(
+                dealt[:].bitcast(U16).rearrange("p (i a c) -> p i a c", a=count, c=P), w1_dealt[:, slices, passes, :]
+            )
+            for i in range(slices.start, slices.stop):
+                for a in range(passes.start, passes.stop):
+                    first = 2 * P * ((i - slices.start) * count + a - passes.start)
+                    w1_codes[i, a] = dealt[:, first : first + 2 * P]
+
         entries = [slice(0, S // 2), slice(S // 2, S)]
-        nc.vector.tensor_copy(v_codes[0][:], tab_codes[0][:].indirect(picks[:]))
-        w1_slices = w1_raw[:].bitcast(U16).rearrange("p (a c i) -> p i a c", a=PASSES1, i=PACK)
-        w1_dealt = [sb("w1_low", [P, 2, PASSES1, 2 * P], U8), at("w1_high", [P, 2, PASSES1, 2 * P], U8, ROWS_AT - KIB)]
-        nc.vector.tensor_copy(w1_dealt[0][:].bitcast(U16), w1_slices[:, 0:2])
-        nc.vector.tensor_copy(v_codes[1][:], tab_codes[1][:].indirect(picks[:]))
+        for a in range(PASSES1 - 1):
+            nc.vector.tensor_copy(v_codes[a][:], tab_codes[a][:].indirect(picks[:]))
+            if a == 0:
+                deal_words(slice(0, 1), slice(0, PASSES1), sb("w1_first", [P, PASSES1 * 2 * P], U8))
+                deal_words(slice(1, 2), slice(0, 1), sb("w1_early", [P, 1 * 2 * P], U8))
         for e in entries:
             nc.vector.tensor_copy(v_codes[-1][:, e], tab_codes[-1][:].indirect(picks[:, e.start // 16 : e.stop // 16]))
-        nc.vector.tensor_copy(w1_dealt[1][:].bitcast(U16), w1_slices[:, 2:4])
+        deal_words(slice(1, 2), slice(1, PASSES1), at("w1_late", [P, (PASSES1 - 1) * 2 * P], U8, TAB_AT[2] + 7 * KIB))
+        deal_words(slice(2, PACK), slice(0, PASSES1), at("w1_pair", [P, PASSES1 * 4 * P], U8, TAB_AT[2] + 5 * KIB + KIB // 2))
         d = {i: bank(3 + i, "d%d" % i, [P, S]) for i in range(1, PACK)}
         d_first = [bank(e, "d0_%d" % e, [P, S // 2]) for e in range(2)]
 
         def first_product(out, i, a, cols, start, stop):
-            plane = planes[:, a * (S + H) : (a + 1) * (S + H)] if a < EARLY else last_plane[:]
+            plane = planes[:, a * (S + H) : (a + 1) * (S + H)]
             nc.tensor.matmul_mx(
                 out=out,
-                lhsT=w1_dealt[i // 2][:, i % 2, a, :].bitcast(FP4X4),
+                lhsT=w1_codes[i, a].bitcast(FP4X4),
                 lhsT_scale=plane[:, S + i * P : S + (i + 1) * P],
                 rhs=v_codes[a][:, cols].bitcast(FP8X4),
                 rhs_scale=plane[:, cols],
@@ -145,53 +148,49 @@ def tile_list_heating_loop_balance_kernel(
                 stop=stop,
             )
 
-        for a in range(PASSES1):
-            for e in range(2):
+        for e in range(2):
+            for a in range(PASSES1):
                 for n in range(2):
                     cols = slice(entries[e].start + n * P, entries[e].start + (n + 1) * P)
                     out = d_first[e][:, n * P : (n + 1) * P]
                     first_product(out, 0, a, cols, (a, n) == (0, 0), (a, n) == (PASSES1 - 1, 1))
-            first_product(d[1][:], 1, a, slice(0, S), a == 0, a == PASSES1 - 1)
-        for i in range(2, PACK):
+        for i in range(1, PACK):
             for a in range(PASSES1):
                 first_product(d[i][:], i, a, slice(0, S), a == 0, a == PASSES1 - 1)
 
-        heat_at = [TAB_AT[1] + KIB // 2, TAB_AT[2] - 3 * KIB, V_AT[0] - 3 * KIB, V_AT[1] + KIB]
-        cond_at = [TAB_AT[1] + 4 * KIB + KIB // 2, TAB_AT[2] + KIB, V_AT[2] + KIB, V_AT[2] - 3 * KIB]
-        heat1_and_more = at("heat1_and_more", [P, S // 2 + T2], F32, heat_at[1] - KIB)
-        heat_sb = [
-            heat1_and_more[:, S // 2 :] if i == 1 else at("heat%d" % i, [P, T2], F32, heat_at[i])[:] for i in range(PACK)
-        ]
-        z_first = at("z_first", [P, 2, T2], F32, cond_at[0])
-        cond_sb = [z_first[:, 1, :]] + [at("cond%d" % i, [P, T2], F32, cond_at[i])[:] for i in range(1, PACK)]
-        wc_codes = [at("wc_codes%d" % a, [P, T2], U32, V_AT[0] + KIB + 4 * KIB * a) for a in range(PASSES2)]
-        wv_raw = at("wv_raw", [P, PACK, N], F32, TAB_AT[1] - 7 * KIB - KIB // 2)
+        half_kib = KIB // 2
+        heat_at = [TAB_AT[1] + half_kib, TAB_AT[1] - 7 * half_kib, V_AT[0] + half_kib, V_AT[2] - 7 * half_kib]
+        cond_at = [TAB_AT[2] + 7 * KIB + half_kib, V_AT[0] - 7 * half_kib, TAB_AT[2] + 2 * KIB, V_AT[2] + half_kib]
+        heat_sb = [at("heat%d" % i, [P, T2], F32, heat_at[i])[:] for i in range(PACK)]
+        z_first = sb("z_first", [P, 2, T2], F32)
+        cond_sb = [at("cond%d" % i, [P, T2], F32, cond_at[i])[:] for i in range(PACK)]
+        wc_codes = [at("wc_codes%d" % a, [P, T2], U32, V_AT[1] - 7 * half_kib + 4 * KIB * a) for a in range(PASSES2)]
+        wv_raw = at("wv_raw", [P, PACK, N], F32, TAB_AT[2] - 7 * KIB)
         wc_plane = at("wc_plane", [P, T2], U8, ROWS_AT + KIB // 2)
         nc.gpsimd.memset(wc_plane[:].bitcast(I32), 0)
         heat_rows = heat.rearrange("(p i) m -> p i m", i=PACK)
         cond_rows = cond.rearrange("(p i) m -> p i m", i=PACK)
-        nc.sync.dma_start(heat_sb[0], heat_rows[:, 0, :])
-        nc.sync.dma_start(cond_sb[0], cond_rows[:, 0, :])
-        nc.sync.dma_start(wv_raw[:], wv.rearrange("(p j) c -> p j c", j=PACK))
         nc.sync.dma_start(heat_sb[1], heat_rows[:, 1, :])
-        nc.sync.dma_start(cond_sb[1], cond_rows[:, 1, :])
-        nc.sync.dma_start(heat_sb[2], heat_rows[:, 2, :])
+        nc.sync.dma_start(heat_sb[0], heat_rows[:, 0, :])
+        nc.sync.dma_start(wv_raw[:], wv.rearrange("(p j) c -> p j c", j=PACK))
         for q in range(QUADS):
             nc.sync.dma_start(
                 wc_plane[32 * q : 32 * q + 4 * PASSES2, :].bitcast(I32),
                 wc_scales[:, 4 * q : 4 * q + 4, :].bitcast(I32),
             )
+        nc.sync.dma_start(cond_sb[0], cond_rows[:, 0, :])
+        nc.sync.dma_start(cond_sb[1], cond_rows[:, 1, :])
+        nc.sync.dma_start(heat_sb[2], heat_rows[:, 2, :])
         for a in range(PASSES2):
             nc.sync.dma_start(wc_codes[a][:].bitcast(I32), wc_words[a].rearrange("p c i -> p (c i)").bitcast(I32))
         nc.sync.dma_start(heat_sb[3], heat_rows[:, 3, :])
-        nc.sync.dma_start(cond_sb[3], cond_rows[:, 3, :])
-        nc.sync.dma_start(cond_sb[2], cond_rows[:, 2, :])
+        for i in (3, 2):
+            nc.sync.dma_start(cond_sb[i], cond_rows[:, i, :])
 
         left_by = {
-            "both_rows": ROWS_AT - 3 * KIB,
-            "h3": WEIGHTED_AT,
-            "h3 low": WEIGHTED_AT,
-            "h3 high": WEIGHTED_AT + KIB,
+            "both_rows": ROWS_AT - 2 * KIB,
+            "zc0": ZC_AT,
+            "zc0 low": ZC_AT - KIB,
         }
 
         def after(name, shape, dtype, tag=None):
@@ -199,35 +198,36 @@ def tile_list_heating_loop_balance_kernel(
                 return at(name, shape, dtype, left_by[tag])
             return sb(name, shape, dtype, tag=tag)
 
-        z_round = {c: sb("z_round%d" % c, [P, CHUNK, PACK], BF16) for c in range(2)}
+        z_round = {0: sb("z_round0", [P, CHUNK, PACK], BF16)}
         z_codes = [sb("z_codes%d" % c, [P, CHUNK], U32) for c in range(CHUNKS)]
         z_plane = [sb("z_plane%d" % c, [P, CHUNK], U8) for c in range(CHUNKS)]
-        zct = [sb("zct%d" % i, [P, T2], BF16) for i in range(PACK)]
+        zct = {i: sb("zct%d" % i, [P, T2], BF16)[:] for i in range(1, PACK)}
         zc_codes = [sb("zc_codes%d" % i, [P, PASSES2 * P], U32) for i in range(PACK)]
         zc_plane = {}
         wv_plane = sb("wv_plane", [P, N], U8)
         acc = {}
         pages, z, act, weighted, zc_rows = {}, {}, {}, {}, {}
+        page_of = [0, 1, 2, 0]
 
         def clear(i, tag=None):
             pages[i] = after("page%d" % i, [P, T2], F32, tag=tag)
             nc.gpsimd.memset(pages[i][:], 0.0)
 
         def scatter(i):
-            nc.vector.tensor_copy(pages[i % 2][:].indirect(places[:]), weighted[i][:, :])
+            nc.vector.tensor_copy(pages[page_of[i]][:].indirect(places[:]), weighted[i][:, :])
 
         def gelu(i):
-            act[i] = at("act3", [P, S], F32, ACT_LAST_AT) if i == 3 else sb("act%d" % i, [P, S], F32)
+            act[i] = at("act2", [P, S], F32, ACT_LAST_AT) if i == 2 else sb("act%d" % i, [P, S], F32)
             nc.scalar.activation(act[i][:], d[i][:], GELU, bias=bias[:, i : i + 1])
 
-        def weigh_on_gpsimd(i):
+        def weigh_on_gpsimd(i, factor):
             h = z_first[:, 0, :S] if i == 2 else sb("h%d" % i, [P, S], F32)
             weighted[i] = after("weighted%d" % i, [P, S], F32, tag="weighted%d" % i)
-            nc.scalar.activation(h[:], act[i][:], COPY, scale=gain_sb[:, i : i + 1])
+            nc.scalar.activation(h[:], act[i][:], COPY, scale=factor)
             nc.gpsimd.tensor_tensor(weighted[i][:], h[:], wgs_sb[:], MULT)
 
         def remainder(engine, i, cols):
-            engine.tensor_tensor(z[i][:, cols], heat_sb[i][:, cols], pages[i % 2][:, cols], SUBTRACT)
+            engine.tensor_tensor(z[i][:, cols], heat_sb[i][:, cols], pages[page_of[i]][:, cols], SUBTRACT)
 
         def couple(i, cols):
             if i not in zc_rows:
@@ -256,22 +256,34 @@ def tile_list_heating_loop_balance_kernel(
                         block = words[:, P * (2 * a + u) : P * (2 * a + u + 1)]
                     nc.tensor.transpose(turned[:, 2 * a + u, :], block, ident[:])
             nc.scalar.copy(
-                zct[i][:].bitcast(F32).rearrange("q (a n u) -> q a n u", a=PASSES2, u=2),
+                zct[i].bitcast(F32).rearrange("q (a n u) -> q a n u", a=PASSES2, u=2),
                 turned[:].rearrange("q (a u) n -> q a n u", u=2),
             )
 
-        def turn_in_lower_banks(i):
-            words = zc_rows[i][:].bitcast(F32)
-            target = zct[i][:].bitcast(F32).rearrange("q (a n u) -> q a n u", a=PASSES2, u=2)
-            for a in range(PASSES2):
-                turned = [bank(2 * a + u, "turned%d_%d_%d" % (i, a, u), [P, P]) for u in range(2)]
-                for u in range(2):
-                    nc.tensor.transpose(turned[u][:], words[:, 2 * P * a + u : 2 * P * (a + 1) : 2], ident[:])
-                    nc.scalar.copy(target[:, a, :, u], turned[u][:])
+        def remainder_on_tensor(i):
+            blocks = T2 // P // 2
+            z_turned = sb("z_turned", [P, T2], F32)
+            sums = [bank(2 + h, "sums%d" % h, [P, blocks, P]) for h in range(2)]
+            for source in (heat_sb[i], pages[page_of[i]][:]):
+                first = source is heat_sb[i]
+                for h in range(2):
+                    for b in range(blocks):
+                        block = source[:, (blocks * h + b) * P : (blocks * h + b + 1) * P]
+                        nc.tensor.matmul(
+                            sums[h][:, b, :], block, ident[:], is_transpose=True,
+                            start=(first and b == 0), stop=(not first and b == blocks - 1),
+                        )
+                    if not first:
+                        nc.scalar.copy(z_turned[:, halves[h]], sums[h][:].rearrange("p b n -> p (b n)"))
+            for h in range(2):
+                back = bank(h, "back%d" % h, [P, blocks, P])
+                for b in range(blocks):
+                    nc.tensor.transpose(back[:, b, :], z_turned[:, (blocks * h + b) * P : (blocks * h + b + 1) * P], ident[:])
+                nc.scalar.copy(z[i][:, halves[h]], back[:].rearrange("p b n -> p (b n)"))
 
         def quantize_zc(i, tag=None):
             zc_plane[i] = after("zc_plane%d" % i, [P, PASSES2 * P], U8, tag=tag)
-            nc.vector.quantize_mx(out=zc_codes[i][:].bitcast(FP8X4), scales=zc_plane[i][:], in_=zct[i][:])
+            nc.vector.quantize_mx(out=zc_codes[i][:].bitcast(FP8X4), scales=zc_plane[i][:], in_=zct[i])
 
         def round_z(copy, c, slots, rows):
             copy(z_round[c][:, :, slots], rows[:, :, c * CHUNK : (c + 1) * CHUNK].rearrange("p e m -> p m e"))
@@ -312,8 +324,8 @@ def tile_list_heating_loop_balance_kernel(
 
         halves = [slice(0, T2 // 2), slice(T2 // 2, T2)]
         whole = slice(0, T2)
-        clear(0)
-        clear(1)
+        for i in range(3):
+            clear(i)
         act[0] = after("act0", [P, S], F32, tag="both_rows")
         weighted[0] = sb("weighted0", [P, S], F32)
         for e, cols in enumerate(entries):
@@ -321,46 +333,49 @@ def tile_list_heating_loop_balance_kernel(
             nc.vector.scalar_tensor_tensor(
                 weighted[0][:, cols], act[0][:, cols], gain_sb[:, 0:1], wgs_sb[:, cols], MULT, MULT
             )
-        for i in (1, 2):
+        for i, factor in ((1, minus_gain[:]), (2, gain_sb[:, 2:3])):
             gelu(i)
-            weigh_on_gpsimd(i)
+            weigh_on_gpsimd(i, factor)
         gelu(3)
-        h_last = after("h3", [P, S], F32, tag="h3")
-        nc.scalar.activation(h_last[:], act[3][:], COPY, scale=gain_sb[:, 3:4])
-        weighted[3] = heat1_and_more[:, :S]
-        nc.gpsimd.tensor_tensor(weighted[3][:, entries[0]], h_last[:, entries[0]], wgs_sb[:, entries[0]], MULT)
         for cols in entries:
             nc.vector.tensor_copy(pages[0][:].indirect(places[:, cols.start // 16 : cols.stop // 16]), weighted[0][:, cols])
         scatter(1)
-        z[0], z[1] = z_first[:, 0, :], z_first[:, 1, :]
-        remainder(nc.gpsimd, 0, whole)
-        couple(0, whole)
-        turn(0)
         scatter(2)
-        remainder(nc.gpsimd, 1, whole)
-        nc.gpsimd.tensor_tensor(weighted[3][:, entries[1]], h_last[:, entries[1]], wgs_sb[:, entries[1]], MULT)
-        z_last = at("z_last", [P, 2, T2], F32, ACT_LAST_AT + KIB)
-        wv_round = z_last[:, 0, :].bitcast(BF16)
+        late = at("late", [P, 5 * T2 // 2], F32, ACT_LAST_AT + KIB)
+        wv_round = late[:, :T2].bitcast(BF16)
+        zct[0] = late[:, T2 : 3 * T2 // 2].bitcast(BF16)
+        z_last = late[:, T2 // 2 :].rearrange("p (e m) -> p e m", e=2)
         nc.scalar.copy(
             wv_round.rearrange("p (t m j) -> p m t j", t=PACK, j=PACK),
             wv_raw[:].rearrange("p j (m t) -> p m t j", t=PACK),
         )
-        zc_rows[1] = at("zc1", [P, T2], BF16, ZC_AT)
-        couple(1, whole)
-        quantize_zc(0, tag="h3 low")
-        wv_codes = after("wv_codes", [P, N], U32, tag="h3 high")
+        z[0], z[1] = z_first[:, 0, :], z_first[:, 1, :]
+        remainder(nc.gpsimd, 0, whole)
+        zc_rows[0] = after("zc0", [P, T2], BF16, tag="zc0")
+        nc.gpsimd.tensor_tensor(zc_rows[0][:], z[0], cond_sb[0], MULT)
+        remainder_on_tensor(1)
+        turn(0)
+        weighted[3] = at("weighted3", [P, S], F32, cond_at[0] - 3 * half_kib)
+        nc.vector.scalar_tensor_tensor(weighted[3][:], act[3][:], gain_sb[:, 3:4], wgs_sb[:], MULT, MULT)
+        zc1_at = cond_at[0] + 2 * KIB
+        zc_rows[1] = at("zc1", [P, T2], BF16, zc1_at)
+        for cols in halves:
+            couple(1, cols)
+        wv_codes = after("wv_codes", [P, N], U32, tag="zc0 low")
         nc.vector.quantize_mx(out=wv_codes[:].bitcast(FP8X4), scales=wv_plane[:], in_=wv_round)
-        turn_in_lower_banks(1)
+        quantize_zc(0)
+        turn(1, b=6)
         for c in range(CHUNKS):
             right(0, c, True, False)
         for c in range(CHUNKS):
-            if c >= 2:
-                z_round[c] = at("z_round%d" % c, [P, CHUNK, PACK], BF16, ZC_AT + (2 * c - 5) * KIB)
+            if c > 0:
+                place = ZC_AT + KIB if c == 1 else zc1_at + (4 * c - 11) * half_kib
+                z_round[c] = at("z_round%d" % c, [P, CHUNK, PACK], BF16, place)
             round_z(nc.scalar.copy, c, slice(0, 2), z_first[:])
         scatter(3)
         z[2], z[3] = z_last[:, 0, :], z_last[:, 1, :]
         remainder(nc.gpsimd, 2, whole)
-        quantize_zc(1, tag="page0")
+        quantize_zc(1, tag="page2")
         for c in range(CHUNKS):
             right(1, c, False, False)
 
@@ -399,7 +414,7 @@ def tile_list_heating_loop_balance_kernel(
         for cols in (slice(0, CHUNK), slice(CHUNK, 2 * CHUNK), halves[1]):
             remainder(nc.vector, 3, cols)
         for c in range(2):
-            round_z(nc.scalar.copy, c, slice(2, 4), z_last[:])
+            round_z(nc.scalar.copy, c, slice(2, 4), z_last)
         couple_sorted(3, 0)
         quantize_z(0)
         close_low(0)
@@ -410,13 +425,13 @@ def tile_list_heating_loop_balance_kernel(
         quantize_z(1)
         close_low(1)
         open_high(1)
-        round_z(nc.scalar.copy, 2, slice(2, 4), z_last[:])
+        round_z(nc.scalar.copy, 2, slice(2, 4), z_last)
         for a in range(PASSES2):
             couple_sorted(2, a)
         turn(2)
         empty(0, 1)
         quantize_zc(3)
-        round_z(nc.vector.tensor_copy, 3, slice(2, 4), z_last[:])
+        round_z(nc.vector.tensor_copy, 3, slice(2, 4), z_last)
         quantize_z(2)
         quantize_zc(2)
         quantize_z(3)
@@ -442,6 +457,6 @@ def tile_list_heating_loop_balance_kernel(
         weave(3, nc.vector.tensor_copy, CHUNK // 4, CHUNK - CHUNK // 4)
         for c in range(2, CHUNKS):
             quantize_y(c)
-        for q in range(QUADS):
-            queue = nc.scalar if q < 2 else nc.sync
-            queue.dma_start(out_2[0, 4 * q : 4 * q + 4, :].bitcast(I32), y_plane[32 * q : 32 * q + 4, :].bitcast(I32))
+        for r in range(4):
+            queue = nc.scalar if r < 2 else nc.sync
+            queue.dma_start(out_2[0, r:16:4, :].bitcast(I32), y_plane[r:P:32, :].bitcast(I32))

@@ -29,6 +29,8 @@ ROW0 = P - 16 * PASSES1
 TAB_AT = [0, 12 * KIB, 30 * KIB]
 ACT_LAST_AT = 81 * KIB
 ZC_AT = 96 * KIB
+TURNED_AT = 100 * KIB
+V_ROWS_AT = 104 * KIB
 ROWS_AT = 78 * KIB
 V_AT = [49 * KIB, 57 * KIB, 65 * KIB]
 CHUNK = 256
@@ -91,7 +93,7 @@ def tile_list_heating_loop_balance_kernel(
         nc.sync.dma_start(wgs_sb[:], wgs)
         nc.sync.dma_start(places[:], offs2)
 
-        v_rows = sb("v_rows", [P, S], U8)
+        v_rows = at("v_rows", [P, S], U8, V_ROWS_AT)
         nc.vector.tensor_copy(
             both_rows[:, S:].rearrange("p (i c) -> p i c", i=PACK), w1_rows[:].rearrange("p (c i) -> p i c", i=PACK)
         )
@@ -159,22 +161,22 @@ def tile_list_heating_loop_balance_kernel(
                 first_product(d[i][:], i, a, slice(0, S), a == 0, a == PASSES1 - 1)
 
         half_kib = KIB // 2
-        heat_at = [TAB_AT[1] + half_kib, TAB_AT[1] - 7 * half_kib, V_AT[0] + half_kib, V_AT[2] - 7 * half_kib]
+        heat_at = [TAB_AT[1] + half_kib, TAB_AT[2] - 7 * half_kib, V_AT[0] + half_kib, V_AT[2] - 7 * half_kib]
         cond_at = [TAB_AT[2] + 7 * KIB + half_kib, V_AT[0] - 7 * half_kib, TAB_AT[2] + 2 * KIB, V_AT[2] + half_kib]
         heat_sb = [at("heat%d" % i, [P, T2], F32, heat_at[i])[:] for i in range(PACK)]
         z_first = sb("z_first", [P, 2, T2], F32)
         cond_sb = [at("cond%d" % i, [P, T2], F32, cond_at[i])[:] for i in range(PACK)]
         wc_codes = [at("wc_codes%d" % a, [P, T2], U32, V_AT[1] - 7 * half_kib + 4 * KIB * a) for a in range(PASSES2)]
-        wv_raw = at("wv_raw", [P, PACK, N], F32, TAB_AT[2] - 7 * KIB)
-        wc_plane = at("wc_plane", [P, T2], U8, ROWS_AT + KIB // 2)
+        wv_raw = at("wv_raw", [P, PACK, N], F32, TAB_AT[1] - 15 * half_kib)
+        wc_plane = at("wc_plane", [P, T2], U8, V_ROWS_AT)
         nc.gpsimd.memset(wc_plane[:].bitcast(I32), 0)
         heat_rows = heat.rearrange("(p i) m -> p i m", i=PACK)
         cond_rows = cond.rearrange("(p i) m -> p i m", i=PACK)
-        nc.sync.dma_start(heat_sb[1], heat_rows[:, 1, :])
         nc.sync.dma_start(heat_sb[0], heat_rows[:, 0, :])
         nc.sync.dma_start(wv_raw[:], wv.rearrange("(p j) c -> p j c", j=PACK))
-        for q in range(QUADS):
-            nc.sync.dma_start(
+        nc.sync.dma_start(heat_sb[1], heat_rows[:, 1, :])
+        for q in (0, 2, 1, 3):
+            nc.gpsimd.dma_start(
                 wc_plane[32 * q : 32 * q + 4 * PASSES2, :].bitcast(I32),
                 wc_scales[:, 4 * q : 4 * q + 4, :].bitcast(I32),
             )
@@ -185,12 +187,12 @@ def tile_list_heating_loop_balance_kernel(
             nc.sync.dma_start(wc_codes[a][:].bitcast(I32), wc_words[a].rearrange("p c i -> p (c i)").bitcast(I32))
         nc.sync.dma_start(heat_sb[3], heat_rows[:, 3, :])
         for i in (3, 2):
-            nc.sync.dma_start(cond_sb[i], cond_rows[:, i, :])
+            for first in (0, T2 // 2):
+                nc.sync.dma_start(cond_sb[i][:, first : first + T2 // 2], cond_rows[:, i, first : first + T2 // 2])
 
         left_by = {
             "both_rows": ROWS_AT - 2 * KIB,
             "zc0": ZC_AT,
-            "zc0 low": ZC_AT - KIB,
         }
 
         def after(name, shape, dtype, tag=None):
@@ -198,7 +200,7 @@ def tile_list_heating_loop_balance_kernel(
                 return at(name, shape, dtype, left_by[tag])
             return sb(name, shape, dtype, tag=tag)
 
-        z_round = {0: sb("z_round0", [P, CHUNK, PACK], BF16)}
+        z_round = {}
         z_codes = [sb("z_codes%d" % c, [P, CHUNK], U32) for c in range(CHUNKS)]
         z_plane = [sb("z_plane%d" % c, [P, CHUNK], U8) for c in range(CHUNKS)]
         zct = {i: sb("zct%d" % i, [P, T2], BF16)[:] for i in range(1, PACK)}
@@ -208,6 +210,7 @@ def tile_list_heating_loop_balance_kernel(
         acc = {}
         pages, z, act, weighted, zc_rows = {}, {}, {}, {}, {}
         page_of = [0, 1, 2, 0]
+        act_at = {2: ACT_LAST_AT, 3: TURNED_AT}
 
         def clear(i, tag=None):
             pages[i] = after("page%d" % i, [P, T2], F32, tag=tag)
@@ -217,7 +220,7 @@ def tile_list_heating_loop_balance_kernel(
             nc.vector.tensor_copy(pages[page_of[i]][:].indirect(places[:]), weighted[i][:, :])
 
         def gelu(i):
-            act[i] = at("act2", [P, S], F32, ACT_LAST_AT) if i == 2 else sb("act%d" % i, [P, S], F32)
+            act[i] = sb("act1", [P, S], F32) if i == 1 else at("act%d" % i, [P, S], F32, act_at[i])
             nc.scalar.activation(act[i][:], d[i][:], GELU, bias=bias[:, i : i + 1])
 
         def weigh_on_gpsimd(i, factor):
@@ -262,7 +265,7 @@ def tile_list_heating_loop_balance_kernel(
 
         def remainder_on_tensor(i):
             blocks = T2 // P // 2
-            z_turned = sb("z_turned", [P, T2], F32)
+            z_turned = at("z_turned", [P, T2], F32, TURNED_AT)
             sums = [bank(2 + h, "sums%d" % h, [P, blocks, P]) for h in range(2)]
             for source in (heat_sb[i], pages[page_of[i]][:]):
                 first = source is heat_sb[i]
@@ -336,7 +339,6 @@ def tile_list_heating_loop_balance_kernel(
         for i, factor in ((1, minus_gain[:]), (2, gain_sb[:, 2:3])):
             gelu(i)
             weigh_on_gpsimd(i, factor)
-        gelu(3)
         for cols in entries:
             nc.vector.tensor_copy(pages[0][:].indirect(places[:, cols.start // 16 : cols.stop // 16]), weighted[0][:, cols])
         scatter(1)
@@ -354,23 +356,23 @@ def tile_list_heating_loop_balance_kernel(
         zc_rows[0] = after("zc0", [P, T2], BF16, tag="zc0")
         nc.gpsimd.tensor_tensor(zc_rows[0][:], z[0], cond_sb[0], MULT)
         remainder_on_tensor(1)
-        turn(0)
-        weighted[3] = at("weighted3", [P, S], F32, cond_at[0] - 3 * half_kib)
-        nc.vector.scalar_tensor_tensor(weighted[3][:], act[3][:], gain_sb[:, 3:4], wgs_sb[:], MULT, MULT)
-        zc1_at = cond_at[0] + 2 * KIB
+        gelu(3)
+        turn(0, b=0)
+        wv_codes = at("wv_codes", [P, N], U32, cond_at[0] - KIB)
+        nc.vector.quantize_mx(out=wv_codes[:].bitcast(FP8X4), scales=wv_plane[:], in_=wv_round)
+        zc1_at = cond_at[0] + 3 * KIB
         zc_rows[1] = at("zc1", [P, T2], BF16, zc1_at)
         for cols in halves:
             couple(1, cols)
-        wv_codes = after("wv_codes", [P, N], U32, tag="zc0 low")
-        nc.vector.quantize_mx(out=wv_codes[:].bitcast(FP8X4), scales=wv_plane[:], in_=wv_round)
+        weighted[3] = sb("weighted3", [P, S], F32)
+        nc.vector.scalar_tensor_tensor(weighted[3][:], act[3][:], gain_sb[:, 3:4], wgs_sb[:], MULT, MULT)
         quantize_zc(0)
-        turn(1, b=6)
+        turn(1)
         for c in range(CHUNKS):
             right(0, c, True, False)
         for c in range(CHUNKS):
-            if c > 0:
-                place = ZC_AT + KIB if c == 1 else zc1_at + (4 * c - 11) * half_kib
-                z_round[c] = at("z_round%d" % c, [P, CHUNK, PACK], BF16, place)
+            place = [cond_at[1], ZC_AT + KIB, zc1_at - 3 * half_kib, zc1_at + half_kib][c]
+            z_round[c] = at("z_round%d" % c, [P, CHUNK, PACK], BF16, place)
             round_z(nc.scalar.copy, c, slice(0, 2), z_first[:])
         scatter(3)
         z[2], z[3] = z_last[:, 0, :], z_last[:, 1, :]

from contextlib import ExitStack

import concourse.mybir as mybir
from concourse.masks import make_identity

K, T, S, H, T2, N = 1536, 2048, 512, 512, 1024, 512
FLOPS = 2 * K * H * S + 2 * H * N * T2 + 2 * N * T2 * T2

F32 = mybir.dt.float32
BF16 = mybir.dt.bfloat16
I32 = mybir.dt.int32
U32 = mybir.dt.uint32
U16 = mybir.dt.uint16
U8 = mybir.dt.uint8
FP8X4 = mybir.dt.float8_e4m3fn_x4
FP4X4 = mybir.dt.float4_e2m1fn_x4
MULT = mybir.AluOpType.mult
SUBTRACT = mybir.AluOpType.subtract
COPY = mybir.ActivationFunctionType.Copy
GELU = mybir.ActivationFunctionType.Gelu_apprx_tanh

P = 128
PACK = 4
QUADS = 4
PASSES1 = K // 512
PASSES2 = T2 // 512
KIB = 1024
ROW0 = P - 16 * PASSES1
TAB_AT = [0, 12 * KIB, 30 * KIB]
ACT_LAST_AT = 81 * KIB
ZC_AT = 96 * KIB
TURNED_AT = 100 * KIB
V_ROWS_AT = 104 * KIB
ROWS_AT = 78 * KIB
V_AT = [49 * KIB, 57 * KIB, 65 * KIB]
CHUNK = 256
CHUNKS = T2 // CHUNK


def tile_list_heating_loop_balance_kernel(
    tc, tab_words, tab_scales, offs, w1_words, w1_scales, b1, gain, offs2, wgs, heat, wv, cond,
    wc_words, wc_scales, out_0, out_1, out_2,
):
    nc = tc.nc
    with ExitStack() as ctx:
        keep = ctx.enter_context(tc.tile_pool(name="keep", bufs=1))
        psum = ctx.enter_context(tc.psum_pool(name="psum", bufs=1))

        def sb(name, shape, dtype, tag=None):
            return keep.tile(shape, dtype, name=name, tag=tag or name, align_bytes=64)

        def bank(b, name, shape):
            return psum.tile(shape, F32, name=name, tag="bank%d" % b)

        shared = ctx.enter_context(tc.tile_pool(name="shared", bufs=1))

        def at(name, shape, dtype, offset):
            return shared.tile(shape, dtype, name=name, tag=name, align_bytes=64, offset=offset)

        picks = keep.tile([P, S // 16], U16, name="picks")
        places = keep.tile([P, S // 16], U16, name="places")
        tab_rows = sb("tab_rows", [P, T], U8)
        w1_rows = at("w1_rows", [P, H], U8, ROWS_AT - 2 * KIB)
        tab_codes = [at("tab_codes%d" % a, [P, T], U32, TAB_AT[a]) for a in range(PASSES1)]
        w1_raw = sb("w1_raw", [P, PASSES1 * 2 * H], U8)
        both_rows = at("both_rows", [P, S + H], U8, ROWS_AT)
        v_codes = [at("v_codes%d" % a, [P, S], U32, V_AT[a]) for a in range(PASSES1)]
        planes = sb("planes", [P, PASSES1 * (S + H)], U8)

        nc.gpsimd.memset(w1_rows[:ROW0, :].bitcast(I32), 0)
        nc.gpsimd.memset(tab_rows[:ROW0, :].bitcast(I32), 0)
        nc.vector.memset(planes[:].bitcast(I32), 0)

        ident = sb("ident", [P, P], F32)
        make_identity(nc, ident[:])

        vectors = sb("vectors", [P, H], F32)
        nc.gpsimd.memset(vectors[: P - 2, :], 0.0)
        wgs_sb = sb("wgs_sb", [P, S], F32)
        nc.sync.dma_start(picks[:], offs)
        for a in range(PASSES1):
            nc.scalar.dma_start(tab_rows[ROW0 + a : P : PASSES1, :].bitcast(I32), tab_scales[a].bitcast(I32))
            nc.sync.dma_start(w1_rows[ROW0 + a : P : PASSES1, :].bitcast(I32), w1_scales[a].bitcast(I32))
        for a in range(PASSES1):
            nc.sync.dma_start(tab_codes[a][:].bitcast(I32), tab_words[a].rearrange("p t i -> p (t i)").bitcast(I32))
            if a == 0:
                nc.sync.dma_start(vectors[P - 2 : P - 1, :], b1.unsqueeze(0))
                nc.sync.dma_start(vectors[P - 1 : P, :], gain.unsqueeze(0))
                nc.sync.dma_start(
                    w1_raw[:].bitcast(I32).rearrange("p (a w) -> p a w", a=PASSES1),
                    w1_words.bitcast(I32).rearrange("a p w -> p a w"),
                )
        nc.sync.dma_start(wgs_sb[:], wgs)
        nc.sync.dma_start(places[:], offs2)

        v_rows = at("v_rows", [P, S], U8, V_ROWS_AT)
        nc.vector.tensor_copy(
            both_rows[:, S:].rearrange("p (i c) -> p i c", i=PACK), w1_rows[:].rearrange("p (c i) -> p i c", i=PACK)
        )
        nc.vector.tensor_copy(v_rows[:], tab_rows[:].indirect(picks[:]))
        nc.vector.tensor_copy(both_rows[:, :S].bitcast(I32), v_rows[:].bitcast(I32))
        for q in (0, 2, 1, 3):
            first = ROW0 + 4 * PASSES1 * q
            nc.scalar.dma_start(
                planes[32 * q : 32 * q + 4, :].bitcast(I32), both_rows[first : first + 4 * PASSES1, :].bitcast(I32)
            )
        turned_vectors = bank(2, "turned_vectors", [P, PACK, P])
        for i in range(PACK):
            nc.tensor.transpose(turned_vectors[:, i, :], vectors[:, i:H:PACK], ident[:])
        per_row = sb("per_row", [P, 2, PACK], F32)
        nc.vector.tensor_copy(per_row[:], turned_vectors[:, :, P - 2 :].rearrange("p i v -> p v i"))
        bias, gain_sb = per_row[:, 0, :], per_row[:, 1, :]
        minus_gain = sb("minus_gain", [P, 1], F32)
        nc.vector.tensor_scalar_mul(minus_gain[:], turned_vectors[:, 1, P - 1 :], -1.0)
        w1_codes = {}
        w1_dealt = w1_raw[:].bitcast(U16).rearrange("p (a c i) -> p i a c", a=PASSES1, i=PACK)

        def deal_words(slices, passes, dealt):
            count = passes.stop - passes.start
            nc.vector.tensor_copy(
                dealt[:].bitcast(U16).rearrange("p (i a c) -> p i a c", a=count, c=P), w1_dealt[:, slices, passes, :]
            )
            for i in range(slices.start, slices.stop):
                for a in range(passes.start, passes.stop):
                    first = 2 * P * ((i - slices.start) * count + a - passes.start)
                    w1_codes[i, a] = dealt[:, first : first + 2 * P]

        entries = [slice(0, S // 2), slice(S // 2, S)]
        for a in range(PASSES1 - 1):
            nc.vector.tensor_copy(v_codes[a][:], tab_codes[a][:].indirect(picks[:]))
            if a == 0:
                deal_words(slice(0, 1), slice(0, PASSES1), sb("w1_first", [P, PASSES1 * 2 * P], U8))
                deal_words(slice(1, 2), slice(0, 1), sb("w1_early", [P, 1 * 2 * P], U8))
        for e in entries:
            nc.vector.tensor_copy(v_codes[-1][:, e], tab_codes[-1][:].indirect(picks[:, e.start // 16 : e.stop // 16]))
        deal_words(slice(1, 2), slice(1, PASSES1), at("w1_late", [P, (PASSES1 - 1) * 2 * P], U8, TAB_AT[2] + 7 * KIB))
        deal_words(slice(2, PACK), slice(0, PASSES1), at("w1_pair", [P, PASSES1 * 4 * P], U8, TAB_AT[2] + 5 * KIB + KIB // 2))
        d = {i: bank(3 + i, "d%d" % i, [P, S]) for i in range(1, PACK)}
        d_first = [bank(e, "d0_%d" % e, [P, S // 2]) for e in range(2)]

        def first_product(out, i, a, cols, start, stop):
            plane = planes[:, a * (S + H) : (a + 1) * (S + H)]
            nc.tensor.matmul_mx(
                out=out,
                lhsT=w1_codes[i, a].bitcast(FP4X4),
                lhsT_scale=plane[:, S + i * P : S + (i + 1) * P],
                rhs=v_codes[a][:, cols].bitcast(FP8X4),
                rhs_scale=plane[:, cols],
                start=start,
                stop=stop,
            )

        for e in range(2):
            for a in range(PASSES1):
                for n in range(2):
                    cols = slice(entries[e].start + n * P, entries[e].start + (n + 1) * P)
                    out = d_first[e][:, n * P : (n + 1) * P]
                    first_product(out, 0, a, cols, (a, n) == (0, 0), (a, n) == (PASSES1 - 1, 1))
        for i in range(1, PACK):
            for a in range(PASSES1):
                first_product(d[i][:], i, a, slice(0, S), a == 0, a == PASSES1 - 1)

        half_kib = KIB // 2
        heat_at = [TAB_AT[1] + half_kib, TAB_AT[2] - 7 * half_kib, V_AT[0] + half_kib, V_AT[2] - 7 * half_kib]
        cond_at = [TAB_AT[2] + 7 * KIB + half_kib, V_AT[0] - 7 * half_kib, TAB_AT[2] + 2 * KIB, V_AT[2] + half_kib]
        heat_sb = [at("heat%d" % i, [P, T2], F32, heat_at[i])[:] for i in range(PACK)]
        z_first = sb("z_first", [P, 2, T2], F32)
        cond_sb = [at("cond%d" % i, [P, T2], F32, cond_at[i])[:] for i in range(PACK)]
        wc_codes = [at("wc_codes%d" % a, [P, T2], U32, V_AT[1] - 7 * half_kib + 4 * KIB * a) for a in range(PASSES2)]
        wv_raw = at("wv_raw", [P, PACK, N], F32, TAB_AT[1] - 15 * half_kib)
        wc_plane = at("wc_plane", [P, T2], U8, V_ROWS_AT)
        nc.gpsimd.memset(wc_plane[:].bitcast(I32), 0)
        heat_rows = heat.rearrange("(p i) m -> p i m", i=PACK)
        cond_rows = cond.rearrange("(p i) m -> p i m", i=PACK)
        nc.sync.dma_start(heat_sb[0], heat_rows[:, 0, :])
        nc.sync.dma_start(wv_raw[:], wv.rearrange("(p j) c -> p j c", j=PACK))
        nc.sync.dma_start(heat_sb[1], heat_rows[:, 1, :])
        for q in (0, 2, 1, 3):
            nc.gpsimd.dma_start(
                wc_plane[32 * q : 32 * q + 4 * PASSES2, :].bitcast(I32),
                wc_scales[:, 4 * q : 4 * q + 4, :].bitcast(I32),
            )
        nc.sync.dma_start(cond_sb[0], cond_rows[:, 0, :])
        nc.sync.dma_start(cond_sb[1], cond_rows[:, 1, :])
        nc.sync.dma_start(heat_sb[2], heat_rows[:, 2, :])
        for a in range(PASSES2):
            nc.sync.dma_start(wc_codes[a][:].bitcast(I32), wc_words[a].rearrange("p c i -> p (c i)").bitcast(I32))
        nc.sync.dma_start(heat_sb[3], heat_rows[:, 3, :])
        for i in (3, 2):
            for first in (0, T2 // 2):
                nc.sync.dma_start(cond_sb[i][:, first : first + T2 // 2], cond_rows[:, i, first : first + T2 // 2])

        left_by = {
            "both_rows": ROWS_AT - 2 * KIB,
            "zc0": ZC_AT,
        }

        def after(name, shape, dtype, tag=None):
            if tag in left_by:
                return at(name, shape, dtype, left_by[tag])
            return sb(name, shape, dtype, tag=tag)

        z_round = {}
        z_codes = [sb("z_codes%d" % c, [P, CHUNK], U32) for c in range(CHUNKS)]
        z_plane = [sb("z_plane%d" % c, [P, CHUNK], U8) for c in range(CHUNKS)]
        zct = {i: sb("zct%d" % i, [P, T2], BF16)[:] for i in range(1, PACK)}
        zc_codes = [sb("zc_codes%d" % i, [P, PASSES2 * P], U32) for i in range(PACK)]
        zc_plane = {}
        wv_plane = sb("wv_plane", [P, N], U8)
        acc = {}
        pages, z, act, weighted, zc_rows = {}, {}, {}, {}, {}
        page_of = [0, 1, 2, 0]
        act_at = {2: ACT_LAST_AT, 3: TURNED_AT}

        def clear(i, tag=None):
            pages[i] = after("page%d" % i, [P, T2], F32, tag=tag)
            nc.gpsimd.memset(pages[i][:], 0.0)

        def scatter(i):
            nc.vector.tensor_copy(pages[page_of[i]][:].indirect(places[:]), weighted[i][:, :])

        def gelu(i):
            act[i] = sb("act1", [P, S], F32) if i == 1 else at("act%d" % i, [P, S], F32, act_at[i])
            nc.scalar.activation(act[i][:], d[i][:], GELU, bias=bias[:, i : i + 1])

        def weigh_on_gpsimd(i, factor):
            h = z_first[:, 0, :S] if i == 2 else sb("h%d" % i, [P, S], F32)
            weighted[i] = after("weighted%d" % i, [P, S], F32, tag="weighted%d" % i)
            nc.scalar.activation(h[:], act[i][:], COPY, scale=factor)
            nc.gpsimd.tensor_tensor(weighted[i][:], h[:], wgs_sb[:], MULT)

        def remainder(engine, i, cols):
            engine.tensor_tensor(z[i][:, cols], heat_sb[i][:, cols], pages[page_of[i]][:, cols], SUBTRACT)

        def couple(i, cols):
            if i not in zc_rows:
                zc_rows[i] = sb("zc%d" % i, [P, T2], BF16)
            nc.vector.tensor_tensor(zc_rows[i][:, cols], z[i][:, cols], cond_sb[i][:, cols], MULT)

        def couple_sorted(i, a):
            if i not in zc_rows:
                zc_rows[i] = sb("zc%d" % i, [P, T2], BF16)
            nc.vector.tensor_tensor(
                zc_rows[i][:, halves[a]].rearrange("p (u q e) -> p u q e", u=2, e=2),
                z[i][:, halves[a]].rearrange("p (q u e) -> p u q e", u=2, e=2),
                cond_sb[i][:, halves[a]].rearrange("p (q u e) -> p u q e", u=2, e=2),
                MULT,
            )

        def turn(i, b=7):
            zc = zc_rows[i]
            turned = bank(b, "turned%d" % i, [P, 2 * PASSES2, P])
            words = zc[:].bitcast(F32)
            for a in range(PASSES2):
                for u in range(2):
                    if i < 2:
                        block = words[:, 2 * P * a + u : 2 * P * (a + 1) : 2]
                    else:
                        block = words[:, P * (2 * a + u) : P * (2 * a + u + 1)]
                    nc.tensor.transpose(turned[:, 2 * a + u, :], block, ident[:])
            nc.scalar.copy(
                zct[i].bitcast(F32).rearrange("q (a n u) -> q a n u", a=PASSES2, u=2),
                turned[:].rearrange("q (a u) n -> q a n u", u=2),
            )

        def remainder_on_tensor(i):
            blocks = T2 // P // 2
            z_turned = at("z_turned", [P, T2], F32, TURNED_AT)
            sums = [bank(2 + h, "sums%d" % h, [P, blocks, P]) for h in range(2)]
            for source in (heat_sb[i], pages[page_of[i]][:]):
                first = source is heat_sb[i]
                for h in range(2):
                    for b in range(blocks):
                        block = source[:, (blocks * h + b) * P : (blocks * h + b + 1) * P]
                        nc.tensor.matmul(
                            sums[h][:, b, :], block, ident[:], is_transpose=True,
                            start=(first and b == 0), stop=(not first and b == blocks - 1),
                        )
                    if not first:
                        nc.scalar.copy(z_turned[:, halves[h]], sums[h][:].rearrange("p b n -> p (b n)"))
            for h in range(2):
                back = bank(h, "back%d" % h, [P, blocks, P])
                for b in range(blocks):
                    nc.tensor.transpose(back[:, b, :], z_turned[:, (blocks * h + b) * P : (blocks * h + b + 1) * P], ident[:])
                nc.scalar.copy(z[i][:, halves[h]], back[:].rearrange("p b n -> p (b n)"))

        def quantize_zc(i, tag=None):
            zc_plane[i] = after("zc_plane%d" % i, [P, PASSES2 * P], U8, tag=tag)
            nc.vector.quantize_mx(out=zc_codes[i][:].bitcast(FP8X4), scales=zc_plane[i][:], in_=zct[i])

        def round_z(copy, c, slots, rows):
            copy(z_round[c][:, :, slots], rows[:, :, c * CHUNK : (c + 1) * CHUNK].rearrange("p e m -> p m e"))

        def quantize_z(c):
            nc.vector.quantize_mx(
                out=z_codes[c][:].bitcast(FP8X4), scales=z_plane[c][:], in_=z_round[c][:].rearrange("p m i -> p (m i)")
            )

        def right(i, c, first, last):
            u = i // 2
            if first:
                acc[u, c] = bank(4 * u + c, "acc%d_%d" % (u, c), [P, 2, CHUNK])
            cols = slice(c * CHUNK, (c + 1) * CHUNK)
            for a in range(PASSES2):
                nc.tensor.matmul_mx(
                    out=acc[u, c][:, i % 2, :],
                    lhsT=zc_codes[i][:, a * P : (a + 1) * P].bitcast(FP8X4),
                    lhsT_scale=zc_plane[i][:, a * P : (a + 1) * P],
                    rhs=wc_codes[a][:, cols].bitcast(FP8X4),
                    rhs_scale=wc_plane[4 * a : P, cols],
                    start=(first and a == 0),
                    stop=(last and a == PASSES2 - 1),
                )

        def left(i, c, first, last):
            if first:
                acc[i // 2, c] = bank(4 * (i // 2) + c, "acc%d_%d" % (i // 2, c), [P, 2, CHUNK])
            nc.tensor.matmul_mx(
                out=acc[i // 2, c][:, i % 2, :],
                lhsT=wv_codes[:, i * P : (i + 1) * P].bitcast(FP8X4),
                lhsT_scale=wv_plane[:, i * P : (i + 1) * P],
                rhs=z_codes[c][:].bitcast(FP8X4),
                rhs_scale=z_plane[c][:],
                start=first,
                stop=last,
            )

        halves = [slice(0, T2 // 2), slice(T2 // 2, T2)]
        whole = slice(0, T2)
        for i in range(3):
            clear(i)
        act[0] = after("act0", [P, S], F32, tag="both_rows")
        weighted[0] = sb("weighted0", [P, S], F32)
        for e, cols in enumerate(entries):
            nc.scalar.activation(act[0][:, cols], d_first[e][:], GELU, bias=bias[:, 0:1])
            nc.vector.scalar_tensor_tensor(
                weighted[0][:, cols], act[0][:, cols], gain_sb[:, 0:1], wgs_sb[:, cols], MULT, MULT
            )
        for i, factor in ((1, minus_gain[:]), (2, gain_sb[:, 2:3])):
            gelu(i)
            weigh_on_gpsimd(i, factor)
        for cols in entries:
            nc.vector.tensor_copy(pages[0][:].indirect(places[:, cols.start // 16 : cols.stop // 16]), weighted[0][:, cols])
        scatter(1)
        scatter(2)
        late = at("late", [P, 5 * T2 // 2], F32, ACT_LAST_AT + KIB)
        wv_round = late[:, :T2].bitcast(BF16)
        zct[0] = late[:, T2 : 3 * T2 // 2].bitcast(BF16)
        z_last = late[:, T2 // 2 :].rearrange("p (e m) -> p e m", e=2)
        nc.scalar.copy(
            wv_round.rearrange("p (t m j) -> p m t j", t=PACK, j=PACK),
            wv_raw[:].rearrange("p j (m t) -> p m t j", t=PACK),
        )
        z[0], z[1] = z_first[:, 0, :], z_first[:, 1, :]
        remainder(nc.gpsimd, 0, whole)
        zc_rows[0] = after("zc0", [P, T2], BF16, tag="zc0")
        nc.gpsimd.tensor_tensor(zc_rows[0][:], z[0], cond_sb[0], MULT)
        remainder_on_tensor(1)
        gelu(3)
        turn(0, b=0)
        wv_codes = at("wv_codes", [P, N], U32, cond_at[0] - KIB)
        nc.vector.quantize_mx(out=wv_codes[:].bitcast(FP8X4), scales=wv_plane[:], in_=wv_round)
        zc1_at = cond_at[0] + 3 * KIB
        zc_rows[1] = at("zc1", [P, T2], BF16, zc1_at)
        for cols in halves:
            couple(1, cols)
        weighted[3] = sb("weighted3", [P, S], F32)
        nc.vector.scalar_tensor_tensor(weighted[3][:], act[3][:], gain_sb[:, 3:4], wgs_sb[:], MULT, MULT)
        quantize_zc(0)
        turn(1)
        for c in range(CHUNKS):
            right(0, c, True, False)
        for c in range(CHUNKS):
            place = [cond_at[1], ZC_AT + KIB, zc1_at - 3 * half_kib, zc1_at + half_kib][c]
            z_round[c] = at("z_round%d" % c, [P, CHUNK, PACK], BF16, place)
            round_z(nc.scalar.copy, c, slice(0, 2), z_first[:])
        scatter(3)
        z[2], z[3] = z_last[:, 0, :], z_last[:, 1, :]
        remainder(nc.gpsimd, 2, whole)
        quantize_zc(1, tag="page2")
        for c in range(CHUNKS):
            right(1, c, False, False)

        y = [sb("y%d" % c, [P, PACK, CHUNK], F32) for c in range(CHUNKS)]
        y_round = [sb("y_round%d" % c, [P, CHUNK * PACK], BF16) for c in range(CHUNKS)]
        y_codes = sb("y_codes", [P, T2], U32)
        y_plane = sb("y_plane", [P, T2], U8)
        out_rows = out_0.rearrange("(p i) m -> p i m", i=PACK)
        out_words = out_1[0].rearrange("p m t -> p (m t)").bitcast(I32)

        def empty(u, c, copy=nc.scalar.copy):
            cols = slice(c * CHUNK, (c + 1) * CHUNK)
            copy(y[c][:, 2 * u : 2 * u + 2, :], acc[u, c][:])
            nc.sync.dma_start(out_rows[:, 2 * u : 2 * u + 2, cols], y[c][:, 2 * u : 2 * u + 2, :])

        def weave(c, copy, first=0, count=CHUNK):
            copy(
                y_round[c][:, PACK * first : PACK * (first + count)].rearrange("p (m j i) -> p m i j", j=4, i=PACK),
                y[c][:, :, first : first + count].rearrange("p i (m j) -> p m i j", j=4),
            )

        def quantize_y(c):
            cols = slice(c * CHUNK, (c + 1) * CHUNK)
            nc.vector.quantize_mx(out=y_codes[:, cols].bitcast(FP8X4), scales=y_plane[:, cols], in_=y_round[c][:])
            if c % 2 == 1:
                nc.sync.dma_start(out_words[:, halves[c // 2]], y_codes[:, halves[c // 2]].bitcast(I32))

        def close_low(c):
            left(0, c, False, False)
            left(1, c, False, True)

        def open_high(c):
            left(2, c, True, False)
            left(3, c, False, False)

        for cols in (slice(0, CHUNK), slice(CHUNK, 2 * CHUNK), halves[1]):
            remainder(nc.vector, 3, cols)
        for c in range(2):
            round_z(nc.scalar.copy, c, slice(2, 4), z_last)
        couple_sorted(3, 0)
        quantize_z(0)
        close_low(0)
        open_high(0)
        empty(0, 0)
        couple_sorted(3, 1)
        turn(3, b=6)
        quantize_z(1)
        close_low(1)
        open_high(1)
        round_z(nc.scalar.copy, 2, slice(2, 4), z_last)
        for a in range(PASSES2):
            couple_sorted(2, a)
        turn(2)
        empty(0, 1)
        quantize_zc(3)
        round_z(nc.vector.tensor_copy, 3, slice(2, 4), z_last)
        quantize_z(2)
        quantize_zc(2)
        quantize_z(3)
        right(3, 0, False, False)
        close_low(2)
        empty(0, 2)
        right(2, 0, False, True)
        empty(1, 0, nc.vector.tensor_copy)
        close_low(3)
        empty(0, 3)
        for c in range(1, CHUNKS):
            if c >= 2:
                open_high(c)
            right(3, c, False, False)
            right(2, c, False, True)
            empty(1, c)
        weave(0, nc.vector.tensor_copy)
        weave(1, nc.vector.tensor_copy)
        quantize_y(0)
        weave(2, nc.vector.tensor_copy)
        quantize_y(1)
        weave(3, nc.scalar.copy, 0, CHUNK // 4)
        weave(3, nc.vector.tensor_copy, CHUNK // 4, CHUNK - CHUNK // 4)
        for c in range(2, CHUNKS):
            quantize_y(c)
        for r in range(4):
            queue = nc.scalar if r < 2 else nc.sync
            queue.dma_start(out_2[0, r:16:4, :].bitcast(I32), y_plane[r:P:32, :].bitcast(I32))
